import numpy as np, ml_dtypes
CORES = [40,64,80,88,96,104,120,144]
N = 8
BF = ml_dtypes.bfloat16
def gentries(a):
    return np.ascontiguousarray(a.reshape(8, 16, -1).transpose(0, 2, 1)).reshape(8, -1)
def gtable(e):
    e = np.asarray(e); return np.ascontiguousarray(e.reshape(8, -1, 16).transpose(0, 2, 1)).reshape(128, -1).astype(np.int32)
W, T, K, C, J, RO = 2048, 256, 8, 16, 3, 5
Q = W // T
def lay(v):
    return np.ascontiguousarray(v.transpose(0, 1, 3, 2)).reshape(N, 128, -1).astype(np.float32).astype(BF)
def pack(x, s, m, z, w, kp):
    return {"rec": lay(x), "st": lay(s.reshape(N, 8, T * K, 16)), "nm": np.stack([gtable(a.reshape(8, -1)) for a in m]), "arr": lay(z),
            "wt": np.ascontiguousarray(w.reshape(N, 128, 1)).astype(np.int32), "kap": np.stack([gtable(a) for a in kp])}
def consts(rng):
    return rng.integers(0, 256, (N, 8, 16)), rng.integers(0, 1024, (N, 8, C))
def make(rng, base, sp, wild):
    share = rng.choice(np.array([0.5, 0.7, 0.9]), (N, 8, 1, 1))
    def mix(n):
        v = np.clip(base + ((rng.random((N, 8, T, n, 16)) - 0.5) * sp).astype(np.int64), 0, 255)
        return np.where((rng.random((N, 8, T, n)) < share)[..., None], v, wild((N, 8, T, n)))
    x = mix(Q).reshape(N, 8, W, 16); s = mix(K); z = mix(1)[:, :, :, 0]
    own = Q * np.arange(T)[:, None] + rng.integers(0, Q, (N, 8, T, K))
    m = np.where(rng.random((N, 8, T, K)) < share, own, rng.integers(0, W, (N, 8, T, K)))
    return x, s, m, z
def setup_inputs(rng):
    x, s, m, z = make(rng, rng.integers(0, 256, (N, 8, T, 1, 16)), 24.0, lambda sh: rng.integers(0, 256, sh + (16,)))
    return pack(x, s, m, z, *consts(rng))
def setup_inputs_spread(rng):
    def uneven(sh):
        return np.minimum((np.exp2(8 * rng.random(sh + (1,))) * rng.random(sh + (16,))).astype(np.int64), 255)
    base = uneven((N, 8, T, 1)); x, s, m, z = make(rng, base, 0.5 * base + 2, uneven)
    m = np.where(rng.random((N, 8, T, K)) < 0.3, np.minimum((W * rng.random((N, 8, T, K)) ** 3).astype(np.int64), W - 1), m)
    w = np.minimum(np.exp2(8 * rng.random((N, 8, 16))).astype(np.int64) - 1, 255); kp = np.minimum(np.exp2(10 * rng.random((N, 8, C))).astype(np.int64) - 1, 1023)
    return pack(x, s, m, z, w, kp)
def setup_inputs_ends(rng):
    def ext(sh):
        k = rng.integers(0, 3, sh + (1,)); return 255 * np.where(k == 2, rng.integers(0, 2, sh + (16,)), k)
    x = ext((N, 8, W)); s = ext((N, 8, T, K)); z = ext((N, 8, T)); h = T // 2
    m = (W - 1) * rng.integers(0, 2, (N, 8, T, K)); w = 255 * rng.integers(0, 2, (N, 8, 16)); kp = 1023 * rng.integers(0, 2, (N, 8, C))
    w[:, 0, 3] = 0; kp[:, 0, 3] = 0
    w[:, 7] = 255; kp[:, 7] = 1023; x[:, 7] = 0; s[:, 7, h:] = 255; m[:, 7, h:] = W - 1
    z[:, 7] = 255 * rng.integers(0, 2, (N, T, 1)); z[:, 7, h:] = 255
    u = (16 * 255 * 255) & (W - 1); c = ((u * u >> 5) + 1023 * u + 1023) & (W - 1); x[0::2, 7, c, 15] = 1
    x[:, 6] = 0; s[:, 6, h:] = 0; z[:, 6, h:] = 0
    s[:, 5, T - 1] = 0; s[:, 5, T - 1, K - 1] = 255; z[:, 5, T - 1] = 255
    s[:, 5, T - 2] = 255; z[:, 5, T - 2] = 0
    s[:, 5, T - 3] = 0; s[:, 5, T - 3, K - 1, 15] = 1; z[:, 5, T - 3] = 255
    s[:, 5, T - 4] = 255; s[:, 5, T - 4, K - 2, 15] = 254; z[:, 5, T - 4] = 0
    x[:, 4] = rng.integers(0, 4, (N, W, 16)); s[:, 4] = rng.integers(252, 256, (N, T, K, 16))
    z[:, 4, :h] = rng.integers(252, 256, (N, h, 16)); z[:, 4, h:] = rng.integers(0, 4, (N, T - h, 16))
    m[:, 4] = rng.integers(0, W, (N, T, K)); w[:, 4] = rng.integers(0, 256, (N, 16)); kp[:, 4] = rng.integers(0, 1024, (N, C))
    return pack(x, s, m, z, w, kp)
def setup_inputs_corners(rng):
    gi = np.arange(8)[None, :]; ri = np.arange(N)[:, None]; row = np.arange(K); lane = np.arange(T)
    kind = np.argsort(rng.random((N, 8, T)), axis=-1) % 8; code = np.argsort(rng.random((N, 8, T)), axis=-1) % 6
    kind[:, :, T - 1] = gi; code[:, :, T - 1] = (gi + ri) % 6
    goal = np.array([0, K - 1, K - 2, K - 1 - J, K - J, 0, 0, 0])[kind]; goal = np.where(kind == 7, rng.integers(0, K, kind.shape), goal)
    z = rng.integers(0, 101, (N, 8, T, 16)); z[kind == 6] = np.array([255, 1] + [0] * 14)
    s = rng.integers(150, 256, (N, 8, T, K, 16)); hit = (row == goal[..., None]) | (kind == 5)[..., None]
    s = np.where(hit[..., None], z[:, :, :, None, :], s)
    tot = np.sum(z, axis=-1); n = Q * lane + (tot & (Q - 1)); far = Q * lane + ((tot + 1) & (Q - 1))
    x = rng.integers(0, 101, (N, 8, W, 16)); x[:, :, 0] = 0; x[:, :, W - 1] = 255
    a, b, c = np.nonzero(code == 3); x[a, b, far[a, b, c]] = 255
    k = code[..., None]; n1 = n[..., None]; last = np.where(row == (goal + J)[..., None], far[..., None], n1)
    m = np.where(k == 4, rng.integers(0, W, (N, 8, T, K)), np.roll(n, -1, axis=2)[..., None])
    m = np.where(k == 0, n1, np.where(k == 1, 0, np.where(k == 2, W - 1, np.where(k == 3, last, m))))
    w, kp = consts(rng); w[:, 0::2, 0] = (W - 1) // 255; w[:, 0::2, 1] = (W - 1) % 255; w[:, 5] = 0
    kp[:, 0] = 1023; kp[:, 3] = 0
    return pack(x, s, m, z, w, kp)
def setup_inputs_crowd(rng):
    v = rng.integers(40, 80, (N, 8, 16)); v[..., 0] |= 1
    v[..., 1] += (np.sum(v, axis=-1) & (Q - 1)) == 1
    w, kp = consts(rng); w[..., 0] ^= 1 - (np.sum(w * v, axis=-1) & 1)
    kp[..., 1] = 2 * (kp[..., 1] >> 1); kp[..., 2] |= 1
    x = v[:, :, None, :] + rng.integers(0, 4, (N, 8, W, 16)); x[:, :, 0::Q] = v[:, :, None, :]
    x[:, :, 1::Q] = v[:, :, None, :] + 100 + rng.integers(0, 75, (N, 8, T, 16))
    s = rng.integers(0, 256, (N, 8, T, K, 16)); s[:, :, :, 0] = v[:, :, None, :]
    z = np.repeat(v[:, :, None, :], T, axis=2)
    go = np.ones((N, 8, T), bool)
    for q in range(1, N):
        for g in range(8):
            mode = int(rng.integers(0, 4)) if q > 2 else int(rng.integers(0, 2))
            if q == 1: mode = 1 if g == 7 else 0
            if q == 2 and g == 3: mode = 1
            if mode == 1: go[q, g, T - 1 if q == 1 else int(rng.integers(0, T))] = False
            if mode == 2: go[q, g] = False
            if mode == 3: go[q, g] = rng.permutation(T) < T // 2
    off = Q * rng.integers(0, T, (N, 8, T, K)) + 1; off[:, 0::2] = off[:, 0::2, :1, :1]
    m = np.where(go[..., None], off, Q * rng.integers(0, T, (N, 8, T, K)))
    y = np.where(go[1][..., None], x[1][np.arange(8)[:, None], m[1, :, :, 1]], np.abs(z[1] - s[1, :, :, K - 1]))
    s[2, :, :, K - 1] = np.maximum(y - rng.integers(0, 4, y.shape), 0)
    return pack(x, s, m, z, w, kp)
def setup_inputs_ties(rng):
    p = rng.integers(20, 236, (N, 8, 16)); e = 20 * (np.arange(16) & 1)
    pats = np.stack([p, p + 10, p - 10, p + e, p + 20 - e], axis=2); a = np.arange(N)[:, None, None]; b = np.arange(8)[None, :, None]
    x = pats[a, b, rng.integers(0, 5, (N, 8, W))]; z = pats[a, b, rng.integers(0, 5, (N, 8, T))]
    s = pats[a, b, rng.integers(0, 5, (N, 8, T * K))].reshape(N, 8, T, K, 16)
    return pack(x, s, rng.integers(0, W, (N, 8, T, K)), z, *consts(rng))
def check_inputs(d):
    bad = []
    for k, hi in (("rec", 255), ("st", 255), ("nm", W - 1), ("arr", 255), ("wt", 255), ("kap", 1023)):
        v = np.asarray(d[k]).astype(np.float64)
        if not (np.all(v >= 0) and np.all(v <= hi)): bad.append("range of " + k)
        elif np.any(v != np.floor(v)): bad.append("whole numbers in " + k)
    return bad
def unlay(a):
    return np.ascontiguousarray(a.astype(np.float32).astype(np.int32).reshape(N, 8, 16, -1).transpose(0, 1, 3, 2))
def reference(rec, st, nm, arr, wt, kap):
    x = unlay(rec); s = unlay(st).reshape(N, 8, T, K, 16); z = unlay(arr)
    m = np.stack([gentries(a) for a in nm]).astype(np.int32).reshape(N, 8, T, K)
    w = wt.astype(np.int32).reshape(N, 8, 1, 16); kp = np.stack([gentries(a) for a in kap]).astype(np.int32)[:, :, None, :]
    ri = np.arange(N)[:, None, None]; gi = np.arange(8)[None, :, None]; li = np.arange(T)[None, None, :]; row = np.arange(K)
    cnt = np.zeros((N, 1, 1, 1), np.int32)
    for t in range(RO):
        n = (Q * li + (np.sum(z, axis=-1) & (Q - 1))).astype(np.int32)
        x[ri, gi, n] = z
        g = np.argmin(np.sum(np.abs(s - z[:, :, :, None, :]), axis=-1, dtype=np.int32), axis=-1)
        mid = (s[ri, gi, li, g] + z) >> 1
        low = row < g[..., None]
        s = np.where(low[..., None], np.concatenate([s[:, :, :, 1:], s[:, :, :, -1:]], axis=3), s)
        m = np.where(low, np.concatenate([m[..., 1:], m[..., -1:]], axis=3), m)
        s[ri, gi, li, g] = mid; m[ri, gi, li, g] = n
        rel = np.zeros((N, 8, T), bool); gone = np.zeros((N, 8, T), np.int32)
        for j in range(1, J + 1):
            live = g + j < K; p = np.minimum(g + j, K - 1)
            b = s[ri, gi, li, p - 1]
            u = (np.sum(w * b, axis=-1, dtype=np.int32) & (W - 1))[..., None]
            c = ((u * u >> 5) + kp * u + kp[..., :1] * j + cnt) & (W - 1)
            old = m[ri, gi, li, p]; c[..., 0] = old
            v = x[ri[..., None], gi[..., None], c]
            f = np.argmin(np.sum(np.abs(v - b[:, :, :, None, :]), axis=-1, dtype=np.int32), axis=-1)
            e = c[ri, gi, li, f]; xe = v[ri, gi, li, f]
            s[ri, gi, li, p] = np.where(live[..., None], (b + xe) >> 1, s[ri, gi, li, p])
            m[ri, gi, li, p] = np.where(live, e, old)
            now = live & (e != old) & ~rel
            gone = np.where(now, old, gone); rel = rel | now
        nxt = np.where(rel[..., None], x[ri, gi, gone], np.abs(z - s[:, :, :, K - 1]))
        cnt = (np.sum(rel, axis=(1, 2)).astype(np.int32) & 63).reshape(N, 1, 1, 1)
        z = np.stack([nxt[(q - 1 - t % 3) % N] for q in range(N)])
    mo = np.stack([gtable(a.reshape(8, -1)) for a in m])
    return {"so": lay(s.reshape(N, 8, T * K, 16)), "mo": mo.astype(np.float32), "zo": lay(z)}

@@ -1,0 +1,760 @@
+from concourse.bass import DstId, RemoteDMATransfer
+from concourse.mybir import dt, AluOpType, AxisListType, ActivationFunctionType
+
+OP = AluOpType
+AF = ActivationFunctionType
+RO, NR = 5, 8
+NB = 6
+NG = 0
+AL = [1] * 10
+AB = [2] * 5
+GS = False
+OBV = False
+LV = 0
+F16 = "float16"
+MAGIC = 12582912.0
+BIG = 32768.0
+DWW = 128 * (17 + 16 - NB)
+
+
+def code(m):
+    return m + 1 if m < NB else 17 + m - NB
+
+
+SCRATCH = {}
+
+
+def _sb(name, w, d):
+    SCRATCH[name] = ("sbuf", [128, w], d)
+
+
+for _n, _w, _d in [
+    ("xw", 2304, "bfloat16"), ("sti", 2048, "bfloat16"), ("ari", 256, "bfloat16"), ("zz", 6 * 256, "bfloat16"),
+    ("ob", 5 * 256, "bfloat16"), ("w0", 3072, "bfloat16"), ("w1", 3072, "bfloat16"), ("kt", DWW, "bfloat16"),
+    ("sob", 2048, "bfloat16"), ("zob", 256, "bfloat16"), ("nmi", 128, "int32"), ("nmf", 128, "float32"),
+    ("mob", 128, "float32"), ("srf", 128, "int32"), ("srp", 128, "uint16"), ("fl", 128, "uint16"),
+    ("wti", 4, "int32"), ("kpi", 4, "int32"), ("wtf", 4, "float32"), ("kpf", 4, "float32"),
+    ("pi", 8, "int32"), ("pf", 8, "float32"), ("pc", 8, "float32"), ("xi", 144, "float32"), ("i1", 128, "float32"),
+    ("i2", 128, "float32"), ("i3", 64, "float32"), ("i4", 16, "float32"), ("i5", 16, "float32"), ("i6", 8, "float32"),
+    ("i7", 64, "float32"), ("i8", 64, "float32"),
+    ("z1", 144, "bfloat16"), ("z4", 144, "bfloat16"), ("zw", 144, "bfloat16"), ("zn", 144, "bfloat16"),
+    ("idb", 128, "bfloat16"), ("nid", 128, "bfloat16"), ("hid", 128, "bfloat16"), ("one", 128, "bfloat16"),
+    ("qrt", 128, "bfloat16"), ("zer", 128, "bfloat16"),
+    ("idh", 128, F16), ("nih", 128, F16), ("i128", 128, F16), ("blk", 128, "float32"), ("m16", 128, "float32"),
+    ("kapr", 128, "float32"), ("kq", 64, "int32"), ("kqf", 64, "float32"), ("k0j", 8, "float32"),
+    ("posk", 64, "float32"), ("poskh", 64, F16), ("ck", 64, F16), ("pa", 128, "bfloat16"), ("pb", 64, "bfloat16"),
+    ("pk", 64, "bfloat16"), ("ti8", 16, "float32"), ("dfl", 16, "float32"), ("jc", 48, "float32"),
+    ("lrep", 8, "uint16"), ("lperm", 8, "uint16"), ("linv", 8, "uint16"), ("larr", 16, "uint16"),
+    ("lzo", 16, "uint16"), ("lst", 128, "uint16"),
+    ("rel", 16, "bfloat16"), ("cnt", 16, "int32"), ("cntf", 8, "float32"), ("ofc", 8, "float32"),
+]:
+    _sb(_n, _w, _d)
+for _h in range(2):
+    for _n, _w, _d in [
+        ("dw", DWW, "bfloat16"), ("ab", 2048, "bfloat16"), ("ge", 256, "bfloat16"), ("kg", 384, "bfloat16"),
+        ("d7", 128, "bfloat16"), ("e1", 64, "float32"), ("tr", 128, "float32"), ("si", 256, "int32"),
+        ("tt", 256, "int32"), ("tf", 128, "float32"), ("c16", 128, "uint16"), ("l16", 96, "uint16"), ("src", 64, "uint16"),
+        ("nm", 96, F16), ("hh", 64 * 12, F16), ("sf", 192, "float32"),
+    ]:
+        _sb(_n + str(_h), _w, _d)
+for _b in range(8):
+    SCRATCH["ps%d" % _b] = ("psum", [128, 512], "float32")
+SCRATCH["dfl_d"] = ("dram", [128, 128], "uint16")
+
+DMAS = ["dwt", "dkp", "dar", "dst", "drc", "dnm", "dr1", "dr2", "dso0", "dso1", "dzo", "dmo", "dm2"]
+SEMAPHORES = ["cv", "cs", "cp", "cg", "sent"] + DMAS + ["ar%d" % i for i in range(2 * RO)]
+
+CV, CPE, LAT, GA, SC, COMM = 1.0, 0.5, 90.0, 1.56, 3.8, 3500.0
+
+
+def build(T, RO=RO):
+    ops = []
+    cur = [0, "i", 0]
+
+    def R(name, lo, hi, step=1):
+        ap = T[name][:, lo:hi] if step == 1 else T[name][:, lo:hi:step]
+        return (ap, (name, lo, hi), len(range(lo, hi, step)), SCRATCH[name][2])
+
+    def C(name, c):
+        return R(name, c, c + 1)
+
+    def G(win, off):
+        return (win[0].indirect(off[0]), win[1], 16 * off[2], win[3], off[1])
+
+    def add(eng, fn, reads, writes, cost, **kw):
+        rd = []
+        for r in reads:
+            if isinstance(r, tuple):
+                rd.append(r[1])
+                if len(r) == 5:
+                    rd.append(r[4])
+        wr = [w[1] for w in writes]
+        for w in writes:
+            if len(w) == 5:
+                rd.append(w[4])
+        ga = sum(r[2] for r in reads if isinstance(r, tuple) and len(r) == 5)
+        d = dict(eng=eng, fn=fn, rd=rd, wr=wr, cost=cost, lat=0.0, sem=None, n=1, after=None, half=cur[0],
+                 cls="%s%d_%d" % (cur[1], cur[0], cur[2]), ga=ga)
+        cur[2] += 1
+        d.update(kw)
+        ops.append(d)
+        return d
+
+    def ap(x):
+        return x[0] if isinstance(x, tuple) else x
+
+    def two(*xs):
+        return all(x[3] in ("bfloat16", "float16", "uint16") for x in xs)
+
+    def vcost(out, ins, tt=False):
+        if len(out) == 5:
+            return 50 + out[2] * SC * CV
+        if len(ins[0]) == 5:
+            return 50 + out[2] * GA * CV
+        f = 0.5 if two(out, *ins) else 1.0
+        if tt and not any(x[1][0].startswith("ps") for x in ins):
+            f *= 2
+        return max(64, out[2] * f) * CV
+
+    def tcopy(out, a):
+        return add("v", lambda e: [e.tensor_copy(out[0], a[0])], [a], [out], vcost(out, [a]))
+
+    def tt(out, a, b, op):
+        return add("v", lambda e: [e.tensor_tensor(out[0], a[0], b[0], op)], [a, b], [out], vcost(out, [a, b], True))
+
+    def ts(out, a, s1, op0, s2=None, op1=None):
+        if op1 is None:
+            fn = lambda e: [e.tensor_scalar(out[0], a[0], ap(s1), None, op0)]
+        else:
+            fn = lambda e: [e.tensor_scalar(out[0], a[0], ap(s1), ap(s2), op0, op1)]
+        return add("v", fn, [a, s1, s2], [out], vcost(out, [a]))
+
+    def mset(out, v):
+        return add("v", lambda e: [e.memset(out[0], v)], [], [out], max(64, out[2] * (0.5 if two(out) else 1)) * CV)
+
+    def act(out, a, func, bias=None):
+        cost = 65 + out[2] * GA * CV if len(a) == 5 else max(64, out[2]) * CV
+        if bias is None:
+            fn = lambda e: [e.activation(out[0], a[0], func)]
+        else:
+            fn = lambda e: [e.activation(out[0], a[0], func, bias=bias[0])]
+        return add("s", fn, [a, bias], [out], cost)
+
+    def scale(out, a, v):
+        return add("s", lambda e: [e.activation(out[0], a[0], AF.Identity, scale=ap(v))], [a, v], [out], max(64, out[2]) * CV)
+
+    def mm(items, first=True, last=True):
+        k = len(items)
+        fn = lambda e: [e.matmul(o[0], l[0], r[0], first and i == 0, last and i == k - 1) for i, (o, l, r) in enumerate(items)]
+        cost = sum(max(64, r[2]) * (4 if r[3] == "float32" else 1) for _, _, r in items) * CPE
+        return add("p", fn, [x for _, l, r in items for x in (l, r)], [o for o, _, _ in items], cost, n=k)
+
+    def iota(out, pat, base, cm=0):
+        if out[3] == "int32":
+            fn = lambda e: [e.iota(out[0], pat, base, cm)]
+        else:
+            fn = lambda e: [e.iota(out[0], pat, base, cm, allow_small_or_imprecise_dtypes=True)]
+        return add("g", fn, [], [out], 130 + 2 * out[2] * CV)
+
+    def gcopy(out, a):
+        return add("g", lambda e: [e.affine_select(out[0], a[0], [[0, out[2]]], OP.is_gt, 0.0, 1, 0)], [a], [out],
+                   170 + 2 * out[2] * CV)
+
+    def dma(eng, sem, pairs, reads, writes, lat):
+        fn = lambda e: [e.dma_start(o, i) for o, i in pairs]
+        return add(eng, fn, reads, writes, 60.0 * len(pairs), lat=lat, sem=sem, n=len(pairs))
+
+    def sel(z, a):
+        return R(z, 15 - a, 143 - a)
+
+    idb, nid, hid, qrt = R("idb", 0, 128), R("nid", 0, 128), R("hid", 0, 128), R("qrt", 0, 128)
+    idh, nih, i128 = R("idh", 0, 128), R("nih", 0, 128), R("i128", 0, 128)
+    X = R("xw", 128, 2176)
+
+    dma("y", "dwt", [(T.wti[:, 0:1], T.wt[:])], [], [R("wti", 0, 4)], 2000)
+    dma("y", "dkp", [(T.kpi[:, 0:1], T.kap[:])], [], [R("kpi", 0, 4)], 2000)
+    dma("y", "dar", [(T.ari[:], T.arr[:])], [], [R("ari", 0, 256)], 2300)
+    dma("y", "dst", [(T.sti[:], T.st[:])], [], [R("sti", 0, 2048)], 4000)
+    dma("y", "drc", [(X[0], T.rec[:])], [], [X], 6000)
+    dma("s", "dnm", [(T.nmi[:, 16 * k:16 * k + 16], T.nm[k::8, :]) for k in range(8)], [], [R("nmi", 0, 128)], 5000)
+
+    iota(R("pi", 0, 8), [[0, 8]], 0, 1)
+    ts(C("pi", 1), C("pi", 0), 15, OP.bitwise_and)
+    ts(C("pi", 2), C("pi", 0), 7, OP.bitwise_and)
+    ts(C("pi", 3), C("pi", 0), 3, OP.arith_shift_right, 1, OP.bitwise_and)
+    ts(C("pi", 4), C("pi", 0), 4, OP.arith_shift_right)
+    ts(C("pi", 5), C("pi", 0), 1, OP.arith_shift_right, 7, OP.bitwise_and)
+    ts(C("pi", 6), C("pi", 0), 1, OP.bitwise_and)
+    tcopy(R("pf", 0, 8), R("pi", 0, 8))
+    ts(C("pc", 0), C("pf", 4), 16.0, OP.mult, 15.0, OP.add)
+    ts(C("pc", 1), C("pf", 2), 32.0, OP.mult, C("pf", 3), OP.add)
+    ts(C("pc", 2), C("pc", 1), 8.0, OP.mult)
+    ts(C("pc", 3), C("pf", 3), 64.0, OP.mult, C("pf", 2), OP.add)
+    ts(C("pc", 7), C("pf", 6), 8.0, OP.mult)
+    ts(C("pc", 4), C("pf", 5), 16.0, OP.mult, C("pc", 7), OP.add)
+    iota(R("xi", 0, 144), [[1, 144]], 0)
+    ts(R("pc", 5, 7), R("xi", 0, 2), C("pf", 1), OP.is_equal)
+    ts(R("z1", 0, 144), R("xi", 0, 144), C("pc", 0), OP.is_equal)
+    scale(R("z4", 0, 144), R("z1", 0, 144), 4096.0)
+    if NG:
+        ts(R("zn", 0, 144), R("z1", 0, 144), -4096.0, OP.mult)
+    tcopy(C("wtf", 0), C("wti", 0))
+    tcopy(C("kpf", 0), C("kpi", 0))
+    scale(R("zw", 0, 144), R("z1", 0, 144), C("wtf", 0))
+    ts(idb, R("xi", 0, 128), C("pf", 0), OP.is_equal)
+    scale(nid, idb, -1.0)
+    scale(hid, idb, 0.5)
+    for o, v in ((idh, 1.0), (nih, -1.0), (i128, 128.0)):
+        ts(o, idb, v, OP.mult)
+    mset(qrt, -0.25)
+    iota(R("one", 0, 128), [[0, 128]], 1)
+    iota(R("zer", 0, 128), [[0, 128]], 0)
+    iota(R("i4", 0, 16), [[2, 16]], 0)
+    ts(R("larr", 0, 16), R("i4", 0, 16), C("pc", 1), OP.add)
+    ts(R("ti8", 0, 16), R("i4", 0, 16), 8.0, OP.mult, C("pc", 2), OP.add)
+    iota(R("i3", 0, 64), [[1, 8], [16, 8]], 0)
+    for h in range(2):
+        ts(R("lst", 64 * h, 64 * h + 64), R("i3", 0, 64), C("pc", 2), OP.add, 128.0 * h, OP.add)
+    iota(R("i7", 0, 64), [[128, 8], [0, 8]], 0)
+    iota(R("i8", 0, 64), [[0, 8], [16, 8]], 0)
+    tcopy(R("pk", 0, 64), R("i7", 0, 64))
+    ts(R("pb", 0, 64), R("i8", 0, 64), C("pf", 1), OP.add)
+    tt(R("posk", 0, 64), R("pk", 0, 64), R("pb", 0, 64), OP.add)
+    tcopy(R("poskh", 0, 64), R("posk", 0, 64))
+    ts(R("ck", 0, 64), R("i7", 0, 64), -1.0, OP.mult, 1024.0, OP.add)
+    iota(R("pa", 0, 8 * NB), [[128, NB], [0, 8]], 128 * code(0))
+    iota(R("pa", 8 * NB, 128), [[128, 16 - NB], [0, 8]], 128 * code(NB))
+    ts(R("lrep", 0, 8), R("xi", 0, 8), 0.0, OP.mult, C("pf", 2), OP.add)
+    ts(C("pc", 7), C("pf", 3), 16.0, OP.mult, C("pf", 2), OP.add)
+    iota(R("i6", 0, 8), [[8, 2], [32, 4]], 0)
+    ts(R("lperm", 0, 8), R("i6", 0, 8), C("pc", 7), OP.add)
+    ts(R("linv", 0, 8), R("xi", 0, 8), 8.0, OP.mult, C("pc", 3), OP.add)
+    iota(R("i5", 0, 16), [[1, 8], [128, 2]], 0)
+    ts(R("lzo", 0, 16), R("i5", 0, 16), C("pc", 4), OP.add)
+    for h in range(2):
+        ts(R("dfl", 8 * h, 8 * h + 8), R("pb", 0, 8), 16384.0 + 2048 * h, OP.add)
+        iota(R("jc", 24 * h, 24 * h + 24), [[4096, 3], [0, 8]], 4096 + 128 * (1 - h))
+    iota(R("i1", 0, 128), [[1, 8], [0, 16]], 0)
+    iota(R("i2", 0, 128), [[1, 16], [0, 8]], 0)
+    ts(R("blk", 0, 128), R("i1", 0, 128), C("pf", 4), OP.is_equal)
+    ts(R("m16", 0, 128), R("i2", 0, 128), C("pf", 1), OP.is_equal, C("kpf", 0), OP.mult)
+    mm([(R("ps5", 0, 128), R("blk", 0, 128), R("m16", 0, 128))])
+    tcopy(R("kapr", 0, 128), R("ps5", 0, 128))
+    ts(R("k0j", 0, 3), R("xi", 1, 4), C("kapr", 0), OP.mult, -31.0 / 64, OP.add)
+    tcopy(R("ofc", 0, 3), R("k0j", 0, 3))
+    tcopy(R("kq", 0, 16), R("kapr", 0, 128, 8))
+    ts(R("kq", 16, 32), R("kq", 0, 16), 31, OP.bitwise_and)
+    tt(R("kq", 32, 48), R("kq", 0, 16), R("kq", 16, 32), OP.subtract)
+    ts(R("kqf", 0, 16), R("kq", 16, 32), C("pc", 5), OP.mult)
+    ts(R("kqf", 16, 32), R("kq", 32, 48), C("pc", 6), OP.mult)
+    tt(R("kqf", 32, 48), R("kqf", 0, 16), R("kqf", 16, 32), OP.add)
+    def zero(name, lo, hi):
+        for c in range(lo, hi, 256):
+            iota(R(name, c, min(hi, c + 256)), [[0, min(hi, c + 256) - c]], 0)
+
+    zero("kt", 0, 256)
+    zero("kt", 128 * (NB + 1), 128 * 17)
+    for m in range(1, 16):
+        act(R("kt", 128 * code(m), 128 * code(m) + 128), R("zer", 0, 128), AF.Identity, C("kqf", 32 + m))
+    for h in range(2):
+        zero("dw%d" % h, 0, 128)
+        zero("dw%d" % h, 128 * (NB + 1), 128 * (17 - max(AL)))
+        mset(R("nm%d" % h, 64, 96), BIG)
+        mset(R("hh%d" % h, 120, 128), 1.0)
+        tcopy(R("nm%d" % h, 0, 64), G(R("nmi", 0, 128), R("lperm", 4 * h, 4 * h + 4)))
+        tcopy(R("zz", 128 * h, 128 * h + 128), G(R("ari", 0, 256), R("larr", 8 * h, 8 * h + 8)))
+
+    lrep8, lrep4 = R("lrep", 0, 8), R("lrep", 0, 4)
+
+    def names(h, tag):
+        s = str(h)
+        cur[:] = [h, tag, 0]
+        return dict(tf="tf" + s, dw="dw" + s, ab="ab" + s, ge="ge" + s, kg="kg" + s, d7="d7" + s, e1="e1" + s, tr="tr" + s,
+                    si="si" + s, tt="tt" + s, c16="c16" + s, l16="l16" + s, src="src" + s, nm="nm" + s, hh="hh" + s,
+                    sf="sf" + s, A="ps%d" % (4 * h), B="ps%d" % (4 * h + 1), Cb="ps%d" % (4 * h + 2), D="ps%d" % (4 * h + 3))
+
+    def lsum(out, z, src, lo, hi, pre=()):
+        return mm(list(pre) + [(out, sel(z, a), R(src, lo + a, hi, 16)) for a in range(16)])
+
+    def settle(n, w, slot, parts, main=True):
+        ps = R(n["D"], 0, 128)
+        mm([(ps, idb, qrt), (ps, hid, parts[0])], True, False)
+        mm([(ps, hid, p) for p in parts[1:]], False, True)
+        if main:
+            s = R(n["dw"], 2048, 2176)
+            ts(s, ps, MAGIC, OP.add, -MAGIC, OP.add)
+            if max(AL) > 1:
+                gcopy(R(n["dw"], 1920, 2048), s)
+            gcopy(R(w[0], w[1] + slot, w[1] + slot + 128), s)
+        else:
+            ts(R(w[0], w[1] + slot, w[1] + slot + 128), ps, MAGIC, OP.add, -MAGIC, OP.add)
+
+    def rows(t, h):
+        n = names(h, "r")
+        w = "w%d" % (t % 2)
+        if t == 0:
+            win, lst, l0 = R("sti", 0, 2048), "lst", 64 * h
+        else:
+            win, lst, l0 = R("w%d" % ((t - 1) % 2), 1536 * h, 1536 * h + 1536), n["src"], 0
+        lv = 2 if t == 0 else LV
+        cur[2] = 5 if t == 0 else 0
+        for a, b, eng in ((0, lv, "v"), (lv, 4, "s"), (4, 8, "s")):
+            if a == b:
+                continue
+            o = R(w, 1536 * h + 128 * a, 1536 * h + 128 * b)
+            src = G(win, R(lst, l0 + 8 * a, l0 + 8 * b))
+            if eng == "v":
+                tcopy(o, src)
+            else:
+                act(o, src, AF.Copy)
+
+    def store(t, h):
+        n = names(h, "s")
+        si = n["si"]
+        z0 = 256 * t + 128 * h
+        ps = R(n["A"], 0, 8)
+        lsum(ps, "z1", "zz", z0, z0 + 128)
+        tcopy(R(si, 0, 8), ps)
+        ts(R(si, 8, 16), R(si, 0, 8), 7, OP.bitwise_and)
+        tt(R(si, 16, 24), R(si, 8, 16), R("ti8", 8 * h, 8 * h + 8), OP.add)
+        tcopy(R(n["l16"], 0, 8), R(si, 16, 24))
+        tcopy(G(X, R(n["l16"], 0, 8)), R("zz", z0, z0 + 128))
+
+    def gap(t, h):
+        n = names(h, "g")
+        si, tr, hh, nm = n["si"], n["tr"], n["hh"], n["nm"]
+        w = ("w%d" % (t % 2), 1536 * h)
+        z = R("zz", 256 * t + 128 * h, 256 * t + 128 * h + 128)
+        for q, b in enumerate((n["Cb"], n["D"])):
+            mm([(R(b, 0, 512), idb, R(w[0], w[1] + 512 * q, w[1] + 512 * q + 512))]
+               + [(R(b, 128 * k, 128 * k + 128), nid, z) for k in range(4)])
+            act(R(n["ab"], 512 * q, 512 * q + 512), R(b, 0, 512), AF.Abs)
+        ps = R(n["B"], 0, 64)
+        lsum(ps, "z4", n["ab"], 0, 1024, [(ps, idb, R("pk", 0, 64)), (ps, idb, R("pb", 0, 64))])
+        act(R(n["e1"], 0, 32), R(n["B"], 32, 64), AF.Copy)
+        tt(R(tr, 0, 32), R(n["B"], 0, 32), R(n["e1"], 0, 32), OP.min)
+        tt(R(tr, 96, 112), R(tr, 0, 16), R(tr, 16, 32), OP.min)
+        tt(R(si, 24, 32), R(tr, 96, 104), R(tr, 104, 112), OP.min)
+        off = R(si, 32, 40)
+        ts(off, R(si, 24, 32), 4095, OP.bitwise_and)
+        tcopy(R(n["l16"], 8, 16), off)
+        ge = R(n["ge"], 0, 128)
+        act(ge, G(R(w[0], w[1], w[1] + 1024), R(n["l16"], 8, 16)), AF.Copy)
+        settle(n, w, 1024, [z, ge])
+        H = lambda i, a=0, b=64: R(hh, 64 * i + a, 64 * i + b)
+        tt(H(2), G(off, lrep4), R("posk", 0, 64), OP.is_gt)
+        tt(H(0), R(hh, 120, 184), H(2), OP.subtract)
+        for j in (1, 2, 3):
+            tt(H(3 + j), H(0), R(nm, 8 * j, 8 * j + 64), OP.mult)
+            pj = R(n["B"], 64 + 8 * j, 72 + 8 * j)
+            mm([(pj, idh, H(3 + j, 8 * k, 8 * k + 8)) for k in range(8)])
+            if j == 1:
+                ts(R(n["l16"], 16, 24), pj, 2047.0, OP.min)
+        ts(R(n["l16"], 24, 40), R(n["B"], 80, 96), 2047.0, OP.min)
+        tt(R(n["sf"], 0, 24), R(n["B"], 72, 96), R("jc", 24 * h, 24 * h + 24), OP.add)
+        tcopy(R(n["sf"], 24, 48), R(n["l16"], 16, 40))
+        tt(H(3), H(0), R("ck", 0, 64), OP.mult)
+        b = n["Cb"]
+        mm([(R(b, 0, 64), idh, R("poskh", 0, 64)), (R(b, 0, 64), i128, H(2))]
+           + [(R(b, 8 * j, 64), idh, H(3, 0, 64 - 8 * j)) for j in range(4)])
+        tcopy(R(n["src"], 0, 64), R(b, 0, 64))
+        tt(H(7, 0, 56), R(nm, 8, 64), H(2, 0, 56), OP.mult)
+        tt(H(8), G(R(si, 16, 24), lrep4), H(0), OP.mult)
+        if t == RO - 1:
+            ts(R("srf", 64 * h, 64 * h + 64), R(b, 0, 64), 1536.0 * h, OP.add)
+
+    def corr(t, h, j):
+        n = names(h, "abc"[j - 1])
+        si, tr, dw, ab, tw = n["si"], n["tr"], n["dw"], n["ab"], n["tt"]
+        w = ("w%d" % (t % 2), 1536 * h)
+        s = R(dw, 2048, 2176)
+        D = lambda m0, m1: R(dw, 128 * code(m0), 128 * code(m1 - 1) + 128)
+        L = lambda m0, m1: R(n["c16"], 8 * m0, 8 * m1)
+        act(D(0, 1), G(X, R(n["l16"], 8 + 8 * j, 16 + 8 * j)), AF.Copy)
+        if j == 3:
+            settle(n, w, 1408, [s, D(0, 1)], False)
+            z = R("zz", 256 * t + 128 * h, 256 * t + 128 * h + 128)
+            tt(R(n["d7"], 0, 128), G(R(w[0], w[1], w[1] + 1536), R(n["src"], 56, 64)), z, OP.subtract)
+            act(R("xw", 2176 * h, 2176 * h + 128), R(n["d7"], 0, 128), AF.Abs)
+        ps = R(n["A"], 0, 8)
+        lsum(ps, "zw", dw, 2048, 2176)
+        u, f = R(si, 48 + 8 * j, 56 + 8 * j), R(si, 72 + 8 * j, 80 + 8 * j)
+        tcopy(R(si, 40, 48), ps)
+        ts(u, R(si, 40, 48), 2047, OP.bitwise_and)
+        sf, tf = n["sf"], n["tf"]
+        tt(R(sf, 96, 104), u, u, OP.mult)
+        tt(R(tf, 0, 128), G(u, lrep8), R("kapr", 0, 128), OP.mult)
+        ts(f, R(sf, 96, 104), 1.0 / 32, OP.mult, C("ofc", 4 * (t % 2) + j - 1), OP.add)
+        tt(R(tw, 0, 128), G(f, lrep8), R(tf, 0, 128), OP.add)
+        ts(R(tw, 136, 256), R(tw, 8, 128), 2047, OP.bitwise_and)
+        tcopy(L(1, 16), R(tw, 136, 256))
+        for b, m0, m1 in ((n["Cb"], 0, 4), (n["D"], 4, NB)):
+            act(D(max(m0, 1), m1), G(X, L(max(m0, 1), m1)), AF.Copy)
+            k = m1 - m0
+            mm([(R(b, 0, 128 * k), idb, D(m0, m1))] + [(R(b, 128 * i, 128 * i + 128), nid, s) for i in range(k)])
+            act(R(ab, 128 * m0, 128 * m1), R(b, 0, 128 * k), AF.Abs)
+        m = NB
+        for k in AL:
+            tt(D(m, m + k), G(X, L(m, m + k)), R(dw, 2176 - 128 * k, 2176), OP.subtract)
+            m += k
+        m = NB
+        for k in AB:
+            if m < 16 - NG:
+                act(R(ab, 128 * m, 128 * (m + k)), D(m, m + k), AF.Abs)
+            else:
+                ts(R(ab, 128 * m, 128 * (m + k)), D(m, m + k), 0.0, OP.max, 2.0, OP.mult)
+            m += k
+        p1, p2 = R(n["A"], 256, 320), R(n["B"], 0, 64)
+        lsum(p1, "z4", ab, 0, 1024, [(p1, idb, R("pa", 0, 64)), (p1, idb, R("pb", 0, 64))])
+        act(R(n["e1"], 0, 64), p1, AF.Copy)
+        pre = [(p2, idb, R("pa", 64, 128)), (p2, idb, R("pb", 0, 64))]
+        if NG:
+            pre += [(R(n["B"], 64 - 8 * NG, 64), sel("zn", a), R(dw, 128 * code(16 - NG) + a, DWW, 16)) for a in range(16)]
+        mm(pre, True, False)
+        mm([(p2, sel("z4", a), R(ab, 1024 + a, 2048, 16)) for a in range(16)], False, True)
+        tt(R(tr, 0, 64), p2, R(n["e1"], 0, 64), OP.min)
+        tt(R(tr, 64, 96), R(tr, 0, 32), R(tr, 32, 64), OP.min)
+        tt(R(tr, 96, 112), R(tr, 64, 80), R(tr, 80, 96), OP.min)
+        key = R(si, 24, 32)
+        tt(key, R(tr, 96, 104), R(tr, 104, 112), OP.min)
+        o = 88 + 16 * j
+        off = R(si, o, o + 8)
+        ts(off, key, 4095, OP.bitwise_and)
+        ts(R(si, o + 8, o + 16), key, 2048 + 127, OP.bitwise_and)
+        lo = 24 + 16 * j
+        kj = R(sf, 40 + 8 * j, 48 + 8 * j)
+        ts(kj, off, 256.0, OP.is_lt, BIG, OP.mult)
+        tt(R(sf, 104, 112), kj, R(sf, 8 * j - 8, 8 * j), OP.add)
+        run = R(si, 168, 176) if j == 3 else R(sf, 112, 120)
+        tt(run, R(sf, 104, 112), R("dfl", 8 * h, 8 * h + 8) if j == 1 else R(sf, 112, 120), OP.min)
+        if j == 3:
+            ts(R(si, 176, 184), run, 4095, OP.bitwise_and)
+            tcopy(R(n["l16"], 88, 96), R(si, 176, 184))
+            ob = R("ob", 256 * t + 128 * h, 256 * t + 128 * h + 128)
+            if OBV:
+                tcopy(ob, G(R("xw", 128 * h, 128 * h + 2176), R(n["l16"], 88, 96)))
+            else:
+                act(ob, G(R("xw", 128 * h, 128 * h + 2176), R(n["l16"], 88, 96)), AF.Copy)
+            snd = add("g", None, [ob], [], 300.0, sem="sent", send=(t, h), src=ob[0])
+            zn = R("zz", 256 * (t + 1) + 128 * h, 256 * (t + 1) + 128 * h + 128)
+            add("x", None, [], [zn], 0.0, lat=COMM, sem="ar%d" % (2 * t + h), after=snd, recv=(t, h))
+            cur[2] += 100
+            if t < RO - 1:
+                ts(R("rel", 8 * h, 8 * h + 8), run, 16384.0, OP.is_lt)
+                cur[2] -= 1
+            cur[2] -= 100
+        tcopy(R(n["l16"], lo, lo + 16), R(si, o, o + 16))
+        if GS:
+            act(R(n["ge"], 0, 128), G(R(dw, 0, DWW), R(n["l16"], lo, lo + 8)), AF.Copy)
+            tcopy(R(n["ge"], 128, 256), G(R(dw, 0, DWW), R(n["l16"], lo + 8, lo + 16)))
+        else:
+            act(R(n["ge"], 0, 256), G(R(dw, 0, DWW), R(n["l16"], lo, lo + 16)), AF.Copy)
+        settle(n, w, 1024 + 128 * j, [s, R(n["ge"], 0, 128), R(n["ge"], 128, 256)], j < 3)
+        act(R(n["kg"], 128 * j - 128, 128 * j), G(R("kt", 0, DWW), R(n["l16"], lo, lo + 8)), AF.Copy)
+
+    def rename(t, h):
+        n = names(h, "n")
+        si, hh, nm, sf = n["si"], n["hh"], n["nm"], n["sf"]
+        H = lambda i, a=0, b=64: R(hh, 64 * i + a, 64 * i + b)
+        ps = R(n["Cb"], 0, 24)
+        lsum(ps, "z1", n["kg"], 0, 384)
+        tt(R(sf, 120, 144), ps, R(si, 56, 80), OP.mult)
+        tt(R(si, 208, 232), R(sf, 120, 144), R(si, 80, 104), OP.add)
+        ts(R(si, 232, 256), R(si, 208, 232), 2047, OP.bitwise_and)
+        tt(R(sf, 144, 168), R(si, 232, 256), R(sf, 24, 48), OP.subtract)
+        ts(R(sf, 168, 192), R(sf, 48, 72), 1.0, OP.is_lt)
+        tt(R(sf, 72, 96), R(sf, 144, 168), R(sf, 168, 192), OP.mult)
+        for j in (1, 2, 3):
+            tt(H(8 + j), G(R(sf, 64 + 8 * j, 72 + 8 * j), lrep4), H(0), OP.mult)
+        b = n["Cb"]
+        mm([(R(b, 64 + 8 * j, 128), idh, H(8 + j, 0, 64 - 8 * j)) for j in range(4)]
+           + [(R(b, 72, 128), idh, R(nm, 8, 64)), (R(b, 64, 120), idh, H(7, 0, 56)), (R(b, 72, 128), nih, H(7, 0, 56))])
+        if t < RO - 1:
+            tcopy(R(nm, 0, 64), R(b, 64, 128))
+        else:
+            tcopy(R("nmf", 64 * h, 64 * h + 64), R(b, 64, 128))
+
+    def count(t):
+        cur[:] = [0, "k", 0]
+        ps = R("ps4", 384, 385)
+        mm([(ps, R("one", 0, 128), C("rel", c)) for c in range(16)])
+        tcopy(C("cnt", 0), ps)
+        ts(C("cnt", 8), C("cnt", 0), 63, OP.bitwise_and)
+        tcopy(C("cntf", 0), C("cnt", 8))
+        q = 4 * ((t + 1) % 2)
+        ts(R("ofc", q, q + 3), R("k0j", 0, 3), C("cntf", 0), OP.add)
+
+    for t in range(RO):
+        for h in range(2):
+            rows(t, h)
+            store(t, h)
+        for h in range(2):
+            gap(t, h)
+        if t == RO - 1:
+            tcopy(R("srp", 0, 128), G(R("srf", 0, 128), R("linv", 0, 8)))
+            dd = (None, ("dfl_d", 0, 128))
+            dma("y", "dr1", [(T.dfl_d[k::8, :], T.srp[:, 16 * k:16 * k + 16]) for k in range(8)], [R("srp", 0, 128)], [dd], 4000)
+            dma("y", "dr2", [(T.fl[:], T.dfl_d[:])], [dd], [R("fl", 0, 128)], 2500)
+        for j in (1, 2, 3):
+            for h in range(2):
+                corr(t, h, j)
+        for h in range(2):
+            rename(t, h)
+        if t < RO - 1:
+            count(t)
+
+    cur[:] = [0, "o", 0]
+    win = R("w%d" % ((RO - 1) % 2), 0, 3072)
+    act(R("sob", 0, 1024), G(win, R("fl", 0, 64)), AF.Copy)
+    tcopy(R("sob", 1024, 2048), G(win, R("fl", 64, 128)))
+    dma("s", "dso0", [(T.so[:, 0:1024], T.sob[:, 0:1024])], [R("sob", 0, 1024)], [], 3000)
+    dma("y", "dso1", [(T.so[:, 1024:2048], T.sob[:, 1024:2048])], [R("sob", 1024, 2048)], [], 3000)
+    tcopy(R("mob", 0, 128), G(R("nmf", 0, 128), R("linv", 0, 8)))
+    for q, (eng, sem) in enumerate((("y", "dmo"), ("s", "dm2"))):
+        dma(eng, sem, [(T.mo[k::8, :], T.mob[:, 16 * k:16 * k + 16]) for k in range(4 * q, 4 * q + 4)], [R("mob", 0, 128)], [], 3500)
+    tcopy(R("zob", 0, 256), G(R("zz", 256 * RO, 256 * RO + 256), R("lzo", 0, 16)))
+    dma("s", "dzo", [(T.zo[:], T.zob[:])], [R("zob", 0, 256)], [], 2500)
+    return ops
+
+
+def link(ops):
+    hist = {}
+    deps = []
+    for i, o in enumerate(ops):
+        d = {}
+        if o["after"] is not None:
+            d[[k for k in range(i) if ops[k] is o["after"]][0]] = False
+        for kind, regs in (("r", o["rd"]), ("w", o["wr"])):
+            for name, lo, hi in regs:
+                psum = name.startswith("ps")
+                for k, kk, l2, h2 in hist.get(name, ()):
+                    if k == i:
+                        continue
+                    same = ops[k]["eng"] == o["eng"] and ops[k]["sem"] is None
+                    over = lo < h2 and l2 < hi
+                    if psum and not same:
+                        d[k] = True
+                    elif psum and o["eng"] == "p":
+                        d.setdefault(k, False)
+                    elif over and (kind == "w" or kk == "w"):
+                        d[k] = True
+        for kind, regs in (("r", o["rd"]), ("w", o["wr"])):
+            for name, lo, hi in regs:
+                hl = hist.setdefault(name, [])
+                if name.startswith("ps"):
+                    if o["eng"] == "p":
+                        hl[:] = [x for x in hl if x[0] == i]
+                elif kind == "w":
+                    hl[:] = [x for x in hl if not (lo <= x[2] and x[3] <= hi)]
+                hl.append((i, kind, lo, hi))
+        deps.append(d)
+    return deps
+
+
+def schedule(ops, deps):
+    n = len(ops)
+    if "succ" not in ops[0]:
+        succ = [[] for _ in range(n)]
+        for i in range(n):
+            for k, w in deps[i].items():
+                succ[k].append((i, ops[k]["lat"] + LAT if w else 0.0))
+        base = [0.0] * n
+        for i in range(n - 1, -1, -1):
+            base[i] = ops[i]["cost"] + max([d + base[k] for k, d in succ[i]] + [ops[i]["lat"]])
+        ops[0]["succ"] = succ
+        ops[0]["base"] = [base[i] - BIAS * ops[i]["half"] - 1e-3 * i for i in range(n)]
+    succ = ops[0]["succ"]
+    prio = [b + 100.0 * OFFS.get(o["cls"], 0) for b, o in zip(ops[0]["base"], ops)]
+    slack = [SLACK + 20.0 * max(0, OFFS.get(o["cls"] + "w", 0)) for o in ops]
+    left = [len(d) for d in deps]
+    ready_at = [0.0] * n
+    ready = {}
+    for i in range(n):
+        if left[i] == 0:
+            ready.setdefault(ops[i]["eng"], []).append(i)
+    free = {}
+    order = []
+    end = 0.0
+    while len(order) < n:
+        best = None
+        for e, lst in ready.items():
+            if not lst:
+                continue
+            f = free.get(e, 0.0)
+            first = max(f, min([ready_at[i] for i in lst]))
+            if best is None or first < best[0]:
+                best = (first, e)
+        first, e = best
+        i = max([i for i in ready[e] if ready_at[i] <= first + slack[i]], key=lambda i: prio[i])
+        st = max(free.get(e, 0.0), ready_at[i])
+        ready[e].remove(i)
+        o = ops[i]
+        fin = st + o["cost"]
+        free[e] = fin
+        o["t0"] = st
+        end = max(end, fin + o["lat"])
+        order.append(i)
+        for k, d in succ[i]:
+            if fin + d > ready_at[k]:
+                ready_at[k] = fin + d
+            left[k] -= 1
+            if left[k] == 0:
+                ready.setdefault(ops[k]["eng"], []).append(k)
+    return order, end
+
+
+SLACK = 30.0
+BIAS = 3000.0
+ITER = 3500
+OFFS = {}
+PLAN = {}
+SETS = [(1.2, 60.0, 0.5, 3000.0), (1.56, 90.0, 0.5, 3500.0), (1.9, 60.0, 0.5, 4000.0), (1.56, 150.0, 0.6, 4000.0)]
+
+
+def replay(rows, order, s):
+    lat = SETS[s][1]
+    fin = [0.0] * len(rows)
+    done = [0.0] * len(rows)
+    free = {}
+    for i in order:
+        e, cs, ls, hard, soft = rows[i]
+        st = free.get(e, 0.0)
+        for k in hard:
+            if done[k] > st:
+                st = done[k]
+        for k in soft:
+            if fin[k] > st:
+                st = fin[k]
+        fin[i] = free[e] = st + cs[s]
+        done[i] = st + cs[s] + ls[s] + lat
+    return max(done)
+
+
+def tune(T):
+    ops = build(T, 3)
+    deps = link(ops)
+    rows = [(o["eng"], [(o["cost"] + o["ga"] * (ga - GA)) * (cpe / CPE if o["eng"] == "p" else 1.0) for ga, _, cpe, _ in SETS],
+             [cm if o["eng"] == "x" else o["lat"] for _, _, _, cm in SETS],
+             [k for k, w in d.items() if w], [k for k, w in d.items() if not w]) for o, d in zip(ops, deps)]
+
+    def score():
+        order, _ = schedule(ops, deps)
+        return sum(replay(rows, order, s) for s in range(len(SETS)))
+
+    cls = sorted(set(o["cls"] for o in ops if o["eng"] in "vsp"))
+    seed = [12345]
+
+    def rnd(k):
+        seed[0] = (seed[0] * 1103515245 + 12345) % 2147483648
+        return (seed[0] >> 8) % k
+
+    best = score()
+    for _ in range(ITER):
+        old = dict(OFFS)
+        for _ in range((1, 3, 6)[rnd(3)]):
+            c = cls[rnd(len(cls))]
+            if rnd(3) == 0:
+                OFFS[c + "w"] = (0, 3, 8, 20)[rnd(4)]
+            else:
+                OFFS[c] = OFFS.get(c, 0) + (-20, -8, -3, -1, 1, 3, 8, 20)[rnd(8)]
+        s = score()
+        if s <= best:
+            best = s
+        else:
+            OFFS.clear()
+            OFFS.update(old)
+    return best / len(SETS)
+
+
+def route(T, topo, t, r):
+    src, dst = T.cores[r], T.cores[(r + 1 + t % 3) % NR]
+    if topo.may_write(src, dst):
+        return dst, dst
+    ok = [c for c in topo.cores_of(src) if T.rank_of(c) is None and topo.may_write(c, dst)]
+    near = [c for c in ok if topo.die(c) == topo.die(src)]
+    return (near or ok)[0], dst
+
+
+def arrivals(T, topo, t, r):
+    q = (r - 1 - t % 3) % NR
+    hop, dst = route(T, topo, t, q)
+    return len(topo.engines(T.cores[q] if hop == dst else hop, dst))
+
+
+def relay_program(g, core, T, topo):
+    sent = 0
+    for t in range(RO):
+        for r in range(NR):
+            hop, dst = route(T, topo, t, r)
+            if hop != core or hop == dst:
+                continue
+            rid, pid = topo.addr(dst, core)
+            for h in range(2):
+                sem = T.sem["ar%d" % (2 * t + h)]
+                z = T.zz[:, 256 * (t + 1) + 128 * h:256 * (t + 1) + 128 * h + 128]
+                g.wait_ge(sem, len(topo.engines(T.cores[r], core)))
+                g.remote_dma(z, z, sem, T.sem.sent, pid, rid, topo.mask(core, dst))
+                sent += len(topo.engines(core, dst))
+    if sent:
+        g.wait_ge(T.sem.sent, sent)
+
+
+def rank_program(g, core, T, topo):
+    rank = T.rank_of(core)
+    if rank is None:
+        relay_program(g, core, T, topo)
+        return
+    ops = build(T)
+    if not PLAN:
+        PLAN["tuned"] = tune(T)
+        deps = link(ops)
+        PLAN["deps"] = deps
+        PLAN["order"], PLAN["end"] = schedule(ops, deps)
+        PLAN["ops"] = ops
+    deps = PLAN["deps"]
+    queue = {"v": g.vector, "s": g.scalar, "p": g.tensor, "g": g, "y": g.sync}
+    csem = {"v": "cv", "s": "cs", "p": "cp", "g": "cg"}
+    count = {}
+    known = {e: {} for e in queue}
+    mark = {}
+    for i in PLAN["order"]:
+        o = ops[i]
+        e = o["eng"]
+        if e == "x":
+            t, h = o["recv"]
+            mark[i] = (o["sem"], arrivals(T, topo, t, rank), {})
+            count[o["sem"]] = mark[i][1]
+            continue
+        kn = known[e]
+        need = sorted((mark[k] for k, w in deps[i].items() if w), key=lambda m: -len(m[2]))
+        top = {}
+        for s, v, _ in need:
+            top[s] = max(top.get(s, 0), v)
+        for s, v, clock in need:
+            if v == top[s] and kn.get(s, 0) < v:
+                queue[e].wait_ge(T.sem[s], v)
+                kn[s] = v
+                for s2, v2 in clock.items():
+                    kn[s2] = max(kn.get(s2, 0), v2)
+        if "send" in o:
+            t, h = o["send"]
+            hop, _ = route(T, topo, t, rank)
+            rid, pid = topo.addr(hop, core)
+            z = T.zz[:, 256 * (t + 1) + 128 * h:256 * (t + 1) + 128 * h + 128]
+            g.remote_dma(z, o["src"], T.sem["ar%d" % (2 * t + h)], T.sem.sent, pid, rid, topo.mask(core, hop))
+            count["sent"] = count.get("sent", 0) + len(topo.engines(core, hop))
+            mark[i] = ("sent", count["sent"], dict(kn))
+            continue
+        ins = o["fn"](queue[e])
+        if o["sem"] is not None:
+            s = o["sem"]
+            for x in ins:
+                x.then_inc(T.sem[s], 16)
+            count[s] = 16 * len(ins)
+        else:
+            s = csem[e]
+            ins[-1].then_inc(T.sem[s], 1)
+            count[s] = count.get(s, 0) + 1
+        mark[i] = (s, count[s], dict(kn))
+    for s, v in count.items():
+        g.wait_ge(T.sem[s], v)

@@ -1,24 +1,28 @@
-from concourse.bass import DstId, RemoteDMATransfer
-from concourse.mybir import dt, AluOpType, AxisListType, ActivationFunctionType
+from concourse.mybir import AluOpType, ActivationFunctionType
 
 OP = AluOpType
 AF = ActivationFunctionType
 RO, NR = 5, 8
 NB = 6
-NG = 0
-AL = [1] * 10
-AB = [2] * 5
-GS = False
-OBV = False
-LV = 0
+Z1 = 9
+AL = [2] * 5
+SG = [(3, 0, 1), (2, 1, 4), (3, 4, 6)]
+SP = [(0, 16)]
+RG = [(0, 2, "v"), (2, 4, "s"), (4, 6, "v"), (6, 8, "s")]
+SI = True
 F16 = "float16"
 MAGIC = 12582912.0
-BIG = 32768.0
+BIG = 33554432.0
+Z2 = 16 - Z1
 DWW = 128 * (17 + 16 - NB)
 
 
 def code(m):
-    return m + 1 if m < NB else 17 + m - NB
+    return 15 - NB + m if m < NB else 17 + m - NB
+
+
+def span(z):
+    return 16 * ((143 * z) // 16)
 
 
 SCRATCH = {}
@@ -29,51 +33,54 @@ def _sb(name, w, d):
 
 
 for _n, _w, _d in [
-    ("xw", 2304, "bfloat16"), ("sti", 2048, "bfloat16"), ("ari", 256, "bfloat16"), ("zz", 6 * 256, "bfloat16"),
-    ("ob", 5 * 256, "bfloat16"), ("w0", 3072, "bfloat16"), ("w1", 3072, "bfloat16"), ("kt", DWW, "bfloat16"),
-    ("sob", 2048, "bfloat16"), ("zob", 256, "bfloat16"), ("nmi", 128, "int32"), ("nmf", 128, "float32"),
-    ("mob", 128, "float32"), ("srf", 128, "int32"), ("srp", 128, "uint16"), ("fl", 128, "uint16"),
-    ("wti", 4, "int32"), ("kpi", 4, "int32"), ("wtf", 4, "float32"), ("kpf", 4, "float32"),
-    ("pi", 8, "int32"), ("pf", 8, "float32"), ("pc", 8, "float32"), ("xi", 144, "float32"), ("i1", 128, "float32"),
-    ("i2", 128, "float32"), ("i3", 64, "float32"), ("i4", 16, "float32"), ("i5", 16, "float32"), ("i6", 8, "float32"),
-    ("i7", 64, "float32"), ("i8", 64, "float32"),
-    ("z1", 144, "bfloat16"), ("z4", 144, "bfloat16"), ("zw", 144, "bfloat16"), ("zn", 144, "bfloat16"),
-    ("idb", 128, "bfloat16"), ("nid", 128, "bfloat16"), ("hid", 128, "bfloat16"), ("one", 128, "bfloat16"),
-    ("qrt", 128, "bfloat16"), ("zer", 128, "bfloat16"),
-    ("idh", 128, F16), ("nih", 128, F16), ("i128", 128, F16), ("blk", 128, "float32"), ("m16", 128, "float32"),
-    ("kapr", 128, "float32"), ("kq", 64, "int32"), ("kqf", 64, "float32"), ("k0j", 8, "float32"),
-    ("posk", 64, "float32"), ("poskh", 64, F16), ("ck", 64, F16), ("pa", 128, "bfloat16"), ("pb", 64, "bfloat16"),
-    ("pk", 64, "bfloat16"), ("ti8", 16, "float32"), ("dfl", 16, "float32"), ("jc", 48, "float32"),
-    ("lrep", 8, "uint16"), ("lperm", 8, "uint16"), ("linv", 8, "uint16"), ("larr", 16, "uint16"),
-    ("lzo", 16, "uint16"), ("lst", 128, "uint16"),
-    ("rel", 16, "bfloat16"), ("cnt", 16, "int32"), ("cntf", 8, "float32"), ("ofc", 8, "float32"),
+    ("zz", 6 * 256, "bfloat16"), ("ob", 5 * 256, "bfloat16"), ("w0", 3072, "bfloat16"), ("w1", 3072, "bfloat16"),
+    ("pi", 16, "int32"), ("pf", 16, "float32"), ("pc", 16, "float32"), ("xi", 144, "float32"), ("i1", 128, "float32"),
+    ("i2", 128, "float32"), ("i3", 128, "float32"), ("i4", 32, "float32"), ("i6", 144, "float32"), ("i7", 64, "float32"),
+    ("i8", 64, "float32"), ("i9", 200, "float32"), ("ia", 200, "float32"), ("ib", 32, "float32"),
+    ("z1", 144, "bfloat16"), ("z4", 144, "bfloat16"), ("zq", 144, "bfloat16"), ("idb", 128, "bfloat16"),
+    ("nid", 128, "bfloat16"), ("hid", 128, "bfloat16"), ("one", 128, "bfloat16"), ("qrt", 128, "bfloat16"),
+    ("idh", 128, F16), ("nih", 128, F16), ("i128", 128, F16), ("bz", 144, F16), ("by", 144, F16),
+    ("blk", 128, "float32"), ("mk8", 16, "float32"), ("k0j", 8, "float32"),
+    ("posk", 64, "float32"), ("poskh", 64, F16), ("ck", 64, F16), ("pa", 200, "bfloat16"), ("pb", 200, "bfloat16"),
+    ("rst", 232, "float32"), ("ub", 32, "bfloat16"), ("ti8", 8, "float32"), ("lrep", 8, "uint16"), ("lrs", 2, "uint16"),
+    ("rel", 16, "bfloat16"), ("cnt", 16, "int32"), ("cntf", 8, "float32"), ("ofc", 16, "float32"),
 ]:
     _sb(_n, _w, _d)
 for _h in range(2):
     for _n, _w, _d in [
-        ("dw", DWW, "bfloat16"), ("ab", 2048, "bfloat16"), ("ge", 256, "bfloat16"), ("kg", 384, "bfloat16"),
-        ("d7", 128, "bfloat16"), ("e1", 64, "float32"), ("tr", 128, "float32"), ("si", 256, "int32"),
-        ("tt", 256, "int32"), ("tf", 128, "float32"), ("c16", 128, "uint16"), ("l16", 96, "uint16"), ("src", 64, "uint16"),
-        ("nm", 96, F16), ("hh", 64 * 12, F16), ("sf", 192, "float32"),
+        ("xw", 2176, "bfloat16"), ("sti", 1024, "bfloat16"), ("sob", 1024, "bfloat16"), ("nmi", 64, "int32"),
+        ("mob", 64, "float32"), ("rn", 512, F16), ("wk", 8, "int32"), ("wf", 8, "float32"), ("zw", 144, "bfloat16"),
+        ("m16", 128, "float32"), ("kapr", 128, "float32"), ("kq", 48, "int32"), ("kqf", 32, "float32"), ("kt", 32, "bfloat16"),
+        ("dw", DWW, "bfloat16"), ("a1", span(Z1), "bfloat16"), ("a2", span(Z2), "bfloat16"), ("gb", span(9), "bfloat16"),
+        ("ge", 256, "bfloat16"), ("kg", 384, "bfloat16"), ("d7", 128, "bfloat16"), ("sc", 264, "float32"),
+        ("si", 368, "int32"), ("tt", 256, "int32"), ("tf", 128, "float32"), ("c16", 128, "uint16"), ("l16", 96, "uint16"),
+        ("src", 64, "uint16"), ("nm", 96, F16), ("hh", 64 * 12, F16), ("sf", 176, "float32"), ("rs", 96, "float32"),
     ]:
         _sb(_n + str(_h), _w, _d)
 for _b in range(8):
     SCRATCH["ps%d" % _b] = ("psum", [128, 512], "float32")
-SCRATCH["dfl_d"] = ("dram", [128, 128], "uint16")
 
-DMAS = ["dwt", "dkp", "dar", "dst", "drc", "dnm", "dr1", "dr2", "dso0", "dso1", "dzo", "dmo", "dm2"]
+DMAS = [n + str(h) for h in range(2) for n in ("dwk", "dar", "dst", "drc", "dnm", "dso", "dzo", "dmo", "dx")]
 SEMAPHORES = ["cv", "cs", "cp", "cg", "sent"] + DMAS + ["ar%d" % i for i in range(2 * RO)]
 
-CV, CPE, LAT, GA, SC, COMM = 1.0, 0.5, 90.0, 1.56, 3.8, 3500.0
+CV, CPE, LAT, GA, SC, COMM, DXL = 1.0, 0.5, 150.0, 1.56, 3.8, 4500.0, 3500.0
+SEG = {"g": (0, 9), 1: (72, Z1), 2: (72 + 8 * Z1, Z2), "u": (200, 4)}
+
+
+def zc(t, h):
+    return 256 * t + 128 * h
 
 
 def build(T, RO=RO):
     ops = []
     cur = [0, "i", 0]
+    now = [0]
 
     def R(name, lo, hi, step=1):
+        n = len(range(lo, hi, step))
+        hi = lo + (n - 1) * step + 1
         ap = T[name][:, lo:hi] if step == 1 else T[name][:, lo:hi:step]
-        return (ap, (name, lo, hi), len(range(lo, hi, step)), SCRATCH[name][2])
+        return (ap, (name, lo, hi, step), n, SCRATCH[name][2])
 
     def C(name, c):
         return R(name, c, c + 1)
@@ -93,8 +100,8 @@ def build(T, RO=RO):
             if len(w) == 5:
                 rd.append(w[4])
         ga = sum(r[2] for r in reads if isinstance(r, tuple) and len(r) == 5)
-        d = dict(eng=eng, fn=fn, rd=rd, wr=wr, cost=cost, lat=0.0, sem=None, n=1, after=None, half=cur[0],
-                 cls="%s%d_%d" % (cur[1], cur[0], cur[2]), ga=ga)
+        d = dict(eng=eng, fn=fn, rd=rd, wr=wr, cost=cost, lat=0.0, sem=None, after=None, half=cur[0], t=now[0],
+                 cls="%s%d_%d" % (cur[1], cur[0], cur[2]), ga=ga, sc=sum(w[2] for w in writes if len(w) == 5))
         cur[2] += 1
         d.update(kw)
         ops.append(d)
@@ -129,16 +136,18 @@ def build(T, RO=RO):
             fn = lambda e: [e.tensor_scalar(out[0], a[0], ap(s1), ap(s2), op0, op1)]
         return add("v", fn, [a, s1, s2], [out], vcost(out, [a]))
 
+    def scan(out, d0, d1, op0, op1):
+        return add("v", lambda e: [e.tensor_tensor_scan(out[0], d0[0], d1[0], 0.0, op0, op1)], [d0, d1], [out], vcost(out, [d0]))
+
     def mset(out, v):
         return add("v", lambda e: [e.memset(out[0], v)], [], [out], max(64, out[2] * (0.5 if two(out) else 1)) * CV)
 
-    def act(out, a, func, bias=None):
+    def act(out, a, func):
         cost = 65 + out[2] * GA * CV if len(a) == 5 else max(64, out[2]) * CV
-        if bias is None:
-            fn = lambda e: [e.activation(out[0], a[0], func)]
-        else:
-            fn = lambda e: [e.activation(out[0], a[0], func, bias=bias[0])]
-        return add("s", fn, [a, bias], [out], cost)
+        return add("s", lambda e: [e.activation(out[0], a[0], func)], [a], [out], cost)
+
+    def pick(e, out, a):
+        return tcopy(out, a) if e == "v" else act(out, a, AF.Copy)
 
     def scale(out, a, v):
         return add("s", lambda e: [e.activation(out[0], a[0], AF.Identity, scale=ap(v))], [a, v], [out], max(64, out[2]) * CV)
@@ -147,7 +156,7 @@ def build(T, RO=RO):
         k = len(items)
         fn = lambda e: [e.matmul(o[0], l[0], r[0], first and i == 0, last and i == k - 1) for i, (o, l, r) in enumerate(items)]
         cost = sum(max(64, r[2]) * (4 if r[3] == "float32" else 1) for _, _, r in items) * CPE
-        return add("p", fn, [x for _, l, r in items for x in (l, r)], [o for o, _, _ in items], cost, n=k)
+        return add("p", fn, [x for _, l, r in items for x in (l, r)], [o for o, _, _ in items], cost)
 
     def iota(out, pat, base, cm=0):
         if out[3] == "int32":
@@ -162,410 +171,424 @@ def build(T, RO=RO):
 
     def dma(eng, sem, pairs, reads, writes, lat):
         fn = lambda e: [e.dma_start(o, i) for o, i in pairs]
-        return add(eng, fn, reads, writes, 60.0 * len(pairs), lat=lat, sem=sem, n=len(pairs))
+        return add(eng, fn, reads, writes, 60.0 * len(pairs), lat=lat, sem=sem)
 
-    def sel(z, a):
-        return R(z, 15 - a, 143 - a)
+    def sel(z, a, top=15):
+        return R(z, top - a, top + 128 - a)
+
+    def slot(buf, z, m):
+        return R(buf, 16 * m, 16 * m + 128 * z, z)
+
+    def halves(buf, lo, ten, h, w, whole=False):
+        return [(T[buf][64 * u:64 * u + 64, lo:lo + w], ten[64 * h:64 * h + 64, :] if whole else ten[64 * h:64 * h + 64, w * u:w * u + w])
+                for u in range(2)]
 
     idb, nid, hid, qrt = R("idb", 0, 128), R("nid", 0, 128), R("hid", 0, 128), R("qrt", 0, 128)
     idh, nih, i128 = R("idh", 0, 128), R("nih", 0, 128), R("i128", 0, 128)
-    X = R("xw", 128, 2176)
 
-    dma("y", "dwt", [(T.wti[:, 0:1], T.wt[:])], [], [R("wti", 0, 4)], 2000)
-    dma("y", "dkp", [(T.kpi[:, 0:1], T.kap[:])], [], [R("kpi", 0, 4)], 2000)
-    dma("y", "dar", [(T.ari[:], T.arr[:])], [], [R("ari", 0, 256)], 2300)
-    dma("y", "dst", [(T.sti[:], T.st[:])], [], [R("sti", 0, 2048)], 4000)
-    dma("y", "drc", [(X[0], T.rec[:])], [], [X], 6000)
-    dma("s", "dnm", [(T.nmi[:, 16 * k:16 * k + 16], T.nm[k::8, :]) for k in range(8)], [], [R("nmi", 0, 128)], 5000)
+    for h in range(2):
+        s = str(h)
+        cur[:] = [h, "l", 0]
+        dma("y", "dar" + s, halves("zz", zc(0, h), T.arr, h, 128), [], [R("zz", zc(0, h), zc(0, h) + 128)], 2300)
+        dma("y", "dst" + s, halves("sti" + s, 0, T.st, h, 1024), [], [R("sti" + s, 0, 1024)], 3000 + 2500 * h)
+        dma("s", "dwk" + s, halves("wk" + s, 0, T.wt, h, 1, True) + halves("wk" + s, 4, T.kap, h, 1, True), [],
+            [R("wk" + s, 0, 8)], 2200)
+        dma("s", "dnm" + s, halves("nmi" + s, 0, T.nm, h, 64), [], [R("nmi" + s, 0, 64)], 2500)
+        dma("y", "drc" + s, halves("xw" + s, 128, T.rec, h, 2048, True), [], [R("xw" + s, 128, 2176)], 5000 + 2500 * h)
 
-    iota(R("pi", 0, 8), [[0, 8]], 0, 1)
-    ts(C("pi", 1), C("pi", 0), 15, OP.bitwise_and)
-    ts(C("pi", 2), C("pi", 0), 7, OP.bitwise_and)
-    ts(C("pi", 3), C("pi", 0), 3, OP.arith_shift_right, 1, OP.bitwise_and)
-    ts(C("pi", 4), C("pi", 0), 4, OP.arith_shift_right)
-    ts(C("pi", 5), C("pi", 0), 1, OP.arith_shift_right, 7, OP.bitwise_and)
-    ts(C("pi", 6), C("pi", 0), 1, OP.bitwise_and)
-    tcopy(R("pf", 0, 8), R("pi", 0, 8))
+    cur[:] = [0, "i", 0]
+    iota(R("pi", 0, 16), [[0, 16]], 0, 1)
+    for c, sh, mk in ((1, 0, 15), (2, 0, 7), (3, 3, 1), (4, 4, 7), (5, 1, 7), (6, 0, 1), (7, 6, 1), (8, 0, 3), (9, 2, 3)):
+        ts(C("pi", c), C("pi", 0), sh, OP.arith_shift_right, mk, OP.bitwise_and)
+    tcopy(R("pf", 0, 16), R("pi", 0, 16))
     ts(C("pc", 0), C("pf", 4), 16.0, OP.mult, 15.0, OP.add)
-    ts(C("pc", 1), C("pf", 2), 32.0, OP.mult, C("pf", 3), OP.add)
-    ts(C("pc", 2), C("pc", 1), 8.0, OP.mult)
-    ts(C("pc", 3), C("pf", 3), 64.0, OP.mult, C("pf", 2), OP.add)
-    ts(C("pc", 7), C("pf", 6), 8.0, OP.mult)
-    ts(C("pc", 4), C("pf", 5), 16.0, OP.mult, C("pc", 7), OP.add)
     iota(R("xi", 0, 144), [[1, 144]], 0)
-    ts(R("pc", 5, 7), R("xi", 0, 2), C("pf", 1), OP.is_equal)
     ts(R("z1", 0, 144), R("xi", 0, 144), C("pc", 0), OP.is_equal)
-    scale(R("z4", 0, 144), R("z1", 0, 144), 4096.0)
-    if NG:
-        ts(R("zn", 0, 144), R("z1", 0, 144), -4096.0, OP.mult)
-    tcopy(C("wtf", 0), C("wti", 0))
-    tcopy(C("kpf", 0), C("kpi", 0))
-    scale(R("zw", 0, 144), R("z1", 0, 144), C("wtf", 0))
     ts(idb, R("xi", 0, 128), C("pf", 0), OP.is_equal)
+    scale(R("z4", 0, 144), R("z1", 0, 144), 4096.0)
     scale(nid, idb, -1.0)
     scale(hid, idb, 0.5)
     for o, v in ((idh, 1.0), (nih, -1.0), (i128, 128.0)):
         ts(o, idb, v, OP.mult)
     mset(qrt, -0.25)
     iota(R("one", 0, 128), [[0, 128]], 1)
-    iota(R("zer", 0, 128), [[0, 128]], 0)
-    iota(R("i4", 0, 16), [[2, 16]], 0)
-    ts(R("larr", 0, 16), R("i4", 0, 16), C("pc", 1), OP.add)
-    ts(R("ti8", 0, 16), R("i4", 0, 16), 8.0, OP.mult, C("pc", 2), OP.add)
-    iota(R("i3", 0, 64), [[1, 8], [16, 8]], 0)
-    for h in range(2):
-        ts(R("lst", 64 * h, 64 * h + 64), R("i3", 0, 64), C("pc", 2), OP.add, 128.0 * h, OP.add)
+    ts(C("pc", 8), C("pf", 1), 8.0, OP.mult)
+    ts(C("pc", 1), C("pf", 7), 1024.0, OP.mult, C("pc", 8), OP.add)
+    ts(R("ti8", 0, 8), R("xi", 0, 8), 128.0, OP.mult, C("pc", 1), OP.add)
+    ts(C("pc", 3), C("pc", 0), -1.0, OP.add, C("pf", 3), OP.add)
+    ts(C("pc", 10), C("pf", 6), 8.0, OP.mult, -8.0, OP.add)
+    tt(C("pc", 4), C("pc", 10), C("pc", 0), OP.add)
+    ts(R("bz", 0, 144), R("xi", 0, 144), C("pc", 3), OP.is_equal)
+    ts(R("by", 0, 144), R("xi", 0, 144), C("pc", 4), OP.is_equal)
+    ts(R("mk8", 0, 8), R("xi", 0, 8), C("pf", 2), OP.is_equal)
+    ts(R("mk8", 8, 16), R("xi", 0, 8), C("pf", 5), OP.is_equal)
+    ts(R("pc", 5, 7), R("xi", 0, 2), C("pf", 1), OP.is_equal)
+    ts(C("pc", 11), C("pf", 8), -8.0, OP.mult, 24.0, OP.add)
+    tt(C("pc", 7), C("pc", 11), C("pf", 9), OP.add)
+    ts(R("lrs", 0, 2), R("xi", 0, 2), 4.0, OP.mult, C("pc", 7), OP.add)
+    ts(R("lrep", 0, 8), R("xi", 0, 8), 0.0, OP.mult, C("pf", 2), OP.add)
     iota(R("i7", 0, 64), [[128, 8], [0, 8]], 0)
-    iota(R("i8", 0, 64), [[0, 8], [16, 8]], 0)
-    tcopy(R("pk", 0, 64), R("i7", 0, 64))
-    ts(R("pb", 0, 64), R("i8", 0, 64), C("pf", 1), OP.add)
-    tt(R("posk", 0, 64), R("pk", 0, 64), R("pb", 0, 64), OP.add)
+    iota(R("i8", 0, 64), [[128, 8], [16, 8]], 0)
+    ts(R("posk", 0, 64), R("i8", 0, 64), C("pf", 1), OP.add)
     tcopy(R("poskh", 0, 64), R("posk", 0, 64))
     ts(R("ck", 0, 64), R("i7", 0, 64), -1.0, OP.mult, 1024.0, OP.add)
-    iota(R("pa", 0, 8 * NB), [[128, NB], [0, 8]], 128 * code(0))
-    iota(R("pa", 8 * NB, 128), [[128, 16 - NB], [0, 8]], 128 * code(NB))
-    ts(R("lrep", 0, 8), R("xi", 0, 8), 0.0, OP.mult, C("pf", 2), OP.add)
-    ts(C("pc", 7), C("pf", 3), 16.0, OP.mult, C("pf", 2), OP.add)
-    iota(R("i6", 0, 8), [[8, 2], [32, 4]], 0)
-    ts(R("lperm", 0, 8), R("i6", 0, 8), C("pc", 7), OP.add)
-    ts(R("linv", 0, 8), R("xi", 0, 8), 8.0, OP.mult, C("pc", 3), OP.add)
-    iota(R("i5", 0, 16), [[1, 8], [128, 2]], 0)
-    ts(R("lzo", 0, 16), R("i5", 0, 16), C("pc", 4), OP.add)
-    for h in range(2):
-        ts(R("dfl", 8 * h, 8 * h + 8), R("pb", 0, 8), 16384.0 + 2048 * h, OP.add)
-        iota(R("jc", 24 * h, 24 * h + 24), [[4096, 3], [0, 8]], 4096 + 128 * (1 - h))
-    iota(R("i1", 0, 128), [[1, 8], [0, 16]], 0)
+    for k, base in (("g", 0), (1, 15 - NB), (2, 15 - NB + Z1)):
+        c0, z = SEG[k]
+        iota(R("i9", c0, c0 + 8 * z), [[0, 8], [128, z]], 128 * base)
+        iota(R("ia", c0, c0 + 8 * z), [[16, 8], [0, z]], 0)
+    ts(R("i1", 0, 128), R("i9", 72, 200), 128.0 * 15, OP.is_ge, 256.0, OP.mult)
+    tt(R("pa", 72, 200), R("i9", 72, 200), R("i1", 0, 128), OP.add)
+    tcopy(R("pa", 0, 72), R("i9", 0, 72))
+    ts(R("pb", 0, 200), R("ia", 0, 200), C("pf", 1), OP.add)
+    iota(R("rst", 0, 232), [[0, 232]], 0)
+    for c0, z in SEG.values():
+        mset(R("rst", c0, c0 + 8 * z, z), BIG)
+    iota(R("i6", 0, 144), [[1, 9], [0, 4], [100, 4]], -300)
+    ts(R("zq", 0, 144), R("i6", 0, 144), C("pf", 4), OP.is_equal)
+    iota(R("ib", 0, 32), [[0, 8], [1, 4]], 0)
+    ts(R("ub", 0, 32), R("ib", 0, 32), C("pf", 9), OP.not_equal, 4194304.0, OP.mult)
+    iota(R("i3", 0, 128), [[1, 8], [0, 16]], 0)
     iota(R("i2", 0, 128), [[1, 16], [0, 8]], 0)
-    ts(R("blk", 0, 128), R("i1", 0, 128), C("pf", 4), OP.is_equal)
-    ts(R("m16", 0, 128), R("i2", 0, 128), C("pf", 1), OP.is_equal, C("kpf", 0), OP.mult)
-    mm([(R("ps5", 0, 128), R("blk", 0, 128), R("m16", 0, 128))])
-    tcopy(R("kapr", 0, 128), R("ps5", 0, 128))
-    ts(R("k0j", 0, 3), R("xi", 1, 4), C("kapr", 0), OP.mult, -31.0 / 64, OP.add)
-    tcopy(R("ofc", 0, 3), R("k0j", 0, 3))
-    tcopy(R("kq", 0, 16), R("kapr", 0, 128, 8))
-    ts(R("kq", 16, 32), R("kq", 0, 16), 31, OP.bitwise_and)
-    tt(R("kq", 32, 48), R("kq", 0, 16), R("kq", 16, 32), OP.subtract)
-    ts(R("kqf", 0, 16), R("kq", 16, 32), C("pc", 5), OP.mult)
-    ts(R("kqf", 16, 32), R("kq", 32, 48), C("pc", 6), OP.mult)
-    tt(R("kqf", 32, 48), R("kqf", 0, 16), R("kqf", 16, 32), OP.add)
-    def zero(name, lo, hi):
-        for c in range(lo, hi, 256):
-            iota(R(name, c, min(hi, c + 256)), [[0, min(hi, c + 256) - c]], 0)
-
-    zero("kt", 0, 256)
-    zero("kt", 128 * (NB + 1), 128 * 17)
-    for m in range(1, 16):
-        act(R("kt", 128 * code(m), 128 * code(m) + 128), R("zer", 0, 128), AF.Identity, C("kqf", 32 + m))
+    ts(R("blk", 0, 128), R("i3", 0, 128), C("pf", 4), OP.is_equal)
+    iota(R("i4", 0, 32), [[0, 4], [16, 8]], -128)
     for h in range(2):
-        zero("dw%d" % h, 0, 128)
-        zero("dw%d" % h, 128 * (NB + 1), 128 * (17 - max(AL)))
-        mset(R("nm%d" % h, 64, 96), BIG)
-        mset(R("hh%d" % h, 120, 128), 1.0)
-        tcopy(R("nm%d" % h, 0, 64), G(R("nmi", 0, 128), R("lperm", 4 * h, 4 * h + 4)))
-        tcopy(R("zz", 128 * h, 128 * h + 128), G(R("ari", 0, 256), R("larr", 8 * h, 8 * h + 8)))
+        s = str(h)
+        cur[:] = [h, "j", 0]
+        B = "ps%d" % (4 * h + 1)
+        wf, kapr, kq, kqf, kt = "wf" + s, "kapr" + s, "kq" + s, "kqf" + s, "kt" + s
+        tcopy(R(wf, 0, 8, 4), R("wk" + s, 0, 8, 4))
+        scale(R("zw" + s, 0, 144), R("zq", 0, 144), C(wf, 0))
+        ts(R("m16" + s, 0, 128), R("i2", 0, 128), C("pf", 1), OP.is_equal, C(wf, 4), OP.mult)
+        mm([(R(B, 0, 128), R("blk", 0, 128), R("m16" + s, 0, 128))])
+        act(R(kapr, 0, 128), R(B, 0, 128), AF.Copy)
+        ts(R("k0j", 3 * h, 3 * h + 3), R("xi", 1, 4), C(kapr, 0), OP.mult, -31.0 / 64, OP.add)
+        tcopy(R("ofc", 3 * h, 3 * h + 3), R("k0j", 3 * h, 3 * h + 3))
+        tcopy(R(kq, 0, 16), R(kapr, 0, 128, 8))
+        ts(R(kq, 16, 32), R(kq, 0, 16), 31, OP.bitwise_and)
+        tt(R(kq, 32, 48), R(kq, 0, 16), R(kq, 16, 32), OP.subtract)
+        ts(R(kqf, 0, 16), R(kq, 16, 32), C("pc", 5), OP.mult)
+        ts(R(kqf, 16, 32), R(kq, 32, 48), C("pc", 6), OP.mult)
+        iota(R(kt, 0, 32), [[0, 32]], 0)
+        tt(R(kt, code(0), code(0) + NB), R(kqf, 0, NB), R(kqf, 16, 16 + NB), OP.add)
+        tt(R(kt, 17, 33 - NB), R(kqf, NB, 16), R(kqf, 16 + NB, 32), OP.add)
+        for c in range(0, 128 * code(0), 384):
+            e = min(c + 384, 128 * code(0))
+            iota(R("dw" + s, c, e), [[0, e - c]], 0)
+        if max(AL) == 1:
+            iota(R("dw" + s, 1920, 2048), [[0, 128]], 0)
+        mset(slot("gb" + s, 9, 8), 0.0)
+        ts(R("nm" + s, 64, 96), R("i4", 0, 32), C("pf", 1), OP.add)
+        ts(R("sf" + s, 32, 40), R("i4", 0, 8), C("pf", 1), OP.add)
+        iota(R("sf" + s, 0, 8), [[0, 8]], 0)
+        iota(R("rs" + s, 0, 32), [[0, 32]], 0)
+        mset(R("hh" + s, 120, 128), 1.0)
+        for k in range(8):
+            ts(R("rn" + s, 64 * k, 64 * k + 64), R("nmi" + s, 0, 64), C("mk8", k), OP.mult)
+        mm([(R(B, 0, 64), sel("bz", 2 * q, 14), R("rn" + s, q, 512, 8)) for q in range(8)])
+        tcopy(R("nm" + s, 0, 64), R(B, 0, 64))
 
-    lrep8, lrep4 = R("lrep", 0, 8), R("lrep", 0, 4)
+    lrep4 = R("lrep", 0, 4)
 
     def names(h, tag):
         s = str(h)
         cur[:] = [h, tag, 0]
-        return dict(tf="tf" + s, dw="dw" + s, ab="ab" + s, ge="ge" + s, kg="kg" + s, d7="d7" + s, e1="e1" + s, tr="tr" + s,
-                    si="si" + s, tt="tt" + s, c16="c16" + s, l16="l16" + s, src="src" + s, nm="nm" + s, hh="hh" + s,
-                    sf="sf" + s, A="ps%d" % (4 * h), B="ps%d" % (4 * h + 1), Cb="ps%d" % (4 * h + 2), D="ps%d" % (4 * h + 3))
+        d = {k: k + s for k in ("tf", "dw", "a1", "a2", "gb", "ge", "kg", "d7", "sc", "si", "tt", "c16", "l16", "src", "nm", "hh",
+                                "sf", "rs", "xw", "zw", "kapr", "kt", "sti", "sob", "mob", "rn")}
+        d.update(A="ps%d" % (4 * h), B="ps%d" % (4 * h + 1), Cb="ps%d" % (4 * h + 2), D="ps%d" % (4 * h + 3))
+        d["bank"] = [d["A"], d["B"], d["Cb"], d["D"]]
+        return d
 
-    def lsum(out, z, src, lo, hi, pre=()):
-        return mm(list(pre) + [(out, sel(z, a), R(src, lo + a, hi, 16)) for a in range(16)])
+    def keys(out, buf, seg):
+        c0, z = SEG[seg]
+        mm([(out, idb, R("pa", c0, c0 + 8 * z)), (out, idb, R("pb", c0, c0 + 8 * z))], True, False)
+        mm([(out, sel("z4", a), R(buf, z * a, z * a + 128 * z, 16)) for a in range(16)], False, True)
 
-    def settle(n, w, slot, parts, main=True):
+    def least(n, ps, seg):
+        c0, z = SEG[seg]
+        scan(R(n["sc"], c0, c0 + 8 * z), R("rst", c0, c0 + 8 * z), ps, OP.add, OP.min)
+
+    def low(n, out, ps, seg, last, c, tmp, mask):
+        c0, z = SEG[seg]
+        if SI:
+            scan(R(n["si"], c, c + 8 * z), R("rst", c0, c0 + 8 * z), ps, OP.add, OP.min)
+            ts(out, R(n["si"], c + last, c + 8 * z, z), mask, OP.bitwise_and)
+        else:
+            c = c0 + (32 if c == 336 else 0)
+            scan(R(n["sc"], c, c + 8 * z), R("rst", c0, c0 + 8 * z), ps, OP.add, OP.min)
+            tcopy(tmp, R(n["sc"], c + last, c + 8 * z, z))
+            ts(out, tmp, mask, OP.bitwise_and)
+
+    def quads(ps, z, src, lo):
+        mm([(ps, idb, R("ub", 0, 32))], True, False)
+        mm([(ps, sel(z, q, 3), R(src, lo + q, lo + 128, 4)) for q in range(4)], False, True)
+
+    def settle(n, w, place, parts, main=True):
         ps = R(n["D"], 0, 128)
         mm([(ps, idb, qrt), (ps, hid, parts[0])], True, False)
         mm([(ps, hid, p) for p in parts[1:]], False, True)
+        keep = R(w[0], w[1] + place, w[1] + place + 128)
         if main:
             s = R(n["dw"], 2048, 2176)
             ts(s, ps, MAGIC, OP.add, -MAGIC, OP.add)
             if max(AL) > 1:
                 gcopy(R(n["dw"], 1920, 2048), s)
-            gcopy(R(w[0], w[1] + slot, w[1] + slot + 128), s)
+            gcopy(keep, s)
         else:
-            ts(R(w[0], w[1] + slot, w[1] + slot + 128), ps, MAGIC, OP.add, -MAGIC, OP.add)
+            ts(keep, ps, MAGIC, OP.add, -MAGIC, OP.add)
 
     def rows(t, h):
         n = names(h, "r")
         w = "w%d" % (t % 2)
         if t == 0:
-            win, lst, l0 = R("sti", 0, 2048), "lst", 64 * h
-        else:
-            win, lst, l0 = R("w%d" % ((t - 1) % 2), 1536 * h, 1536 * h + 1536), n["src"], 0
-        lv = 2 if t == 0 else LV
-        cur[2] = 5 if t == 0 else 0
-        for a, b, eng in ((0, lv, "v"), (lv, 4, "s"), (4, 8, "s")):
-            if a == b:
-                continue
-            o = R(w, 1536 * h + 128 * a, 1536 * h + 128 * b)
-            src = G(win, R(lst, l0 + 8 * a, l0 + 8 * b))
-            if eng == "v":
-                tcopy(o, src)
-            else:
-                act(o, src, AF.Copy)
+            cur[2] = 5
+            for k in range(8):
+                pick("sv"[k % 2 * (1 - h)], R(w, 1536 * h + 128 * k, 1536 * h + 128 * k + 128), R(n["sti"], k, 1024, 8))
+            return
+        win = R("w%d" % ((t - 1) % 2), 1536 * h, 1536 * h + 1536)
+        for a, b, e in RG:
+            pick(e, R(w, 1536 * h + 128 * a, 1536 * h + 128 * b), G(win, R(n["src"], 8 * a, 8 * b)))
 
     def store(t, h):
         n = names(h, "s")
         si = n["si"]
-        z0 = 256 * t + 128 * h
-        ps = R(n["A"], 0, 8)
-        lsum(ps, "z1", "zz", z0, z0 + 128)
-        tcopy(R(si, 0, 8), ps)
-        ts(R(si, 8, 16), R(si, 0, 8), 7, OP.bitwise_and)
-        tt(R(si, 16, 24), R(si, 8, 16), R("ti8", 8 * h, 8 * h + 8), OP.add)
-        tcopy(R(n["l16"], 0, 8), R(si, 16, 24))
+        z0 = zc(t, h)
+        ps = R(n["A"], 0, 32)
+        quads(ps, "zq", "zz", z0)
+        low(n, R(si, 16, 24), ps, "u", 3, 336, R(si, 0, 8), 7)
+        tt(R(si, 32, 40), R(si, 16, 24), R("ti8", 0, 8), OP.add)
+        tcopy(R(n["l16"], 0, 8), R(si, 32, 40))
+        X = R(n["xw"], 128, 2176)
         tcopy(G(X, R(n["l16"], 0, 8)), R("zz", z0, z0 + 128))
+        x = T[n["xw"]]
+        dma("y", "dx%d" % h, [(x[0:64, 1152:2176], x[64:128, 1152:2176]), (x[64:128, 128:1152], x[0:64, 128:1152])], [X], [X], DXL)
 
     def gap(t, h):
         n = names(h, "g")
-        si, tr, hh, nm = n["si"], n["tr"], n["hh"], n["nm"]
+        si, hh, nm, sf = n["si"], n["hh"], n["nm"], n["sf"]
         w = ("w%d" % (t % 2), 1536 * h)
-        z = R("zz", 256 * t + 128 * h, 256 * t + 128 * h + 128)
+        z = R("zz", zc(t, h), zc(t, h) + 128)
         for q, b in enumerate((n["Cb"], n["D"])):
-            mm([(R(b, 0, 512), idb, R(w[0], w[1] + 512 * q, w[1] + 512 * q + 512))]
-               + [(R(b, 128 * k, 128 * k + 128), nid, z) for k in range(4)])
-            act(R(n["ab"], 512 * q, 512 * q + 512), R(b, 0, 512), AF.Abs)
-        ps = R(n["B"], 0, 64)
-        lsum(ps, "z4", n["ab"], 0, 1024, [(ps, idb, R("pk", 0, 64)), (ps, idb, R("pb", 0, 64))])
-        act(R(n["e1"], 0, 32), R(n["B"], 32, 64), AF.Copy)
-        tt(R(tr, 0, 32), R(n["B"], 0, 32), R(n["e1"], 0, 32), OP.min)
-        tt(R(tr, 96, 112), R(tr, 0, 16), R(tr, 16, 32), OP.min)
-        tt(R(si, 24, 32), R(tr, 96, 104), R(tr, 104, 112), OP.min)
-        off = R(si, 32, 40)
-        ts(off, R(si, 24, 32), 4095, OP.bitwise_and)
-        tcopy(R(n["l16"], 8, 16), off)
+            mm([(R(b, 0, 512), idb, R(w[0], w[1] + 512 * q, w[1] + 512 * q + 512))], True, False)
+            mm([(R(b, 128 * k, 128 * k + 128), nid, z) for k in range(4)], False, True)
+            for k in range(4):
+                act(slot(n["gb"], 9, 4 * q + k), R(b, 128 * k, 128 * k + 128), AF.Abs)
+        ps = R(n["B"], 0, 72)
+        keys(ps, n["gb"], "g")
+        off = R(si, 56, 64)
+        low(n, off, ps, "g", 7, 264, R(si, 48, 56), 4095)
+        tcopy(R(n["l16"], 16, 24), off)
         ge = R(n["ge"], 0, 128)
-        act(ge, G(R(w[0], w[1], w[1] + 1024), R(n["l16"], 8, 16)), AF.Copy)
+        act(ge, G(R(w[0], w[1], w[1] + 1024), R(n["l16"], 16, 24)), AF.Copy)
         settle(n, w, 1024, [z, ge])
         H = lambda i, a=0, b=64: R(hh, 64 * i + a, 64 * i + b)
         tt(H(2), G(off, lrep4), R("posk", 0, 64), OP.is_gt)
         tt(H(0), R(hh, 120, 184), H(2), OP.subtract)
         for j in (1, 2, 3):
             tt(H(3 + j), H(0), R(nm, 8 * j, 8 * j + 64), OP.mult)
-            pj = R(n["B"], 64 + 8 * j, 72 + 8 * j)
-            mm([(pj, idh, H(3 + j, 8 * k, 8 * k + 8)) for k in range(8)])
-            if j == 1:
-                ts(R(n["l16"], 16, 24), pj, 2047.0, OP.min)
-        ts(R(n["l16"], 24, 40), R(n["B"], 80, 96), 2047.0, OP.min)
-        tt(R(n["sf"], 0, 24), R(n["B"], 72, 96), R("jc", 24 * h, 24 * h + 24), OP.add)
-        tcopy(R(n["sf"], 24, 48), R(n["l16"], 16, 40))
+            mm([(R(n["B"], 120 + 8 * j, 128 + 8 * j), idh, H(3 + j, 8 * k, 8 * k + 8)) for k in range(8)])
+        tcopy(R(n["l16"], 24, 48), R(n["B"], 128, 152))
+        act(R(sf, 8, 32), R(n["B"], 128, 152), AF.Copy)
+        tt(R(sf, 40, 72), R(sf, 8, 40), R(sf, 0, 32), OP.subtract)
+        tcopy(R(n["rs"], 32, 64), G(R(sf, 40, 72), R("lrs", 0, 2)))
         tt(H(3), H(0), R("ck", 0, 64), OP.mult)
-        b = n["Cb"]
-        mm([(R(b, 0, 64), idh, R("poskh", 0, 64)), (R(b, 0, 64), i128, H(2))]
-           + [(R(b, 8 * j, 64), idh, H(3, 0, 64 - 8 * j)) for j in range(4)])
-        tcopy(R(n["src"], 0, 64), R(b, 0, 64))
+        b = n["B"]
+        mm([(R(b, 384, 448), idh, R("poskh", 0, 64)), (R(b, 384, 448), i128, H(2))]
+           + [(R(b, 384 + 8 * j, 448), idh, H(3, 0, 64 - 8 * j)) for j in range(4)])
+        tcopy(R(n["src"], 0, 64), R(b, 384, 448))
         tt(H(7, 0, 56), R(nm, 8, 64), H(2, 0, 56), OP.mult)
-        tt(H(8), G(R(si, 16, 24), lrep4), H(0), OP.mult)
-        if t == RO - 1:
-            ts(R("srf", 64 * h, 64 * h + 64), R(b, 0, 64), 1536.0 * h, OP.add)
+        tt(H(8), G(R(si, 32, 40), lrep4), H(0), OP.mult)
 
     def corr(t, h, j):
         n = names(h, "abc"[j - 1])
-        si, tr, dw, ab, tw = n["si"], n["tr"], n["dw"], n["ab"], n["tt"]
+        si, dw, tw, sf, tf, rs = n["si"], n["dw"], n["tt"], n["sf"], n["tf"], n["rs"]
         w = ("w%d" % (t % 2), 1536 * h)
+        X = R(n["xw"], 128, 2176)
         s = R(dw, 2048, 2176)
         D = lambda m0, m1: R(dw, 128 * code(m0), 128 * code(m1 - 1) + 128)
         L = lambda m0, m1: R(n["c16"], 8 * m0, 8 * m1)
-        act(D(0, 1), G(X, R(n["l16"], 8 + 8 * j, 16 + 8 * j)), AF.Copy)
+        AB = lambda m: slot(n["a1"], Z1, m) if m < Z1 else slot(n["a2"], Z2, m - Z1)
+        ps = R(n["A"], 0, 32)
+        quads(ps, n["zw"], dw, 2048)
+        u, f = R(si, 64 + 8 * j, 72 + 8 * j), R(si, 88 + 8 * j, 96 + 8 * j)
+        low(n, u, ps, "u", 3, 232, R(si, 64, 72), 2047)
+        tt(R(sf, 72, 80), u, u, OP.mult)
+        ts(f, R(sf, 72, 80), 1.0 / 32, OP.mult, C("ofc", 8 * (t % 2) + 3 * h + j - 1), OP.add)
+        for m0, m1 in SP:
+            rep = R("lrep", 0, (m1 - m0) // 2)
+            tt(R(tf, 8 * m0, 8 * m1), G(u, rep), R(n["kapr"], 8 * m0, 8 * m1), OP.mult)
+            tt(R(tw, 8 * m0, 8 * m1), G(f, rep), R(tf, 8 * m0, 8 * m1), OP.add)
+            m0 = max(m0, 1)
+            ts(R(tw, 128 + 8 * m0, 128 + 8 * m1), R(tw, 8 * m0, 8 * m1), 2047, OP.bitwise_and)
+            tcopy(L(m0, m1), R(tw, 128 + 8 * m0, 128 + 8 * m1))
+        act(D(0, 1), G(X, R(n["l16"], 16 + 8 * j, 24 + 8 * j)), AF.Copy)
         if j == 3:
+            back = cur[2]
+            cur[2] = 100
             settle(n, w, 1408, [s, D(0, 1)], False)
-            z = R("zz", 256 * t + 128 * h, 256 * t + 128 * h + 128)
+            z = R("zz", zc(t, h), zc(t, h) + 128)
             tt(R(n["d7"], 0, 128), G(R(w[0], w[1], w[1] + 1536), R(n["src"], 56, 64)), z, OP.subtract)
-            act(R("xw", 2176 * h, 2176 * h + 128), R(n["d7"], 0, 128), AF.Abs)
-        ps = R(n["A"], 0, 8)
-        lsum(ps, "zw", dw, 2048, 2176)
-        u, f = R(si, 48 + 8 * j, 56 + 8 * j), R(si, 72 + 8 * j, 80 + 8 * j)
-        tcopy(R(si, 40, 48), ps)
-        ts(u, R(si, 40, 48), 2047, OP.bitwise_and)
-        sf, tf = n["sf"], n["tf"]
-        tt(R(sf, 96, 104), u, u, OP.mult)
-        tt(R(tf, 0, 128), G(u, lrep8), R("kapr", 0, 128), OP.mult)
-        ts(f, R(sf, 96, 104), 1.0 / 32, OP.mult, C("ofc", 4 * (t % 2) + j - 1), OP.add)
-        tt(R(tw, 0, 128), G(f, lrep8), R(tf, 0, 128), OP.add)
-        ts(R(tw, 136, 256), R(tw, 8, 128), 2047, OP.bitwise_and)
-        tcopy(L(1, 16), R(tw, 136, 256))
-        for b, m0, m1 in ((n["Cb"], 0, 4), (n["D"], 4, NB)):
-            act(D(max(m0, 1), m1), G(X, L(max(m0, 1), m1)), AF.Copy)
+            act(R(n["xw"], 0, 128), R(n["d7"], 0, 128), AF.Abs)
+            cur[2] = back
+        for b, m0, m1 in SG:
+            b = n["bank"][b]
+            if m1 > 1:
+                act(D(m0, m1), G(X, L(m0, m1)), AF.Copy)
             k = m1 - m0
             mm([(R(b, 0, 128 * k), idb, D(m0, m1))] + [(R(b, 128 * i, 128 * i + 128), nid, s) for i in range(k)])
-            act(R(ab, 128 * m0, 128 * m1), R(b, 0, 128 * k), AF.Abs)
+            for i in range(k):
+                act(AB(m0 + i), R(b, 128 * i, 128 * i + 128), AF.Abs)
         m = NB
         for k in AL:
             tt(D(m, m + k), G(X, L(m, m + k)), R(dw, 2176 - 128 * k, 2176), OP.subtract)
+            for i in range(k):
+                act(AB(m + i), D(m + i, m + i + 1), AF.Abs)
             m += k
-        m = NB
-        for k in AB:
-            if m < 16 - NG:
-                act(R(ab, 128 * m, 128 * (m + k)), D(m, m + k), AF.Abs)
-            else:
-                ts(R(ab, 128 * m, 128 * (m + k)), D(m, m + k), 0.0, OP.max, 2.0, OP.mult)
-            m += k
-        p1, p2 = R(n["A"], 256, 320), R(n["B"], 0, 64)
-        lsum(p1, "z4", ab, 0, 1024, [(p1, idb, R("pa", 0, 64)), (p1, idb, R("pb", 0, 64))])
-        act(R(n["e1"], 0, 64), p1, AF.Copy)
-        pre = [(p2, idb, R("pa", 64, 128)), (p2, idb, R("pb", 0, 64))]
-        if NG:
-            pre += [(R(n["B"], 64 - 8 * NG, 64), sel("zn", a), R(dw, 128 * code(16 - NG) + a, DWW, 16)) for a in range(16)]
-        mm(pre, True, False)
-        mm([(p2, sel("z4", a), R(ab, 1024 + a, 2048, 16)) for a in range(16)], False, True)
-        tt(R(tr, 0, 64), p2, R(n["e1"], 0, 64), OP.min)
-        tt(R(tr, 64, 96), R(tr, 0, 32), R(tr, 32, 64), OP.min)
-        tt(R(tr, 96, 112), R(tr, 64, 80), R(tr, 80, 96), OP.min)
-        key = R(si, 24, 32)
-        tt(key, R(tr, 96, 104), R(tr, 104, 112), OP.min)
-        o = 88 + 16 * j
-        off = R(si, o, o + 8)
-        ts(off, key, 4095, OP.bitwise_and)
-        ts(R(si, o + 8, o + 16), key, 2048 + 127, OP.bitwise_and)
-        lo = 24 + 16 * j
-        kj = R(sf, 40 + 8 * j, 48 + 8 * j)
-        ts(kj, off, 256.0, OP.is_lt, BIG, OP.mult)
-        tt(R(sf, 104, 112), kj, R(sf, 8 * j - 8, 8 * j), OP.add)
-        run = R(si, 168, 176) if j == 3 else R(sf, 112, 120)
-        tt(run, R(sf, 104, 112), R("dfl", 8 * h, 8 * h + 8) if j == 1 else R(sf, 112, 120), OP.min)
+        p1, p2 = R(n["A"], 256, 256 + 8 * Z1), R(n["B"], 0, 8 * Z2)
+        keys(p1, n["a1"], 1)
+        least(n, p1, 1)
+        keys(p2, n["a2"], 2)
+        least(n, p2, 2)
+        key = R(si, 112 + 8 * j, 120 + 8 * j)
+        tt(key, R(n["sc"], 71 + Z1, 72 + 8 * Z1, Z1), R(n["sc"], 71 + 8 * Z1 + Z2, 200, Z2), OP.min)
+        ts(R(si, 144, 152), key, 4095, OP.bitwise_and)
+        ts(R(si, 152, 160), key, 2048 + 127, OP.bitwise_and)
+        tt(R(rs, 4 - j, 32, 4), key, R(n["sc"], 72, 72 + 8 * Z1, Z1), OP.is_ge)
         if j == 3:
-            ts(R(si, 176, 184), run, 4095, OP.bitwise_and)
-            tcopy(R(n["l16"], 88, 96), R(si, 176, 184))
-            ob = R("ob", 256 * t + 128 * h, 256 * t + 128 * h + 128)
-            if OBV:
-                tcopy(ob, G(R("xw", 128 * h, 128 * h + 2176), R(n["l16"], 88, 96)))
-            else:
-                act(ob, G(R("xw", 128 * h, 128 * h + 2176), R(n["l16"], 88, 96)), AF.Copy)
+            back = cur[2]
+            cur[2] = 200
+            scan(R(rs, 64, 96), R(rs, 0, 32), R(rs, 32, 64), OP.mult, OP.add)
+            ts(R(n["l16"], 64, 72), R(rs, 67, 96, 4), 128.0, OP.add)
+            ob = R("ob", zc(t, h), zc(t, h) + 128)
+            act(ob, G(R(n["xw"], 0, 2176), R(n["l16"], 64, 72)), AF.Copy)
             snd = add("g", None, [ob], [], 300.0, sem="sent", send=(t, h), src=ob[0])
-            zn = R("zz", 256 * (t + 1) + 128 * h, 256 * (t + 1) + 128 * h + 128)
+            zn = R("zz", zc(t + 1, h), zc(t + 1, h) + 128)
             add("x", None, [], [zn], 0.0, lat=COMM, sem="ar%d" % (2 * t + h), after=snd, recv=(t, h))
-            cur[2] += 100
             if t < RO - 1:
-                ts(R("rel", 8 * h, 8 * h + 8), run, 16384.0, OP.is_lt)
-                cur[2] -= 1
-            cur[2] -= 100
-        tcopy(R(n["l16"], lo, lo + 16), R(si, o, o + 16))
-        if GS:
-            act(R(n["ge"], 0, 128), G(R(dw, 0, DWW), R(n["l16"], lo, lo + 8)), AF.Copy)
-            tcopy(R(n["ge"], 128, 256), G(R(dw, 0, DWW), R(n["l16"], lo + 8, lo + 16)))
-        else:
-            act(R(n["ge"], 0, 256), G(R(dw, 0, DWW), R(n["l16"], lo, lo + 16)), AF.Copy)
+                ts(R("rel", 8 * h, 8 * h + 8), R(rs, 67, 96, 4), 0.0, OP.is_ge)
+            cur[2] = back
+        tcopy(R(n["l16"], 48, 64), R(si, 144, 160))
+        act(R(n["ge"], 0, 256), G(R(dw, 0, DWW), R(n["l16"], 48, 64)), AF.Copy)
         settle(n, w, 1024 + 128 * j, [s, R(n["ge"], 0, 128), R(n["ge"], 128, 256)], j < 3)
-        act(R(n["kg"], 128 * j - 128, 128 * j), G(R("kt", 0, DWW), R(n["l16"], lo, lo + 8)), AF.Copy)
 
     def rename(t, h):
         n = names(h, "n")
         si, hh, nm, sf = n["si"], n["hh"], n["nm"], n["sf"]
         H = lambda i, a=0, b=64: R(hh, 64 * i + a, 64 * i + b)
-        ps = R(n["Cb"], 0, 24)
-        lsum(ps, "z1", n["kg"], 0, 384)
-        tt(R(sf, 120, 144), ps, R(si, 56, 80), OP.mult)
-        tt(R(si, 208, 232), R(sf, 120, 144), R(si, 80, 104), OP.add)
-        ts(R(si, 232, 256), R(si, 208, 232), 2047, OP.bitwise_and)
-        tt(R(sf, 144, 168), R(si, 232, 256), R(sf, 24, 48), OP.subtract)
-        ts(R(sf, 168, 192), R(sf, 48, 72), 1.0, OP.is_lt)
-        tt(R(sf, 72, 96), R(sf, 144, 168), R(sf, 168, 192), OP.mult)
+        ts(R(si, 160, 184), R(si, 120, 144), 7, OP.arith_shift_right, 31, OP.bitwise_and)
+        tcopy(R(n["l16"], 72, 96), R(si, 160, 184))
+        act(R(n["kg"], 0, 384), G(R(n["kt"], 0, 32), R(n["l16"], 72, 96)), AF.Copy)
+        b = n["B"]
+        ps = R(b, 200, 224)
+        mm([(ps, sel("z1", a), R(n["kg"], a, 384, 16)) for a in range(16)])
+        tt(R(sf, 104, 128), ps, R(si, 72, 96), OP.mult)
+        tt(R(si, 184, 208), R(sf, 104, 128), R(si, 96, 120), OP.add)
+        ts(R(si, 208, 232), R(si, 184, 208), 2047, OP.bitwise_and)
+        tt(R(sf, 128, 152), R(si, 208, 232), R(sf, 8, 32), OP.subtract)
+        ts(R(sf, 152, 176), R(si, 160, 184), code(0) + 0.5, OP.is_gt)
+        tt(R(sf, 80, 104), R(sf, 128, 152), R(sf, 152, 176), OP.mult)
         for j in (1, 2, 3):
-            tt(H(8 + j), G(R(sf, 64 + 8 * j, 72 + 8 * j), lrep4), H(0), OP.mult)
-        b = n["Cb"]
+            tt(H(8 + j), G(R(sf, 72 + 8 * j, 80 + 8 * j), lrep4), H(0), OP.mult)
         mm([(R(b, 64 + 8 * j, 128), idh, H(8 + j, 0, 64 - 8 * j)) for j in range(4)]
            + [(R(b, 72, 128), idh, R(nm, 8, 64)), (R(b, 64, 120), idh, H(7, 0, 56)), (R(b, 72, 128), nih, H(7, 0, 56))])
         if t < RO - 1:
             tcopy(R(nm, 0, 64), R(b, 64, 128))
-        else:
-            tcopy(R("nmf", 64 * h, 64 * h + 64), R(b, 64, 128))
 
     def count(t):
         cur[:] = [0, "k", 0]
-        ps = R("ps4", 384, 385)
+        ps = R("ps4", 500, 501)
         mm([(ps, R("one", 0, 128), C("rel", c)) for c in range(16)])
         tcopy(C("cnt", 0), ps)
         ts(C("cnt", 8), C("cnt", 0), 63, OP.bitwise_and)
         tcopy(C("cntf", 0), C("cnt", 8))
-        q = 4 * ((t + 1) % 2)
-        ts(R("ofc", q, q + 3), R("k0j", 0, 3), C("cntf", 0), OP.add)
+        q = 8 * ((t + 1) % 2)
+        ts(R("ofc", q, q + 6), R("k0j", 0, 6), C("cntf", 0), OP.add)
+
+    def outputs(h):
+        n = names(h, "o")
+        s = str(h)
+        win = R("w%d" % ((RO - 1) % 2), 1536 * h, 1536 * h + 1536)
+        for k in range(8):
+            pick("sv"[k % 2], R(n["sob"], k, 1024, 8), G(win, R(n["src"], 8 * k, 8 * k + 8)))
+        dma("y", "dso" + s, [(b, a) for a, b in halves(n["sob"], 0, T.so, h, 1024)], [R(n["sob"], 0, 1024)], [], 3000)
+        for q in range(8):
+            ts(R(n["rn"], q, 512, 8), R(n["B"], 64, 128), C("mk8", 8 + q), OP.mult)
+        mm([(R(n["A"], 0, 64), sel("by", k, 7), R(n["rn"], 64 * k, 64 * k + 64)) for k in range(8)])
+        act(R(n["mob"], 0, 64), R(n["A"], 0, 64), AF.Copy)
+        dma("y", "dmo" + s, [(b, a) for a, b in halves(n["mob"], 0, T.mo, h, 64)], [R(n["mob"], 0, 64)], [], 2500)
+        z0 = zc(RO, h)
+        dma("s", "dzo" + s, [(b, a) for a, b in halves("zz", z0, T.zo, h, 128)], [R("zz", z0, z0 + 128)], [], 2500)
 
     for t in range(RO):
+        now[0] = t
         for h in range(2):
             rows(t, h)
             store(t, h)
-        for h in range(2):
             gap(t, h)
-        if t == RO - 1:
-            tcopy(R("srp", 0, 128), G(R("srf", 0, 128), R("linv", 0, 8)))
-            dd = (None, ("dfl_d", 0, 128))
-            dma("y", "dr1", [(T.dfl_d[k::8, :], T.srp[:, 16 * k:16 * k + 16]) for k in range(8)], [R("srp", 0, 128)], [dd], 4000)
-            dma("y", "dr2", [(T.fl[:], T.dfl_d[:])], [dd], [R("fl", 0, 128)], 2500)
-        for j in (1, 2, 3):
-            for h in range(2):
+            for j in (1, 2, 3):
                 corr(t, h, j)
-        for h in range(2):
             rename(t, h)
         if t < RO - 1:
             count(t)
-
-    cur[:] = [0, "o", 0]
-    win = R("w%d" % ((RO - 1) % 2), 0, 3072)
-    act(R("sob", 0, 1024), G(win, R("fl", 0, 64)), AF.Copy)
-    tcopy(R("sob", 1024, 2048), G(win, R("fl", 64, 128)))
-    dma("s", "dso0", [(T.so[:, 0:1024], T.sob[:, 0:1024])], [R("sob", 0, 1024)], [], 3000)
-    dma("y", "dso1", [(T.so[:, 1024:2048], T.sob[:, 1024:2048])], [R("sob", 1024, 2048)], [], 3000)
-    tcopy(R("mob", 0, 128), G(R("nmf", 0, 128), R("linv", 0, 8)))
-    for q, (eng, sem) in enumerate((("y", "dmo"), ("s", "dm2"))):
-        dma(eng, sem, [(T.mo[k::8, :], T.mob[:, 16 * k:16 * k + 16]) for k in range(4 * q, 4 * q + 4)], [R("mob", 0, 128)], [], 3500)
-    tcopy(R("zob", 0, 256), G(R("zz", 256 * RO, 256 * RO + 256), R("lzo", 0, 16)))
-    dma("s", "dzo", [(T.zo[:], T.zob[:])], [R("zob", 0, 256)], [], 2500)
+    for h in range(2):
+        outputs(h)
     return ops
+
+
+def meet(a, b):
+    (_, l1, h1, s1), (_, l2, h2, s2) = a, b
+    if l1 >= h2 or l2 >= h1:
+        return False
+    if s1 == s2:
+        return (l1 - l2) % s1 == 0
+    if s1 < s2:
+        l1, h1, s1, l2, h2, s2 = l2, h2, s2, l1, h1, s1
+    return any(l2 <= c < h2 and (c - l2) % s2 == 0 for c in range(l1, h1, s1))
 
 
 def link(ops):
     hist = {}
     deps = []
     for i, o in enumerate(ops):
+        o["at"] = i
         d = {}
         if o["after"] is not None:
-            d[[k for k in range(i) if ops[k] is o["after"]][0]] = False
+            d[o["after"]["at"]] = False
         for kind, regs in (("r", o["rd"]), ("w", o["wr"])):
-            for name, lo, hi in regs:
-                psum = name.startswith("ps")
-                for k, kk, l2, h2 in hist.get(name, ()):
+            for reg in regs:
+                psum = reg[0].startswith("ps")
+                for k, kk, r2 in hist.get(reg[0], ()):
                     if k == i:
                         continue
                     same = ops[k]["eng"] == o["eng"] and ops[k]["sem"] is None
-                    over = lo < h2 and l2 < hi
                     if psum and not same:
                         d[k] = True
                     elif psum and o["eng"] == "p":
                         d.setdefault(k, False)
-                    elif over and (kind == "w" or kk == "w"):
+                    elif (kind == "w" or kk == "w") and meet(reg, r2):
                         d[k] = True
         for kind, regs in (("r", o["rd"]), ("w", o["wr"])):
-            for name, lo, hi in regs:
-                hl = hist.setdefault(name, [])
-                if name.startswith("ps"):
+            for reg in regs:
+                hl = hist.setdefault(reg[0], [])
+                if reg[0].startswith("ps"):
                     if o["eng"] == "p":
                         hl[:] = [x for x in hl if x[0] == i]
                 elif kind == "w":
-                    hl[:] = [x for x in hl if not (lo <= x[2] and x[3] <= hi)]
-                hl.append((i, kind, lo, hi))
+                    hl[:] = [x for x in hl if not (x[2] == reg or (reg[3] == 1 and reg[1] <= x[2][1] and x[2][2] <= reg[2]))]
+                hl.append((i, kind, reg))
         deps.append(d)
     return deps
 
 
 def schedule(ops, deps):
     n = len(ops)
-    if "succ" not in ops[0]:
-        succ = [[] for _ in range(n)]
-        for i in range(n):
-            for k, w in deps[i].items():
-                succ[k].append((i, ops[k]["lat"] + LAT if w else 0.0))
-        base = [0.0] * n
-        for i in range(n - 1, -1, -1):
-            base[i] = ops[i]["cost"] + max([d + base[k] for k, d in succ[i]] + [ops[i]["lat"]])
-        ops[0]["succ"] = succ
-        ops[0]["base"] = [base[i] - BIAS * ops[i]["half"] - 1e-3 * i for i in range(n)]
-    succ = ops[0]["succ"]
-    prio = [b + 100.0 * OFFS.get(o["cls"], 0) for b, o in zip(ops[0]["base"], ops)]
-    slack = [SLACK + 20.0 * max(0, OFFS.get(o["cls"] + "w", 0)) for o in ops]
+    succ = [[] for _ in range(n)]
+    for i in range(n):
+        for k, w in deps[i].items():
+            succ[k].append((i, ops[k]["lat"] + LAT if w else 0.0))
+    base = [0.0] * n
+    for i in range(n - 1, -1, -1):
+        base[i] = ops[i]["cost"] + max([d + base[k] for k, d in succ[i]] + [ops[i]["lat"]])
+    prio = [base[i] - BIAS * ops[i]["half"] - 1e-3 * i for i in range(n)]
     left = [len(d) for d in deps]
     ready_at = [0.0] * n
     ready = {}
@@ -574,41 +597,34 @@ def schedule(ops, deps):
             ready.setdefault(ops[i]["eng"], []).append(i)
     free = {}
     order = []
-    end = 0.0
     while len(order) < n:
-        best = None
-        for e, lst in ready.items():
-            if not lst:
-                continue
-            f = free.get(e, 0.0)
-            first = max(f, min([ready_at[i] for i in lst]))
-            if best is None or first < best[0]:
-                best = (first, e)
-        first, e = best
-        i = max([i for i in ready[e] if ready_at[i] <= first + slack[i]], key=lambda i: prio[i])
-        st = max(free.get(e, 0.0), ready_at[i])
+        first, e = min((max(free.get(e, 0.0), min(ready_at[i] for i in lst)), e) for e, lst in ready.items() if lst)
+        i = max([i for i in ready[e] if ready_at[i] <= first + 30.0], key=lambda i: prio[i])
         ready[e].remove(i)
-        o = ops[i]
-        fin = st + o["cost"]
-        free[e] = fin
-        o["t0"] = st
-        end = max(end, fin + o["lat"])
+        fin = free[e] = max(free.get(e, 0.0), ready_at[i]) + ops[i]["cost"]
         order.append(i)
         for k, d in succ[i]:
-            if fin + d > ready_at[k]:
-                ready_at[k] = fin + d
+            ready_at[k] = max(ready_at[k], fin + d)
             left[k] -= 1
             if left[k] == 0:
                 ready.setdefault(ops[k]["eng"], []).append(k)
-    return order, end
+    return order
 
 
-SLACK = 30.0
 BIAS = 3000.0
-ITER = 3500
-OFFS = {}
+PASSES = 4000
+LAST = 300
+HEAT = 200.0
+SEED = 7
 PLAN = {}
-SETS = [(1.2, 60.0, 0.5, 3000.0), (1.56, 90.0, 0.5, 3500.0), (1.9, 60.0, 0.5, 4000.0), (1.56, 150.0, 0.6, 4000.0)]
+SETS = [(1.3, 150.0, 0.5, 5000.0, 2.5), (1.56, 150.0, 0.5, 4500.0, 3.8), (2.0, 100.0, 0.5, 4000.0, 5.5), (1.56, 220.0, 0.5, 6000.0, 3.8)]
+
+
+def table(ops, deps):
+    return [(o["eng"], [(o["cost"] + o["ga"] * (ga - GA) + o["sc"] * (sc - SC)) * (cpe / CPE if o["eng"] == "p" else 1.0)
+                        for ga, _, cpe, _, sc in SETS],
+             [cm if o["eng"] == "x" else o["lat"] for _, _, _, cm, _ in SETS],
+             [k for k, w in d.items() if w], [k for k, w in d.items() if not w]) for o, d in zip(ops, deps)]
 
 
 def replay(rows, order, s):
@@ -630,40 +646,151 @@ def replay(rows, order, s):
     return max(done)
 
 
-def tune(T):
+def chain(rows, order, s):
+    lat = SETS[s][1]
+    n = len(rows)
+    fin, done, why, held = [0.0] * n, [0.0] * n, [-1] * n, [False] * n
+    last = {}
+    for i in order:
+        e, cs, ls, hard, soft = rows[i]
+        st, w = 0.0, -1
+        for k in hard:
+            if done[k] > st:
+                st, w = done[k], k
+        for k in soft:
+            if fin[k] > st:
+                st, w = fin[k], k
+        k = last.get(e, -1)
+        if k >= 0 and fin[k] > st + 1.0:
+            st, w = fin[k], k
+            held[i] = True
+        why[i] = w
+        last[e] = i
+        fin[i] = st + cs[s]
+        done[i] = fin[i] + ls[s] + lat
+    i = max(range(n), key=lambda i: done[i])
+    pairs = []
+    while i >= 0:
+        if held[i]:
+            pairs.append((i, why[i]))
+        i = why[i]
+    return pairs
+
+
+def place(seq, eng, cost, pred):
+    start = [0.0] * len(eng)
+    busy = {}
+    for i in seq:
+        st = 0.0
+        for k, d in pred[i]:
+            v = start[k] + d
+            if v > st:
+                st = v
+        a, b = busy.setdefault(eng[i], ([], []))
+        c = cost[i]
+        lo, hi = 0, len(b)
+        while lo < hi:
+            mid = (lo + hi) // 2
+            if b[mid] <= st:
+                lo = mid + 1
+            else:
+                hi = mid
+        while lo < len(a) and a[lo] < st + c:
+            if b[lo] > st:
+                st = b[lo]
+            lo += 1
+        a.insert(lo, st)
+        b.insert(lo, st + c)
+        start[i] = st
+    return start
+
+
+def links(ops, deps):
+    cost = [o["cost"] + 0.01 for o in ops]
+    return ([o["eng"] for o in ops], cost,
+            [[(k, cost[k] + (ops[k]["lat"] + LAT if w else 0.0)) for k, w in d.items()] for d in deps])
+
+
+def valid(key, deps):
+    key = list(key)
+    for i, d in enumerate(deps):
+        for k in d:
+            if key[k] >= key[i]:
+                key[i] = key[k] + 1e-3
+    return sorted(range(len(key)), key=lambda i: key[i])
+
+
+def refine(ops, deps, order, passes):
+    n = len(ops)
+    rows = table(ops, deps)
+    eng, cost, fwd = links(ops, deps)
+    bwd = [[(n, ops[i]["lat"])] for i in range(n)]
+    for i in range(n):
+        for k, d in fwd[i]:
+            bwd[k].append((i, d - cost[k] + cost[i]))
+    seed = [SEED]
+
+    def rnd():
+        seed[0] = (seed[0] * 1103515245 + 12345) % 2147483648
+        return (seed[0] >> 8) / 8388608.0
+
+    def score(o):
+        return sum(replay(rows, o, s) for s in range(len(SETS)))
+
+    best = now = score(order)
+    keep = order
+    cls = sorted(set(o["cls"] for o in ops))
+    start = place(order, eng, cost, fwd)
+    held = None
+    for it in range(passes):
+        shift = {}
+        if it % 3:
+            if not held:
+                held = [chain(rows, order, s) for s in range(len(SETS))]
+            pairs = held[int(rnd() * len(held))]
+            for _ in range(1 + int(rnd() * 2)):
+                i, k = pairs[int(rnd() * len(pairs))]
+                if rnd() < 0.5:
+                    shift[ops[i]["cls"]] = start[k] - start[i] - 1.0 - 400.0 * rnd() * rnd()
+                else:
+                    shift[ops[k]["cls"]] = start[i] - start[k] + 1.0 + 1500.0 * rnd() * rnd()
+        else:
+            for _ in range(1 + int(rnd() * 5)):
+                shift[cls[int(rnd() * len(cls))]] = (rnd() - 0.5) * (300.0, 1000.0, 3000.0)[int(rnd() * 3)]
+        st = place(valid([start[i] + shift.get(ops[i]["cls"], 0.0) for i in range(n)], deps), eng, cost, fwd)
+        if it % 7 == 0:
+            back = place([n] + sorted(range(n), key=lambda i: -st[i] - cost[i]), eng + ["t"], cost + [0.0], bwd + [[]])
+            st = place(sorted(range(n), key=lambda i: -back[i] - cost[i]), eng, cost, fwd)
+        o = sorted(range(n), key=lambda i: st[i])
+        s = score(o)
+        if s <= now + HEAT * (1.0 - it / passes) * rnd():
+            now, order, start, held = s, o, st, None
+            if s < best:
+                best, keep = s, o
+    start = place(keep, eng, cost, fwd)
+    for i in range(n):
+        ops[i]["t0"] = start[i]
+    return keep, best / len(SETS)
+
+
+def plan(T):
     ops = build(T, 3)
     deps = link(ops)
-    rows = [(o["eng"], [(o["cost"] + o["ga"] * (ga - GA)) * (cpe / CPE if o["eng"] == "p" else 1.0) for ga, _, cpe, _ in SETS],
-             [cm if o["eng"] == "x" else o["lat"] for _, _, _, cm in SETS],
-             [k for k, w in d.items() if w], [k for k, w in d.items() if not w]) for o, d in zip(ops, deps)]
-
-    def score():
-        order, _ = schedule(ops, deps)
-        return sum(replay(rows, order, s) for s in range(len(SETS)))
-
-    cls = sorted(set(o["cls"] for o in ops if o["eng"] in "vsp"))
-    seed = [12345]
-
-    def rnd(k):
-        seed[0] = (seed[0] * 1103515245 + 12345) % 2147483648
-        return (seed[0] >> 8) % k
-
-    best = score()
-    for _ in range(ITER):
-        old = dict(OFFS)
-        for _ in range((1, 3, 6)[rnd(3)]):
-            c = cls[rnd(len(cls))]
-            if rnd(3) == 0:
-                OFFS[c + "w"] = (0, 3, 8, 20)[rnd(4)]
-            else:
-                OFFS[c] = OFFS.get(c, 0) + (-20, -8, -3, -1, 1, 3, 8, 20)[rnd(8)]
-        s = score()
-        if s <= best:
-            best = s
-        else:
-            OFFS.clear()
-            OFFS.update(old)
-    return best / len(SETS)
+    refine(ops, deps, schedule(ops, deps), PASSES)
+    at = {(o["t"], o["cls"]): o["t0"] for o in ops}
+    sends = [o["t0"] for o in ops if o["eng"] == "x"]
+    step = sends[2] - sends[0]
+    ops = build(T)
+    deps = link(ops)
+    key = []
+    for o in ops:
+        q = min(o["t"], 1) if o["t"] < RO - 1 else 2
+        key.append(at[q, o["cls"]] + step * (o["t"] - q))
+    eng, cost, fwd = links(ops, deps)
+    st = place(valid(key, deps), eng, cost, fwd)
+    PLAN["deps"] = deps
+    PLAN["ops"] = ops
+    PLAN["order"], PLAN["end"] = refine(ops, deps, sorted(range(len(ops)), key=lambda i: st[i]), LAST)
 
 
 def route(T, topo, t, r):
@@ -681,6 +808,10 @@ def arrivals(T, topo, t, r):
     return len(topo.engines(T.cores[q] if hop == dst else hop, dst))
 
 
+def landing(T, t, h):
+    return T.zz[:, zc(t + 1, h):zc(t + 1, h) + 128]
+
+
 def relay_program(g, core, T, topo):
     sent = 0
     for t in range(RO):
@@ -691,7 +822,7 @@ def relay_program(g, core, T, topo):
             rid, pid = topo.addr(dst, core)
             for h in range(2):
                 sem = T.sem["ar%d" % (2 * t + h)]
-                z = T.zz[:, 256 * (t + 1) + 128 * h:256 * (t + 1) + 128 * h + 128]
+                z = landing(T, t, h)
                 g.wait_ge(sem, len(topo.engines(T.cores[r], core)))
                 g.remote_dma(z, z, sem, T.sem.sent, pid, rid, topo.mask(core, dst))
                 sent += len(topo.engines(core, dst))
@@ -704,13 +835,9 @@ def rank_program(g, core, T, topo):
     if rank is None:
         relay_program(g, core, T, topo)
         return
-    ops = build(T)
     if not PLAN:
-        PLAN["tuned"] = tune(T)
-        deps = link(ops)
-        PLAN["deps"] = deps
-        PLAN["order"], PLAN["end"] = schedule(ops, deps)
-        PLAN["ops"] = ops
+        plan(T)
+    ops = build(T)
     deps = PLAN["deps"]
     queue = {"v": g.vector, "s": g.scalar, "p": g.tensor, "g": g, "y": g.sync}
     csem = {"v": "cv", "s": "cs", "p": "cp", "g": "cg"}
@@ -740,8 +867,7 @@ def rank_program(g, core, T, topo):
             t, h = o["send"]
             hop, _ = route(T, topo, t, rank)
             rid, pid = topo.addr(hop, core)
-            z = T.zz[:, 256 * (t + 1) + 128 * h:256 * (t + 1) + 128 * h + 128]
-            g.remote_dma(z, o["src"], T.sem["ar%d" % (2 * t + h)], T.sem.sent, pid, rid, topo.mask(core, hop))
+            g.remote_dma(landing(T, t, h), o["src"], T.sem["ar%d" % (2 * t + h)], T.sem.sent, pid, rid, topo.mask(core, hop))
             count["sent"] = count.get("sent", 0) + len(topo.engines(core, hop))
             mark[i] = ("sent", count["sent"], dict(kn))
             continue
@@ -750,7 +876,7 @@ def rank_program(g, core, T, topo):
             s = o["sem"]
             for x in ins:
                 x.then_inc(T.sem[s], 16)
-            count[s] = 16 * len(ins)
+            count[s] = count.get(s, 0) + 16 * len(ins)
         else:
             s = csem[e]
             ins[-1].then_inc(T.sem[s], 1)

@@ -4,21 +4,23 @@ OP = AluOpType
 AF = ActivationFunctionType
 RO, NR = 5, 8
 NB = 6
-Z1 = 9
+N1 = 10
 AL = [2] * 5
 SG = [(3, 0, 1), (2, 1, 4), (3, 4, 6)]
-SP = [(0, 16)]
+SP = [(0, 6), (6, 16)]
 RG = [(0, 2, "v"), (2, 4, "s"), (4, 6, "v"), (6, 8, "s")]
-SI = True
 F16 = "float16"
 MAGIC = 12582912.0
 BIG = 33554432.0
-Z2 = 16 - Z1
+N2 = 16 - N1
+DUP = max(AL)
+Z1, Z2 = N1 | 1, (N2 + 1) | 1
+PW = 72 + 8 * (Z1 + Z2)
 DWW = 128 * (17 + 16 - NB)
 
 
 def code(m):
-    return 15 - NB + m if m < NB else 17 + m - NB
+    return 17 - DUP - NB + m if m < NB else 17 + m - NB
 
 
 def span(z):
@@ -34,16 +36,16 @@ def _sb(name, w, d):
 
 for _n, _w, _d in [
     ("zz", 6 * 256, "bfloat16"), ("ob", 5 * 256, "bfloat16"), ("w0", 3072, "bfloat16"), ("w1", 3072, "bfloat16"),
-    ("pi", 16, "int32"), ("pf", 16, "float32"), ("pc", 16, "float32"), ("xi", 144, "float32"), ("i1", 128, "float32"),
+    ("pi", 16, "int32"), ("pf", 16, "float32"), ("pc", 16, "float32"), ("xi", 144, "float32"), ("i1", PW, "float32"),
     ("i2", 128, "float32"), ("i3", 128, "float32"), ("i4", 32, "float32"), ("i6", 144, "float32"), ("i7", 64, "float32"),
-    ("i8", 64, "float32"), ("i9", 200, "float32"), ("ia", 200, "float32"), ("ib", 32, "float32"),
+    ("i8", 64, "float32"), ("i9", PW, "float32"), ("ia", PW, "float32"), ("ib", 48, "float32"),
     ("z1", 144, "bfloat16"), ("z4", 144, "bfloat16"), ("zq", 144, "bfloat16"), ("idb", 128, "bfloat16"),
     ("nid", 128, "bfloat16"), ("hid", 128, "bfloat16"), ("one", 128, "bfloat16"), ("qrt", 128, "bfloat16"),
     ("idh", 128, F16), ("nih", 128, F16), ("i128", 128, F16), ("bz", 144, F16), ("by", 144, F16),
-    ("blk", 128, "float32"), ("mk8", 16, "float32"), ("k0j", 8, "float32"),
-    ("posk", 64, "float32"), ("poskh", 64, F16), ("ck", 64, F16), ("pa", 200, "bfloat16"), ("pb", 200, "bfloat16"),
-    ("rst", 232, "float32"), ("ub", 32, "bfloat16"), ("ti8", 8, "float32"), ("lrep", 8, "uint16"), ("lrs", 2, "uint16"),
-    ("rel", 16, "bfloat16"), ("cnt", 16, "int32"), ("cntf", 8, "float32"), ("ofc", 16, "float32"),
+    ("blk", 128, "float32"), ("mk8", 16, "float32"), ("k0j", 48, "float32"), ("ij", 24, "float32"), ("lr2", 8, "uint16"),
+    ("posk", 64, "float32"), ("poskh", 64, F16), ("ck", 64, F16), ("pa", PW, "bfloat16"), ("pb", PW, "bfloat16"),
+    ("rst", PW + 32, "float32"), ("ub", 32, "bfloat16"), ("pd", 8 * Z1, "bfloat16"), ("ti8", 8, "float32"), ("lrep", 8, "uint16"), ("lrs", 2, "uint16"), ("lr4", 16, "uint16"),
+    ("rel", 16, "bfloat16"), ("cnt", 16, "int32"), ("cntf", 8, "float32"),
 ]:
     _sb(_n, _w, _d)
 for _h in range(2):
@@ -52,9 +54,9 @@ for _h in range(2):
         ("mob", 64, "float32"), ("rn", 512, F16), ("wk", 8, "int32"), ("wf", 8, "float32"), ("zw", 144, "bfloat16"),
         ("m16", 128, "float32"), ("kapr", 128, "float32"), ("kq", 48, "int32"), ("kqf", 32, "float32"), ("kt", 32, "bfloat16"),
         ("dw", DWW, "bfloat16"), ("a1", span(Z1), "bfloat16"), ("a2", span(Z2), "bfloat16"), ("gb", span(9), "bfloat16"),
-        ("ge", 256, "bfloat16"), ("kg", 384, "bfloat16"), ("d7", 128, "bfloat16"), ("sc", 264, "float32"),
-        ("si", 368, "int32"), ("tt", 256, "int32"), ("tf", 128, "float32"), ("c16", 128, "uint16"), ("l16", 96, "uint16"),
-        ("src", 64, "uint16"), ("nm", 96, F16), ("hh", 64 * 12, F16), ("sf", 176, "float32"), ("rs", 96, "float32"),
+        ("ge", 256, "bfloat16"), ("kg", 384, "bfloat16"), ("d7", 128, "bfloat16"), ("sc", 9 * Z1 * Z2, "float32"),
+        ("fu", 80, "int32"), ("ff", 72, "float32"), ("si", 368 + 24 * Z2, "int32"), ("tt", 256, "int32"), ("tf", 128, "float32"), ("c16", 128, "uint16"), ("l16", 96, "uint16"),
+        ("src", 64, "uint16"), ("nm", 96, F16), ("hh", 64 * 16, F16), ("sf", 176, "float32"), ("rs", 96, "float32"),
     ]:
         _sb(_n + str(_h), _w, _d)
 for _b in range(8):
@@ -63,8 +65,8 @@ for _b in range(8):
 DMAS = [n + str(h) for h in range(2) for n in ("dwk", "dar", "dst", "drc", "dnm", "dso", "dzo", "dmo", "dx")]
 SEMAPHORES = ["cv", "cs", "cp", "cg", "sent"] + DMAS + ["ar%d" % i for i in range(2 * RO)]
 
-CV, CPE, LAT, GA, SC, COMM, DXL = 1.0, 0.5, 150.0, 1.56, 3.8, 4500.0, 3500.0
-SEG = {"g": (0, 9), 1: (72, Z1), 2: (72 + 8 * Z1, Z2), "u": (200, 4)}
+CV, CPE, LAT, GA, SC, COMM, DXL = 1.0, 0.55, 215.0, 1.65, 4.3, 5200.0, 4200.0
+SEG = {"g": (0, 9), 1: (72, Z1), 2: (72 + 8 * Z1, Z2), "u": (PW, 4)}
 
 
 def zc(t, h):
@@ -115,9 +117,9 @@ def build(T, RO=RO):
 
     def vcost(out, ins, tt=False):
         if len(out) == 5:
-            return 50 + out[2] * SC * CV
+            return 60 + out[2] * SC * CV
         if len(ins[0]) == 5:
-            return 50 + out[2] * GA * CV
+            return 60 + out[2] * GA * CV
         f = 0.5 if two(out, *ins) else 1.0
         if tt and not any(x[1][0].startswith("ps") for x in ins):
             f *= 2
@@ -143,7 +145,7 @@ def build(T, RO=RO):
         return add("v", lambda e: [e.memset(out[0], v)], [], [out], max(64, out[2] * (0.5 if two(out) else 1)) * CV)
 
     def act(out, a, func):
-        cost = 65 + out[2] * GA * CV if len(a) == 5 else max(64, out[2]) * CV
+        cost = 78 + out[2] * GA * CV if len(a) == 5 else max(64, out[2]) * CV
         return add("s", lambda e: [e.activation(out[0], a[0], func)], [a], [out], cost)
 
     def pick(e, out, a):
@@ -227,22 +229,32 @@ def build(T, RO=RO):
     tt(C("pc", 7), C("pc", 11), C("pf", 9), OP.add)
     ts(R("lrs", 0, 2), R("xi", 0, 2), 4.0, OP.mult, C("pc", 7), OP.add)
     ts(R("lrep", 0, 8), R("xi", 0, 8), 0.0, OP.mult, C("pf", 2), OP.add)
+    ts(C("pc", 12), C("pf", 2), 3.0, OP.mult, 1.0, OP.add)
+    ts(R("lr2", 0, 8), R("xi", 0, 8), 0.0, OP.mult, C("pc", 12), OP.add)
+    iota(R("ij", 0, 24), [[1, 3], [0, 8]], 1)
+    iota(R("ib", 32, 48), [[8, 4], [0, 4]], 0)
+    ts(R("lr4", 0, 16), R("ib", 32, 48), C("pf", 2), OP.add)
     iota(R("i7", 0, 64), [[128, 8], [0, 8]], 0)
     iota(R("i8", 0, 64), [[128, 8], [16, 8]], 0)
     ts(R("posk", 0, 64), R("i8", 0, 64), C("pf", 1), OP.add)
     tcopy(R("poskh", 0, 64), R("posk", 0, 64))
     ts(R("ck", 0, 64), R("i7", 0, 64), -1.0, OP.mult, 1024.0, OP.add)
-    for k, base in (("g", 0), (1, 15 - NB), (2, 15 - NB + Z1)):
+    for k, base in (("g", 0), (1, code(0)), (2, code(0) + N1)):
         c0, z = SEG[k]
         iota(R("i9", c0, c0 + 8 * z), [[0, 8], [128, z]], 128 * base)
         iota(R("ia", c0, c0 + 8 * z), [[16, 8], [0, z]], 0)
-    ts(R("i1", 0, 128), R("i9", 72, 200), 128.0 * 15, OP.is_ge, 256.0, OP.mult)
-    tt(R("pa", 72, 200), R("i9", 72, 200), R("i1", 0, 128), OP.add)
+    ts(R("i1", 0, PW - 72), R("i9", 72, PW), 128.0 * (17 - DUP), OP.is_ge, 128.0 * DUP, OP.mult)
+    tt(R("pa", 72, PW), R("i9", 72, PW), R("i1", 0, PW - 72), OP.add)
+    for m in range(N2, Z2):
+        mset(R("pa", SEG[2][0] + m, PW, Z2), -BIG)
     tcopy(R("pa", 0, 72), R("i9", 0, 72))
-    ts(R("pb", 0, 200), R("ia", 0, 200), C("pf", 1), OP.add)
-    iota(R("rst", 0, 232), [[0, 232]], 0)
-    for c0, z in SEG.values():
+    ts(R("pb", 0, PW), R("ia", 0, PW), C("pf", 1), OP.add)
+    iota(R("rst", 0, PW + 32), [[0, PW + 32]], 0)
+    for k in ("g", 1, "u"):
+        c0, z = SEG[k]
         mset(R("rst", c0, c0 + 8 * z, z), BIG)
+    iota(R("pd", 0, 8 * Z1), [[0, 8 * Z1]], 0)
+    mset(R("pd", 0, 8 * Z1, Z1), -128.0)
     iota(R("i6", 0, 144), [[1, 9], [0, 4], [100, 4]], -300)
     ts(R("zq", 0, 144), R("i6", 0, 144), C("pf", 4), OP.is_equal)
     iota(R("ib", 0, 32), [[0, 8], [1, 4]], 0)
@@ -260,23 +272,25 @@ def build(T, RO=RO):
         scale(R("zw" + s, 0, 144), R("zq", 0, 144), C(wf, 0))
         ts(R("m16" + s, 0, 128), R("i2", 0, 128), C("pf", 1), OP.is_equal, C(wf, 4), OP.mult)
         mm([(R(B, 0, 128), R("blk", 0, 128), R("m16" + s, 0, 128))])
-        act(R(kapr, 0, 128), R(B, 0, 128), AF.Copy)
-        ts(R("k0j", 3 * h, 3 * h + 3), R("xi", 1, 4), C(kapr, 0), OP.mult, -31.0 / 64, OP.add)
-        tcopy(R("ofc", 3 * h, 3 * h + 3), R("k0j", 3 * h, 3 * h + 3))
+        scale(R(kapr, 0, 128), R(B, 0, 128), 32.0)
+        ts(R("k0j", 24 * h, 24 * h + 24), R("ij", 0, 24), C(kapr, 0), OP.mult)
+        iota(R("fu" + s, 0, 80), [[0, 80]], 0)
+        tcopy(R("fu" + s, 2, 72, 3), R("k0j", 24 * h, 24 * h + 24))
         tcopy(R(kq, 0, 16), R(kapr, 0, 128, 8))
-        ts(R(kq, 16, 32), R(kq, 0, 16), 31, OP.bitwise_and)
+        ts(R(kq, 16, 32), R(kq, 0, 16), 1023, OP.bitwise_and)
         tt(R(kq, 32, 48), R(kq, 0, 16), R(kq, 16, 32), OP.subtract)
         ts(R(kqf, 0, 16), R(kq, 16, 32), C("pc", 5), OP.mult)
         ts(R(kqf, 16, 32), R(kq, 32, 48), C("pc", 6), OP.mult)
         iota(R(kt, 0, 32), [[0, 32]], 0)
         tt(R(kt, code(0), code(0) + NB), R(kqf, 0, NB), R(kqf, 16, 16 + NB), OP.add)
         tt(R(kt, 17, 33 - NB), R(kqf, NB, 16), R(kqf, 16 + NB, 32), OP.add)
-        for c in range(0, 128 * code(0), 384):
-            e = min(c + 384, 128 * code(0))
+        for c in range(0, 128 * (code(0) - 2), 384):
+            e = min(c + 384, 128 * (code(0) - 2))
             iota(R("dw" + s, c, e), [[0, e - c]], 0)
-        if max(AL) == 1:
-            iota(R("dw" + s, 1920, 2048), [[0, 128]], 0)
-        mset(slot("gb" + s, 9, 8), 0.0)
+        for buf, z, m0 in (("gb", 9, 8), ("a1", Z1, N1), ("a2", Z2, N2)):
+            for m in range(m0, z):
+                iota(slot(buf + s, z, m), [[0, 128]], 0)
+        iota(R("sc" + s, Z2 * (N1 - 1), Z2 * (N1 - 1) + 8 * Z1 * Z2, Z1), [[0, 8 * Z2]], 0)
         ts(R("nm" + s, 64, 96), R("i4", 0, 32), C("pf", 1), OP.add)
         ts(R("sf" + s, 32, 40), R("i4", 0, 8), C("pf", 1), OP.add)
         iota(R("sf" + s, 0, 8), [[0, 8]], 0)
@@ -293,30 +307,27 @@ def build(T, RO=RO):
         s = str(h)
         cur[:] = [h, tag, 0]
         d = {k: k + s for k in ("tf", "dw", "a1", "a2", "gb", "ge", "kg", "d7", "sc", "si", "tt", "c16", "l16", "src", "nm", "hh",
-                                "sf", "rs", "xw", "zw", "kapr", "kt", "sti", "sob", "mob", "rn")}
+                                "sf", "rs", "xw", "zw", "kapr", "kt", "sti", "sob", "mob", "rn", "fu", "ff")}
         d.update(A="ps%d" % (4 * h), B="ps%d" % (4 * h + 1), Cb="ps%d" % (4 * h + 2), D="ps%d" % (4 * h + 3))
         d["bank"] = [d["A"], d["B"], d["Cb"], d["D"]]
         return d
 
-    def keys(out, buf, seg):
+    def keys(out, buf, seg, more=()):
         c0, z = SEG[seg]
-        mm([(out, idb, R("pa", c0, c0 + 8 * z)), (out, idb, R("pb", c0, c0 + 8 * z))], True, False)
+        mm([(out, idb, R("pa", c0, c0 + 8 * z)), (out, idb, R("pb", c0, c0 + 8 * z))] + [(out, idb, x) for x in more], True, False)
         mm([(out, sel("z4", a), R(buf, z * a, z * a + 128 * z, 16)) for a in range(16)], False, True)
 
-    def least(n, ps, seg):
+    def least(buf, c, ps, seg, last):
         c0, z = SEG[seg]
-        scan(R(n["sc"], c0, c0 + 8 * z), R("rst", c0, c0 + 8 * z), ps, OP.add, OP.min)
+        scan(R(buf, c, c + 8 * z), R("rst", c0, c0 + 8 * z), ps, OP.add, OP.min)
+        return R(buf, c + last, c + 8 * z, z)
 
-    def low(n, out, ps, seg, last, c, tmp, mask):
-        c0, z = SEG[seg]
-        if SI:
-            scan(R(n["si"], c, c + 8 * z), R("rst", c0, c0 + 8 * z), ps, OP.add, OP.min)
-            ts(out, R(n["si"], c + last, c + 8 * z, z), mask, OP.bitwise_and)
-        else:
-            c = c0 + (32 if c == 336 else 0)
-            scan(R(n["sc"], c, c + 8 * z), R("rst", c0, c0 + 8 * z), ps, OP.add, OP.min)
-            tcopy(tmp, R(n["sc"], c + last, c + 8 * z, z))
-            ts(out, tmp, mask, OP.bitwise_and)
+    def bits(pieces, lst, tmp):
+        c = 0
+        for a, mask in pieces:
+            ts(R(tmp[1][0], tmp[1][1] + c, tmp[1][1] + c + a[2]), a, mask, OP.bitwise_and)
+            c += a[2]
+        tcopy(lst, tmp)
 
     def quads(ps, z, src, lo):
         mm([(ps, idb, R("ub", 0, 32))], True, False)
@@ -330,8 +341,8 @@ def build(T, RO=RO):
         if main:
             s = R(n["dw"], 2048, 2176)
             ts(s, ps, MAGIC, OP.add, -MAGIC, OP.add)
-            if max(AL) > 1:
-                gcopy(R(n["dw"], 1920, 2048), s)
+            for i in range(1, DUP):
+                gcopy(R(n["dw"], 2048 - 128 * i, 2176 - 128 * i), s)
             gcopy(keep, s)
         else:
             ts(keep, ps, MAGIC, OP.add, -MAGIC, OP.add)
@@ -354,9 +365,9 @@ def build(T, RO=RO):
         z0 = zc(t, h)
         ps = R(n["A"], 0, 32)
         quads(ps, "zq", "zz", z0)
-        low(n, R(si, 16, 24), ps, "u", 3, 336, R(si, 0, 8), 7)
-        tt(R(si, 32, 40), R(si, 16, 24), R("ti8", 0, 8), OP.add)
-        tcopy(R(n["l16"], 0, 8), R(si, 32, 40))
+        ts(R(si, 16, 24), least(si, 336, ps, "u", 3), 7, OP.bitwise_and)
+        tt(R(n["sf"], 72, 80), R(si, 16, 24), R("ti8", 0, 8), OP.add)
+        tcopy(R(n["l16"], 0, 8), R(n["sf"], 72, 80))
         X = R(n["xw"], 128, 2176)
         tcopy(G(X, R(n["l16"], 0, 8)), R("zz", z0, z0 + 128))
         x = T[n["xw"]]
@@ -375,8 +386,8 @@ def build(T, RO=RO):
         ps = R(n["B"], 0, 72)
         keys(ps, n["gb"], "g")
         off = R(si, 56, 64)
-        low(n, off, ps, "g", 7, 264, R(si, 48, 56), 4095)
-        tcopy(R(n["l16"], 16, 24), off)
+        key = least(si, 264, ps, "g", 7)
+        bits([(key, 4095)], R(n["l16"], 16, 24), off)
         ge = R(n["ge"], 0, 128)
         act(ge, G(R(w[0], w[1], w[1] + 1024), R(n["l16"], 16, 24)), AF.Copy)
         settle(n, w, 1024, [z, ge])
@@ -396,7 +407,9 @@ def build(T, RO=RO):
            + [(R(b, 384 + 8 * j, 448), idh, H(3, 0, 64 - 8 * j)) for j in range(4)])
         tcopy(R(n["src"], 0, 64), R(b, 384, 448))
         tt(H(7, 0, 56), R(nm, 8, 64), H(2, 0, 56), OP.mult)
-        tt(H(8), G(R(si, 32, 40), lrep4), H(0), OP.mult)
+        gcopy(H(12), H(0))
+        gcopy(H(13), H(0))
+        gcopy(H(14, 0, 128), H(12, 0, 128))
 
     def corr(t, h, j):
         n = names(h, "abc"[j - 1])
@@ -404,30 +417,36 @@ def build(T, RO=RO):
         w = ("w%d" % (t % 2), 1536 * h)
         X = R(n["xw"], 128, 2176)
         s = R(dw, 2048, 2176)
-        D = lambda m0, m1: R(dw, 128 * code(m0), 128 * code(m1 - 1) + 128)
+        c0 = code(0) - 3 + j
+        D = lambda m0, m1: R(dw, 128 * code(m0), 128 * code(m1 - 1) + 128) if m0 else R(dw, 128 * c0, 128 * c0 + 128)
         L = lambda m0, m1: R(n["c16"], 8 * m0, 8 * m1)
-        AB = lambda m: slot(n["a1"], Z1, m) if m < Z1 else slot(n["a2"], Z2, m - Z1)
+        AB = lambda m: slot(n["a1"], Z1, m) if m < N1 else slot(n["a2"], Z2, m - N1)
         ps = R(n["A"], 0, 32)
         quads(ps, n["zw"], dw, 2048)
-        u, f = R(si, 64 + 8 * j, 72 + 8 * j), R(si, 88 + 8 * j, 96 + 8 * j)
-        low(n, u, ps, "u", 3, 232, R(si, 64, 72), 2047)
-        tt(R(sf, 72, 80), u, u, OP.mult)
-        ts(f, R(sf, 72, 80), 1.0 / 32, OP.mult, C("ofc", 8 * (t % 2) + 3 * h + j - 1), OP.add)
+        fu, c = n["fu"], 24 * j - 24
+        ts(R(fu, c + 1, c + 24, 3), least(si, 232, ps, "u", 3), 2047, OP.bitwise_and)
+        u, f = R(fu, c, c + 24), R(n["ff"], c, c + 24)
+        scan(f, u, R(fu, c + 1, c + 25), OP.mult, OP.add)
         for m0, m1 in SP:
-            rep = R("lrep", 0, (m1 - m0) // 2)
+            rep = R("lr2", 0, (m1 - m0) // 2)
             tt(R(tf, 8 * m0, 8 * m1), G(u, rep), R(n["kapr"], 8 * m0, 8 * m1), OP.mult)
             tt(R(tw, 8 * m0, 8 * m1), G(f, rep), R(tf, 8 * m0, 8 * m1), OP.add)
             m0 = max(m0, 1)
-            ts(R(tw, 128 + 8 * m0, 128 + 8 * m1), R(tw, 8 * m0, 8 * m1), 2047, OP.bitwise_and)
+            ts(R(tw, 128 + 8 * m0, 128 + 8 * m1), R(tw, 8 * m0, 8 * m1), 5, OP.arith_shift_right, 2047, OP.bitwise_and)
             tcopy(L(m0, m1), R(tw, 128 + 8 * m0, 128 + 8 * m1))
-        act(D(0, 1), G(X, R(n["l16"], 16 + 8 * j, 24 + 8 * j)), AF.Copy)
+        if j == 1:
+            back = cur[2]
+            cur[2] = 300
+            act(R(dw, 128 * c0, 128 * c0 + 384), G(X, R(n["l16"], 24, 48)), AF.Copy)
+            cur[2] = back
         if j == 3:
             back = cur[2]
             cur[2] = 100
             settle(n, w, 1408, [s, D(0, 1)], False)
             z = R("zz", zc(t, h), zc(t, h) + 128)
-            tt(R(n["d7"], 0, 128), G(R(w[0], w[1], w[1] + 1536), R(n["src"], 56, 64)), z, OP.subtract)
-            act(R(n["xw"], 0, 128), R(n["d7"], 0, 128), AF.Abs)
+            act(R(n["d7"], 0, 128), G(R(w[0], w[1], w[1] + 1536), R(n["src"], 56, 64)), AF.Copy)
+            mm([(R(n["A"], 128, 256), nid, z), (R(n["A"], 128, 256), idb, R(n["d7"], 0, 128))])
+            act(R(n["xw"], 0, 128), R(n["A"], 128, 256), AF.Abs)
             cur[2] = back
         for b, m0, m1 in SG:
             b = n["bank"][b]
@@ -444,15 +463,13 @@ def build(T, RO=RO):
                 act(AB(m + i), D(m + i, m + i + 1), AF.Abs)
             m += k
         p1, p2 = R(n["A"], 256, 256 + 8 * Z1), R(n["B"], 0, 8 * Z2)
-        keys(p1, n["a1"], 1)
-        least(n, p1, 1)
+        keys(p1, n["a1"], 1, [R("pd", 0, 8 * Z1)] * (3 - j))
+        scan(R(n["sc"], 0, 8 * Z1 * Z2, Z2), R("rst", 72, 72 + 8 * Z1), p1, OP.add, OP.min)
         keys(p2, n["a2"], 2)
-        least(n, p2, 2)
-        key = R(si, 112 + 8 * j, 120 + 8 * j)
-        tt(key, R(n["sc"], 71 + Z1, 72 + 8 * Z1, Z1), R(n["sc"], 71 + 8 * Z1 + Z2, 200, Z2), OP.min)
-        ts(R(si, 144, 152), key, 4095, OP.bitwise_and)
-        ts(R(si, 152, 160), key, 2048 + 127, OP.bitwise_and)
-        tt(R(rs, 4 - j, 32, 4), key, R(n["sc"], 72, 72 + 8 * Z1, Z1), OP.is_ge)
+        kb = 368 + 8 * Z2 * (j - 1)
+        scan(R(si, kb, kb + 8 * Z2), R(n["sc"], Z2 * (N1 - 1), Z2 * (N1 - 1) + 8 * Z1 * Z2, Z1), p2, OP.max, OP.min)
+        key = R(si, kb + N2 - 1, kb + 8 * Z2, Z2)
+        tt(R(rs, 4 - j, 32, 4), key, R(n["sc"], 0, 8 * Z1 * Z2, Z1 * Z2), OP.is_ge)
         if j == 3:
             back = cur[2]
             cur[2] = 200
@@ -466,7 +483,7 @@ def build(T, RO=RO):
             if t < RO - 1:
                 ts(R("rel", 8 * h, 8 * h + 8), R(rs, 67, 96, 4), 0.0, OP.is_ge)
             cur[2] = back
-        tcopy(R(n["l16"], 48, 64), R(si, 144, 160))
+        bits([(key, 4095), (key, 2048 + 127)], R(n["l16"], 48, 64), R(si, 144, 160))
         act(R(n["ge"], 0, 256), G(R(dw, 0, DWW), R(n["l16"], 48, 64)), AF.Copy)
         settle(n, w, 1024 + 128 * j, [s, R(n["ge"], 0, 128), R(n["ge"], 128, 256)], j < 3)
 
@@ -474,20 +491,19 @@ def build(T, RO=RO):
         n = names(h, "n")
         si, hh, nm, sf = n["si"], n["hh"], n["nm"], n["sf"]
         H = lambda i, a=0, b=64: R(hh, 64 * i + a, 64 * i + b)
-        ts(R(si, 160, 184), R(si, 120, 144), 7, OP.arith_shift_right, 31, OP.bitwise_and)
+        ts(R(si, 160, 184), R(si, 368 + N2 - 1, 368 + 24 * Z2, Z2), 7, OP.arith_shift_right, 31, OP.bitwise_and)
         tcopy(R(n["l16"], 72, 96), R(si, 160, 184))
         act(R(n["kg"], 0, 384), G(R(n["kt"], 0, 32), R(n["l16"], 72, 96)), AF.Copy)
         b = n["B"]
         ps = R(b, 200, 224)
         mm([(ps, sel("z1", a), R(n["kg"], a, 384, 16)) for a in range(16)])
-        tt(R(sf, 104, 128), ps, R(si, 72, 96), OP.mult)
-        tt(R(si, 184, 208), R(sf, 104, 128), R(si, 96, 120), OP.add)
-        ts(R(si, 208, 232), R(si, 184, 208), 2047, OP.bitwise_and)
+        tt(R(sf, 104, 128), ps, R(n["fu"], 1, 72, 3), OP.mult)
+        tt(R(si, 184, 208), R(sf, 104, 128), R(n["ff"], 1, 72, 3), OP.add)
+        ts(R(si, 208, 232), R(si, 184, 208), 5, OP.arith_shift_right, 2047, OP.bitwise_and)
         tt(R(sf, 128, 152), R(si, 208, 232), R(sf, 8, 32), OP.subtract)
         ts(R(sf, 152, 176), R(si, 160, 184), code(0) + 0.5, OP.is_gt)
         tt(R(sf, 80, 104), R(sf, 128, 152), R(sf, 152, 176), OP.mult)
-        for j in (1, 2, 3):
-            tt(H(8 + j), G(R(sf, 72 + 8 * j, 80 + 8 * j), lrep4), H(0), OP.mult)
+        tt(H(8, 0, 240), G(R(sf, 72, 104), R("lr4", 0, 15)), H(12, 0, 240), OP.mult)
         mm([(R(b, 64 + 8 * j, 128), idh, H(8 + j, 0, 64 - 8 * j)) for j in range(4)]
            + [(R(b, 72, 128), idh, R(nm, 8, 64)), (R(b, 64, 120), idh, H(7, 0, 56)), (R(b, 72, 128), nih, H(7, 0, 56))])
         if t < RO - 1:
@@ -499,9 +515,9 @@ def build(T, RO=RO):
         mm([(ps, R("one", 0, 128), C("rel", c)) for c in range(16)])
         tcopy(C("cnt", 0), ps)
         ts(C("cnt", 8), C("cnt", 0), 63, OP.bitwise_and)
-        tcopy(C("cntf", 0), C("cnt", 8))
-        q = 8 * ((t + 1) % 2)
-        ts(R("ofc", q, q + 6), R("k0j", 0, 6), C("cntf", 0), OP.add)
+        ts(C("cntf", 0), C("cnt", 8), 32.0, OP.mult)
+        for h in range(2):
+            ts(R("fu%d" % h, 2, 72, 3), R("k0j", 24 * h, 24 * h + 24), C("cntf", 0), OP.add)
 
     def outputs(h):
         n = names(h, "o")
@@ -579,7 +595,22 @@ def link(ops):
     return deps
 
 
-def schedule(ops, deps):
+def thin(deps):
+    seen = []
+    out = []
+    for d in deps:
+        below = 0
+        keep = {}
+        for k in sorted(d, reverse=True):
+            if not below >> k & 1:
+                keep[k] = d[k]
+                below |= seen[k] | 1 << k
+        seen.append(below)
+        out.append(keep)
+    return out
+
+
+def schedule(ops, deps, bias):
     n = len(ops)
     succ = [[] for _ in range(n)]
     for i in range(n):
@@ -588,7 +619,7 @@ def schedule(ops, deps):
     base = [0.0] * n
     for i in range(n - 1, -1, -1):
         base[i] = ops[i]["cost"] + max([d + base[k] for k, d in succ[i]] + [ops[i]["lat"]])
-    prio = [base[i] - BIAS * ops[i]["half"] - 1e-3 * i for i in range(n)]
+    prio = [base[i] - bias * ops[i]["half"] - 1e-3 * i for i in range(n)]
     left = [len(d) for d in deps]
     ready_at = [0.0] * n
     ready = {}
@@ -611,19 +642,22 @@ def schedule(ops, deps):
     return order
 
 
-BIAS = 3000.0
-PASSES = 4000
+BIAS = (3500.0, 4500.0, 5500.0)
+TRY = 200
+CUT = 600.0
+PASSES = 5000
 LAST = 300
 HEAT = 200.0
-SEED = 7
+SEED = 5
 PLAN = {}
-SETS = [(1.3, 150.0, 0.5, 5000.0, 2.5), (1.56, 150.0, 0.5, 4500.0, 3.8), (2.0, 100.0, 0.5, 4000.0, 5.5), (1.56, 220.0, 0.5, 6000.0, 3.8)]
+SETS = [(1.56, 235.0, 0.5, 5400.0, 3.8), (2.05, 130.0, 0.5, 4200.0, 6.0), (1.3, 275.0, 0.5, 5800.0, 2.5),
+        (1.8, 140.0, 0.65, 6200.0, 5.0), (2.0, 210.0, 0.5, 4200.0, 5.0)]
 
 
 def table(ops, deps):
     return [(o["eng"], [(o["cost"] + o["ga"] * (ga - GA) + o["sc"] * (sc - SC)) * (cpe / CPE if o["eng"] == "p" else 1.0)
                         for ga, _, cpe, _, sc in SETS],
-             [cm if o["eng"] == "x" else o["lat"] for _, _, _, cm, _ in SETS],
+             [o["lat"] * cm / COMM for _, _, _, cm, _ in SETS],
              [k for k, w in d.items() if w], [k for k, w in d.items() if not w]) for o, d in zip(ops, deps)]
 
 
@@ -720,7 +754,7 @@ def valid(key, deps):
     return sorted(range(len(key)), key=lambda i: key[i])
 
 
-def refine(ops, deps, order, passes):
+def refine(ops, deps, order, passes, first):
     n = len(ops)
     rows = table(ops, deps)
     eng, cost, fwd = links(ops, deps)
@@ -728,16 +762,22 @@ def refine(ops, deps, order, passes):
     for i in range(n):
         for k, d in fwd[i]:
             bwd[k].append((i, d - cost[k] + cost[i]))
-    seed = [SEED]
+    seed = [first]
 
     def rnd():
         seed[0] = (seed[0] * 1103515245 + 12345) % 2147483648
         return (seed[0] >> 8) / 8388608.0
 
-    def score(o):
-        return sum(replay(rows, o, s) for s in range(len(SETS)))
+    def score(o, was=None):
+        got = []
+        for s in range(len(SETS)):
+            got.append(replay(rows, o, s))
+            if was and sum(got) > sum(was[:s + 1]) + CUT:
+                return None
+        return got
 
-    best = now = score(order)
+    each = score(order)
+    best = now = sum(each)
     keep = order
     cls = sorted(set(o["cls"] for o in ops))
     start = place(order, eng, cost, fwd)
@@ -762,9 +802,10 @@ def refine(ops, deps, order, passes):
             back = place([n] + sorted(range(n), key=lambda i: -st[i] - cost[i]), eng + ["t"], cost + [0.0], bwd + [[]])
             st = place(sorted(range(n), key=lambda i: -back[i] - cost[i]), eng, cost, fwd)
         o = sorted(range(n), key=lambda i: st[i])
-        s = score(o)
-        if s <= now + HEAT * (1.0 - it / passes) * rnd():
-            now, order, start, held = s, o, st, None
+        got = score(o, each)
+        if got and sum(got) <= now + HEAT * (1.0 - it / passes) * rnd():
+            s = sum(got)
+            now, order, start, held, each = s, o, st, None, got
             if s < best:
                 best, keep = s, o
     start = place(keep, eng, cost, fwd)
@@ -775,22 +816,23 @@ def refine(ops, deps, order, passes):
 
 def plan(T):
     ops = build(T, 3)
-    deps = link(ops)
-    refine(ops, deps, schedule(ops, deps), PASSES)
+    deps = thin(link(ops))
+    tries = [refine(ops, deps, schedule(ops, deps, b), TRY, SEED + k) for k, b in enumerate(BIAS)]
+    refine(ops, deps, min(tries, key=lambda x: x[1])[0], PASSES, SEED)
     at = {(o["t"], o["cls"]): o["t0"] for o in ops}
     sends = [o["t0"] for o in ops if o["eng"] == "x"]
     step = sends[2] - sends[0]
     ops = build(T)
-    deps = link(ops)
+    PLAN["deps"] = link(ops)
+    deps = thin(PLAN["deps"])
     key = []
     for o in ops:
         q = min(o["t"], 1) if o["t"] < RO - 1 else 2
         key.append(at[q, o["cls"]] + step * (o["t"] - q))
     eng, cost, fwd = links(ops, deps)
     st = place(valid(key, deps), eng, cost, fwd)
-    PLAN["deps"] = deps
     PLAN["ops"] = ops
-    PLAN["order"], PLAN["end"] = refine(ops, deps, sorted(range(len(ops)), key=lambda i: st[i]), LAST)
+    PLAN["order"], PLAN["end"] = refine(ops, deps, sorted(range(len(ops)), key=lambda i: st[i]), LAST, SEED)
 
 
 def route(T, topo, t, r):

from concourse.mybir import AluOpType, ActivationFunctionType

OP = AluOpType
AF = ActivationFunctionType
RO, NR = 5, 8
NB = 6
N1 = 10
AL = [2] * 5
SG = [(3, 0, 1), (2, 1, 4), (3, 4, 6)]
SP = [(0, 6), (6, 16)]
RG = [(0, 2, "v"), (2, 4, "s"), (4, 6, "v"), (6, 8, "s")]
F16 = "float16"
MAGIC = 12582912.0
BIG = 33554432.0
N2 = 16 - N1
DUP = max(AL)
Z1, Z2 = N1 | 1, (N2 + 1) | 1
PW = 72 + 8 * (Z1 + Z2)
DWW = 128 * (17 + 16 - NB)


def code(m):
    return 17 - DUP - NB + m if m < NB else 17 + m - NB


def span(z):
    return 16 * ((143 * z) // 16)


SCRATCH = {}


def _sb(name, w, d):
    SCRATCH[name] = ("sbuf", [128, w], d)


for _n, _w, _d in [
    ("zz", 6 * 256, "bfloat16"), ("ob", 5 * 256, "bfloat16"), ("w0", 3072, "bfloat16"), ("w1", 3072, "bfloat16"),
    ("pi", 16, "int32"), ("pf", 16, "float32"), ("pc", 16, "float32"), ("xi", 144, "float32"), ("i1", PW, "float32"),
    ("i2", 128, "float32"), ("i3", 128, "float32"), ("i4", 32, "float32"), ("i6", 144, "float32"), ("i7", 64, "float32"),
    ("i8", 64, "float32"), ("i9", PW, "float32"), ("ia", PW, "float32"), ("ib", 48, "float32"),
    ("z1", 144, "bfloat16"), ("z4", 144, "bfloat16"), ("zq", 144, "bfloat16"), ("idb", 128, "bfloat16"),
    ("nid", 128, "bfloat16"), ("hid", 128, "bfloat16"), ("one", 128, "bfloat16"), ("qrt", 128, "bfloat16"),
    ("idh", 128, F16), ("nih", 128, F16), ("i128", 128, F16), ("bz", 144, F16), ("by", 144, F16),
    ("blk", 128, "float32"), ("mk8", 16, "float32"), ("k0j", 48, "float32"), ("ij", 24, "float32"), ("lr2", 8, "uint16"),
    ("posk", 64, "float32"), ("poskh", 64, F16), ("ck", 64, F16), ("pa", PW, "bfloat16"), ("pb", PW, "bfloat16"),
    ("rst", PW + 32, "float32"), ("ub", 32, "bfloat16"), ("pd", 8 * Z1, "bfloat16"), ("ti8", 8, "float32"), ("lrep", 8, "uint16"), ("lrs", 2, "uint16"), ("lr4", 16, "uint16"),
    ("rel", 16, "bfloat16"), ("cnt", 16, "int32"), ("cntf", 8, "float32"),
]:
    _sb(_n, _w, _d)
for _h in range(2):
    for _n, _w, _d in [
        ("xw", 2176, "bfloat16"), ("sti", 1024, "bfloat16"), ("sob", 1024, "bfloat16"), ("nmi", 64, "int32"),
        ("mob", 64, "float32"), ("rn", 512, F16), ("wk", 8, "int32"), ("wf", 8, "float32"), ("zw", 144, "bfloat16"),
        ("m16", 128, "float32"), ("kapr", 128, "float32"), ("kq", 48, "int32"), ("kqf", 32, "float32"), ("kt", 32, "bfloat16"),
        ("dw", DWW, "bfloat16"), ("a1", span(Z1), "bfloat16"), ("a2", span(Z2), "bfloat16"), ("gb", span(9), "bfloat16"),
        ("ge", 256, "bfloat16"), ("kg", 384, "bfloat16"), ("d7", 128, "bfloat16"), ("sc", 9 * Z1 * Z2, "float32"),
        ("fu", 80, "int32"), ("ff", 72, "float32"), ("si", 368 + 24 * Z2, "int32"), ("tt", 256, "int32"), ("tf", 128, "float32"), ("c16", 128, "uint16"), ("l16", 96, "uint16"),
        ("src", 64, "uint16"), ("nm", 96, F16), ("hh", 64 * 16, F16), ("sf", 176, "float32"), ("rs", 96, "float32"),
    ]:
        _sb(_n + str(_h), _w, _d)
for _b in range(8):
    SCRATCH["ps%d" % _b] = ("psum", [128, 512], "float32")

DMAS = [n + str(h) for h in range(2) for n in ("dwk", "dar", "dst", "drc", "dnm", "dso", "dzo", "dmo", "dx")]
SEMAPHORES = ["cv", "cs", "cp", "cg", "sent"] + DMAS + ["ar%d" % i for i in range(2 * RO)]

CV, CPE, LAT, GA, SC, COMM, DXL = 1.0, 0.55, 215.0, 1.65, 4.3, 5200.0, 4200.0
SEG = {"g": (0, 9), 1: (72, Z1), 2: (72 + 8 * Z1, Z2), "u": (PW, 4)}


def zc(t, h):
    return 256 * t + 128 * h


def build(T, RO=RO):
    ops = []
    cur = [0, "i", 0]
    now = [0]

    def R(name, lo, hi, step=1):
        n = len(range(lo, hi, step))
        hi = lo + (n - 1) * step + 1
        ap = T[name][:, lo:hi] if step == 1 else T[name][:, lo:hi:step]
        return (ap, (name, lo, hi, step), n, SCRATCH[name][2])

    def C(name, c):
        return R(name, c, c + 1)

    def G(win, off):
        return (win[0].indirect(off[0]), win[1], 16 * off[2], win[3], off[1])

    def add(eng, fn, reads, writes, cost, **kw):
        rd = []
        for r in reads:
            if isinstance(r, tuple):
                rd.append(r[1])
                if len(r) == 5:
                    rd.append(r[4])
        wr = [w[1] for w in writes]
        for w in writes:
            if len(w) == 5:
                rd.append(w[4])
        ga = sum(r[2] for r in reads if isinstance(r, tuple) and len(r) == 5)
        d = dict(eng=eng, fn=fn, rd=rd, wr=wr, cost=cost, lat=0.0, sem=None, after=None, half=cur[0], t=now[0],
                 cls="%s%d_%d" % (cur[1], cur[0], cur[2]), ga=ga, sc=sum(w[2] for w in writes if len(w) == 5))
        cur[2] += 1
        d.update(kw)
        ops.append(d)
        return d

    def ap(x):
        return x[0] if isinstance(x, tuple) else x

    def two(*xs):
        return all(x[3] in ("bfloat16", "float16", "uint16") for x in xs)

    def vcost(out, ins, tt=False):
        if len(out) == 5:
            return 60 + out[2] * SC * CV
        if len(ins[0]) == 5:
            return 60 + out[2] * GA * CV
        f = 0.5 if two(out, *ins) else 1.0
        if tt and not any(x[1][0].startswith("ps") for x in ins):
            f *= 2
        return max(64, out[2] * f) * CV

    def tcopy(out, a):
        return add("v", lambda e: [e.tensor_copy(out[0], a[0])], [a], [out], vcost(out, [a]))

    def tt(out, a, b, op):
        return add("v", lambda e: [e.tensor_tensor(out[0], a[0], b[0], op)], [a, b], [out], vcost(out, [a, b], True))

    def ts(out, a, s1, op0, s2=None, op1=None):
        if op1 is None:
            fn = lambda e: [e.tensor_scalar(out[0], a[0], ap(s1), None, op0)]
        else:
            fn = lambda e: [e.tensor_scalar(out[0], a[0], ap(s1), ap(s2), op0, op1)]
        return add("v", fn, [a, s1, s2], [out], vcost(out, [a]))

    def scan(out, d0, d1, op0, op1):
        return add("v", lambda e: [e.tensor_tensor_scan(out[0], d0[0], d1[0], 0.0, op0, op1)], [d0, d1], [out], vcost(out, [d0]))

    def mset(out, v):
        return add("v", lambda e: [e.memset(out[0], v)], [], [out], max(64, out[2] * (0.5 if two(out) else 1)) * CV)

    def act(out, a, func):
        cost = 78 + out[2] * GA * CV if len(a) == 5 else max(64, out[2]) * CV
        return add("s", lambda e: [e.activation(out[0], a[0], func)], [a], [out], cost)

    def pick(e, out, a):
        return tcopy(out, a) if e == "v" else act(out, a, AF.Copy)

    def scale(out, a, v):
        return add("s", lambda e: [e.activation(out[0], a[0], AF.Identity, scale=ap(v))], [a, v], [out], max(64, out[2]) * CV)

    def mm(items, first=True, last=True):
        k = len(items)
        fn = lambda e: [e.matmul(o[0], l[0], r[0], first and i == 0, last and i == k - 1) for i, (o, l, r) in enumerate(items)]
        cost = sum(max(64, r[2]) * (4 if r[3] == "float32" else 1) for _, _, r in items) * CPE
        return add("p", fn, [x for _, l, r in items for x in (l, r)], [o for o, _, _ in items], cost)

    def iota(out, pat, base, cm=0):
        if out[3] == "int32":
            fn = lambda e: [e.iota(out[0], pat, base, cm)]
        else:
            fn = lambda e: [e.iota(out[0], pat, base, cm, allow_small_or_imprecise_dtypes=True)]
        return add("g", fn, [], [out], 130 + 2 * out[2] * CV)

    def gcopy(out, a):
        return add("g", lambda e: [e.affine_select(out[0], a[0], [[0, out[2]]], OP.is_gt, 0.0, 1, 0)], [a], [out],
                   170 + 2 * out[2] * CV)

    def dma(eng, sem, pairs, reads, writes, lat):
        fn = lambda e: [e.dma_start(o, i) for o, i in pairs]
        return add(eng, fn, reads, writes, 60.0 * len(pairs), lat=lat, sem=sem)

    def sel(z, a, top=15):
        return R(z, top - a, top + 128 - a)

    def slot(buf, z, m):
        return R(buf, 16 * m, 16 * m + 128 * z, z)

    def halves(buf, lo, ten, h, w, whole=False):
        return [(T[buf][64 * u:64 * u + 64, lo:lo + w], ten[64 * h:64 * h + 64, :] if whole else ten[64 * h:64 * h + 64, w * u:w * u + w])
                for u in range(2)]

    idb, nid, hid, qrt = R("idb", 0, 128), R("nid", 0, 128), R("hid", 0, 128), R("qrt", 0, 128)
    idh, nih, i128 = R("idh", 0, 128), R("nih", 0, 128), R("i128", 0, 128)

    for h in range(2):
        s = str(h)
        cur[:] = [h, "l", 0]
        dma("y", "dar" + s, halves("zz", zc(0, h), T.arr, h, 128), [], [R("zz", zc(0, h), zc(0, h) + 128)], 2300)
        dma("y", "dst" + s, halves("sti" + s, 0, T.st, h, 1024), [], [R("sti" + s, 0, 1024)], 3000 + 2500 * h)
        dma("s", "dwk" + s, halves("wk" + s, 0, T.wt, h, 1, True) + halves("wk" + s, 4, T.kap, h, 1, True), [],
            [R("wk" + s, 0, 8)], 2200)
        dma("s", "dnm" + s, halves("nmi" + s, 0, T.nm, h, 64), [], [R("nmi" + s, 0, 64)], 2500)
        dma("y", "drc" + s, halves("xw" + s, 128, T.rec, h, 2048, True), [], [R("xw" + s, 128, 2176)], 5000 + 2500 * h)

    cur[:] = [0, "i", 0]
    iota(R("pi", 0, 16), [[0, 16]], 0, 1)
    for c, sh, mk in ((1, 0, 15), (2, 0, 7), (3, 3, 1), (4, 4, 7), (5, 1, 7), (6, 0, 1), (7, 6, 1), (8, 0, 3), (9, 2, 3)):
        ts(C("pi", c), C("pi", 0), sh, OP.arith_shift_right, mk, OP.bitwise_and)
    tcopy(R("pf", 0, 16), R("pi", 0, 16))
    ts(C("pc", 0), C("pf", 4), 16.0, OP.mult, 15.0, OP.add)
    iota(R("xi", 0, 144), [[1, 144]], 0)
    ts(R("z1", 0, 144), R("xi", 0, 144), C("pc", 0), OP.is_equal)
    ts(idb, R("xi", 0, 128), C("pf", 0), OP.is_equal)
    scale(R("z4", 0, 144), R("z1", 0, 144), 4096.0)
    scale(nid, idb, -1.0)
    scale(hid, idb, 0.5)
    for o, v in ((idh, 1.0), (nih, -1.0), (i128, 128.0)):
        ts(o, idb, v, OP.mult)
    mset(qrt, -0.25)
    iota(R("one", 0, 128), [[0, 128]], 1)
    ts(C("pc", 8), C("pf", 1), 8.0, OP.mult)
    ts(C("pc", 1), C("pf", 7), 1024.0, OP.mult, C("pc", 8), OP.add)
    ts(R("ti8", 0, 8), R("xi", 0, 8), 128.0, OP.mult, C("pc", 1), OP.add)
    ts(C("pc", 3), C("pc", 0), -1.0, OP.add, C("pf", 3), OP.add)
    ts(C("pc", 10), C("pf", 6), 8.0, OP.mult, -8.0, OP.add)
    tt(C("pc", 4), C("pc", 10), C("pc", 0), OP.add)
    ts(R("bz", 0, 144), R("xi", 0, 144), C("pc", 3), OP.is_equal)
    ts(R("by", 0, 144), R("xi", 0, 144), C("pc", 4), OP.is_equal)
    ts(R("mk8", 0, 8), R("xi", 0, 8), C("pf", 2), OP.is_equal)
    ts(R("mk8", 8, 16), R("xi", 0, 8), C("pf", 5), OP.is_equal)
    ts(R("pc", 5, 7), R("xi", 0, 2), C("pf", 1), OP.is_equal)
    ts(C("pc", 11), C("pf", 8), -8.0, OP.mult, 24.0, OP.add)
    tt(C("pc", 7), C("pc", 11), C("pf", 9), OP.add)
    ts(R("lrs", 0, 2), R("xi", 0, 2), 4.0, OP.mult, C("pc", 7), OP.add)
    ts(R("lrep", 0, 8), R("xi", 0, 8), 0.0, OP.mult, C("pf", 2), OP.add)
    ts(C("pc", 12), C("pf", 2), 3.0, OP.mult, 1.0, OP.add)
    ts(R("lr2", 0, 8), R("xi", 0, 8), 0.0, OP.mult, C("pc", 12), OP.add)
    iota(R("ij", 0, 24), [[1, 3], [0, 8]], 1)
    iota(R("ib", 32, 48), [[8, 4], [0, 4]], 0)
    ts(R("lr4", 0, 16), R("ib", 32, 48), C("pf", 2), OP.add)
    iota(R("i7", 0, 64), [[128, 8], [0, 8]], 0)
    iota(R("i8", 0, 64), [[128, 8], [16, 8]], 0)
    ts(R("posk", 0, 64), R("i8", 0, 64), C("pf", 1), OP.add)
    tcopy(R("poskh", 0, 64), R("posk", 0, 64))
    ts(R("ck", 0, 64), R("i7", 0, 64), -1.0, OP.mult, 1024.0, OP.add)
    for k, base in (("g", 0), (1, code(0)), (2, code(0) + N1)):
        c0, z = SEG[k]
        iota(R("i9", c0, c0 + 8 * z), [[0, 8], [128, z]], 128 * base)
        iota(R("ia", c0, c0 + 8 * z), [[16, 8], [0, z]], 0)
    ts(R("i1", 0, PW - 72), R("i9", 72, PW), 128.0 * (17 - DUP), OP.is_ge, 128.0 * DUP, OP.mult)
    tt(R("pa", 72, PW), R("i9", 72, PW), R("i1", 0, PW - 72), OP.add)
    for m in range(N2, Z2):
        mset(R("pa", SEG[2][0] + m, PW, Z2), -BIG)
    tcopy(R("pa", 0, 72), R("i9", 0, 72))
    ts(R("pb", 0, PW), R("ia", 0, PW), C("pf", 1), OP.add)
    iota(R("rst", 0, PW + 32), [[0, PW + 32]], 0)
    for k in ("g", 1, "u"):
        c0, z = SEG[k]
        mset(R("rst", c0, c0 + 8 * z, z), BIG)
    iota(R("pd", 0, 8 * Z1), [[0, 8 * Z1]], 0)
    mset(R("pd", 0, 8 * Z1, Z1), -128.0)
    iota(R("i6", 0, 144), [[1, 9], [0, 4], [100, 4]], -300)
    ts(R("zq", 0, 144), R("i6", 0, 144), C("pf", 4), OP.is_equal)
    iota(R("ib", 0, 32), [[0, 8], [1, 4]], 0)
    ts(R("ub", 0, 32), R("ib", 0, 32), C("pf", 9), OP.not_equal, 4194304.0, OP.mult)
    iota(R("i3", 0, 128), [[1, 8], [0, 16]], 0)
    iota(R("i2", 0, 128), [[1, 16], [0, 8]], 0)
    ts(R("blk", 0, 128), R("i3", 0, 128), C("pf", 4), OP.is_equal)
    iota(R("i4", 0, 32), [[0, 4], [16, 8]], -128)
    for h in range(2):
        s = str(h)
        cur[:] = [h, "j", 0]
        B = "ps%d" % (4 * h + 1)
        wf, kapr, kq, kqf, kt = "wf" + s, "kapr" + s, "kq" + s, "kqf" + s, "kt" + s
        tcopy(R(wf, 0, 8, 4), R("wk" + s, 0, 8, 4))
        scale(R("zw" + s, 0, 144), R("zq", 0, 144), C(wf, 0))
        ts(R("m16" + s, 0, 128), R("i2", 0, 128), C("pf", 1), OP.is_equal, C(wf, 4), OP.mult)
        mm([(R(B, 0, 128), R("blk", 0, 128), R("m16" + s, 0, 128))])
        scale(R(kapr, 0, 128), R(B, 0, 128), 32.0)
        ts(R("k0j", 24 * h, 24 * h + 24), R("ij", 0, 24), C(kapr, 0), OP.mult)
        iota(R("fu" + s, 0, 80), [[0, 80]], 0)
        tcopy(R("fu" + s, 2, 72, 3), R("k0j", 24 * h, 24 * h + 24))
        tcopy(R(kq, 0, 16), R(kapr, 0, 128, 8))
        ts(R(kq, 16, 32), R(kq, 0, 16), 1023, OP.bitwise_and)
        tt(R(kq, 32, 48), R(kq, 0, 16), R(kq, 16, 32), OP.subtract)
        ts(R(kqf, 0, 16), R(kq, 16, 32), C("pc", 5), OP.mult)
        ts(R(kqf, 16, 32), R(kq, 32, 48), C("pc", 6), OP.mult)
        iota(R(kt, 0, 32), [[0, 32]], 0)
        tt(R(kt, code(0), code(0) + NB), R(kqf, 0, NB), R(kqf, 16, 16 + NB), OP.add)
        tt(R(kt, 17, 33 - NB), R(kqf, NB, 16), R(kqf, 16 + NB, 32), OP.add)
        for c in range(0, 128 * (code(0) - 2), 384):
            e = min(c + 384, 128 * (code(0) - 2))
            iota(R("dw" + s, c, e), [[0, e - c]], 0)
        for buf, z, m0 in (("gb", 9, 8), ("a1", Z1, N1), ("a2", Z2, N2)):
            for m in range(m0, z):
                iota(slot(buf + s, z, m), [[0, 128]], 0)
        iota(R("sc" + s, Z2 * (N1 - 1), Z2 * (N1 - 1) + 8 * Z1 * Z2, Z1), [[0, 8 * Z2]], 0)
        ts(R("nm" + s, 64, 96), R("i4", 0, 32), C("pf", 1), OP.add)
        ts(R("sf" + s, 32, 40), R("i4", 0, 8), C("pf", 1), OP.add)
        iota(R("sf" + s, 0, 8), [[0, 8]], 0)
        iota(R("rs" + s, 0, 32), [[0, 32]], 0)
        mset(R("hh" + s, 120, 128), 1.0)
        for k in range(8):
            ts(R("rn" + s, 64 * k, 64 * k + 64), R("nmi" + s, 0, 64), C("mk8", k), OP.mult)
        mm([(R(B, 0, 64), sel("bz", 2 * q, 14), R("rn" + s, q, 512, 8)) for q in range(8)])
        tcopy(R("nm" + s, 0, 64), R(B, 0, 64))

    lrep4 = R("lrep", 0, 4)

    def names(h, tag):
        s = str(h)
        cur[:] = [h, tag, 0]
        d = {k: k + s for k in ("tf", "dw", "a1", "a2", "gb", "ge", "kg", "d7", "sc", "si", "tt", "c16", "l16", "src", "nm", "hh",
                                "sf", "rs", "xw", "zw", "kapr", "kt", "sti", "sob", "mob", "rn", "fu", "ff")}
        d.update(A="ps%d" % (4 * h), B="ps%d" % (4 * h + 1), Cb="ps%d" % (4 * h + 2), D="ps%d" % (4 * h + 3))
        d["bank"] = [d["A"], d["B"], d["Cb"], d["D"]]
        return d

    def keys(out, buf, seg, more=()):
        c0, z = SEG[seg]
        mm([(out, idb, R("pa", c0, c0 + 8 * z)), (out, idb, R("pb", c0, c0 + 8 * z))] + [(out, idb, x) for x in more], True, False)
        mm([(out, sel("z4", a), R(buf, z * a, z * a + 128 * z, 16)) for a in range(16)], False, True)

    def least(buf, c, ps, seg, last):
        c0, z = SEG[seg]
        scan(R(buf, c, c + 8 * z), R("rst", c0, c0 + 8 * z), ps, OP.add, OP.min)
        return R(buf, c + last, c + 8 * z, z)

    def bits(pieces, lst, tmp):
        c = 0
        for a, mask in pieces:
            ts(R(tmp[1][0], tmp[1][1] + c, tmp[1][1] + c + a[2]), a, mask, OP.bitwise_and)
            c += a[2]
        tcopy(lst, tmp)

    def quads(ps, z, src, lo):
        mm([(ps, idb, R("ub", 0, 32))], True, False)
        mm([(ps, sel(z, q, 3), R(src, lo + q, lo + 128, 4)) for q in range(4)], False, True)

    def settle(n, w, place, parts, main=True):
        ps = R(n["D"], 0, 128)
        mm([(ps, idb, qrt), (ps, hid, parts[0])], True, False)
        mm([(ps, hid, p) for p in parts[1:]], False, True)
        keep = R(w[0], w[1] + place, w[1] + place + 128)
        if main:
            s = R(n["dw"], 2048, 2176)
            ts(s, ps, MAGIC, OP.add, -MAGIC, OP.add)
            for i in range(1, DUP):
                gcopy(R(n["dw"], 2048 - 128 * i, 2176 - 128 * i), s)
            gcopy(keep, s)
        else:
            ts(keep, ps, MAGIC, OP.add, -MAGIC, OP.add)

    def rows(t, h):
        n = names(h, "r")
        w = "w%d" % (t % 2)
        if t == 0:
            cur[2] = 5
            for k in range(8):
                pick("sv"[k % 2 * (1 - h)], R(w, 1536 * h + 128 * k, 1536 * h + 128 * k + 128), R(n["sti"], k, 1024, 8))
            return
        win = R("w%d" % ((t - 1) % 2), 1536 * h, 1536 * h + 1536)
        for a, b, e in RG:
            pick(e, R(w, 1536 * h + 128 * a, 1536 * h + 128 * b), G(win, R(n["src"], 8 * a, 8 * b)))

    def store(t, h):
        n = names(h, "s")
        si = n["si"]
        z0 = zc(t, h)
        ps = R(n["A"], 0, 32)
        quads(ps, "zq", "zz", z0)
        ts(R(si, 16, 24), least(si, 336, ps, "u", 3), 7, OP.bitwise_and)
        tt(R(n["sf"], 72, 80), R(si, 16, 24), R("ti8", 0, 8), OP.add)
        tcopy(R(n["l16"], 0, 8), R(n["sf"], 72, 80))
        X = R(n["xw"], 128, 2176)
        tcopy(G(X, R(n["l16"], 0, 8)), R("zz", z0, z0 + 128))
        x = T[n["xw"]]
        dma("y", "dx%d" % h, [(x[0:64, 1152:2176], x[64:128, 1152:2176]), (x[64:128, 128:1152], x[0:64, 128:1152])], [X], [X], DXL)

    def gap(t, h):
        n = names(h, "g")
        si, hh, nm, sf = n["si"], n["hh"], n["nm"], n["sf"]
        w = ("w%d" % (t % 2), 1536 * h)
        z = R("zz", zc(t, h), zc(t, h) + 128)
        for q, b in enumerate((n["Cb"], n["D"])):
            mm([(R(b, 0, 512), idb, R(w[0], w[1] + 512 * q, w[1] + 512 * q + 512))], True, False)
            mm([(R(b, 128 * k, 128 * k + 128), nid, z) for k in range(4)], False, True)
            for k in range(4):
                act(slot(n["gb"], 9, 4 * q + k), R(b, 128 * k, 128 * k + 128), AF.Abs)
        ps = R(n["B"], 0, 72)
        keys(ps, n["gb"], "g")
        off = R(si, 56, 64)
        key = least(si, 264, ps, "g", 7)
        bits([(key, 4095)], R(n["l16"], 16, 24), off)
        ge = R(n["ge"], 0, 128)
        act(ge, G(R(w[0], w[1], w[1] + 1024), R(n["l16"], 16, 24)), AF.Copy)
        settle(n, w, 1024, [z, ge])
        H = lambda i, a=0, b=64: R(hh, 64 * i + a, 64 * i + b)
        tt(H(2), G(off, lrep4), R("posk", 0, 64), OP.is_gt)
        tt(H(0), R(hh, 120, 184), H(2), OP.subtract)
        for j in (1, 2, 3):
            tt(H(3 + j), H(0), R(nm, 8 * j, 8 * j + 64), OP.mult)
            mm([(R(n["B"], 120 + 8 * j, 128 + 8 * j), idh, H(3 + j, 8 * k, 8 * k + 8)) for k in range(8)])
        tcopy(R(n["l16"], 24, 48), R(n["B"], 128, 152))
        act(R(sf, 8, 32), R(n["B"], 128, 152), AF.Copy)
        tt(R(sf, 40, 72), R(sf, 8, 40), R(sf, 0, 32), OP.subtract)
        tcopy(R(n["rs"], 32, 64), G(R(sf, 40, 72), R("lrs", 0, 2)))
        tt(H(3), H(0), R("ck", 0, 64), OP.mult)
        b = n["B"]
        mm([(R(b, 384, 448), idh, R("poskh", 0, 64)), (R(b, 384, 448), i128, H(2))]
           + [(R(b, 384 + 8 * j, 448), idh, H(3, 0, 64 - 8 * j)) for j in range(4)])
        tcopy(R(n["src"], 0, 64), R(b, 384, 448))
        tt(H(7, 0, 56), R(nm, 8, 64), H(2, 0, 56), OP.mult)
        gcopy(H(12), H(0))
        gcopy(H(13), H(0))
        gcopy(H(14, 0, 128), H(12, 0, 128))

    def corr(t, h, j):
        n = names(h, "abc"[j - 1])
        si, dw, tw, sf, tf, rs = n["si"], n["dw"], n["tt"], n["sf"], n["tf"], n["rs"]
        w = ("w%d" % (t % 2), 1536 * h)
        X = R(n["xw"], 128, 2176)
        s = R(dw, 2048, 2176)
        c0 = code(0) - 3 + j
        D = lambda m0, m1: R(dw, 128 * code(m0), 128 * code(m1 - 1) + 128) if m0 else R(dw, 128 * c0, 128 * c0 + 128)
        L = lambda m0, m1: R(n["c16"], 8 * m0, 8 * m1)
        AB = lambda m: slot(n["a1"], Z1, m) if m < N1 else slot(n["a2"], Z2, m - N1)
        ps = R(n["A"], 0, 32)
        quads(ps, n["zw"], dw, 2048)
        fu, c = n["fu"], 24 * j - 24
        ts(R(fu, c + 1, c + 24, 3), least(si, 232, ps, "u", 3), 2047, OP.bitwise_and)
        u, f = R(fu, c, c + 24), R(n["ff"], c, c + 24)
        scan(f, u, R(fu, c + 1, c + 25), OP.mult, OP.add)
        for m0, m1 in SP:
            rep = R("lr2", 0, (m1 - m0) // 2)
            tt(R(tf, 8 * m0, 8 * m1), G(u, rep), R(n["kapr"], 8 * m0, 8 * m1), OP.mult)
            tt(R(tw, 8 * m0, 8 * m1), G(f, rep), R(tf, 8 * m0, 8 * m1), OP.add)
            m0 = max(m0, 1)
            ts(R(tw, 128 + 8 * m0, 128 + 8 * m1), R(tw, 8 * m0, 8 * m1), 5, OP.arith_shift_right, 2047, OP.bitwise_and)
            tcopy(L(m0, m1), R(tw, 128 + 8 * m0, 128 + 8 * m1))
        if j == 1:
            back = cur[2]
            cur[2] = 300
            act(R(dw, 128 * c0, 128 * c0 + 384), G(X, R(n["l16"], 24, 48)), AF.Copy)
            cur[2] = back
        if j == 3:
            back = cur[2]
            cur[2] = 100
            settle(n, w, 1408, [s, D(0, 1)], False)
            z = R("zz", zc(t, h), zc(t, h) + 128)
            act(R(n["d7"], 0, 128), G(R(w[0], w[1], w[1] + 1536), R(n["src"], 56, 64)), AF.Copy)
            mm([(R(n["A"], 128, 256), nid, z), (R(n["A"], 128, 256), idb, R(n["d7"], 0, 128))])
            act(R(n["xw"], 0, 128), R(n["A"], 128, 256), AF.Abs)
            cur[2] = back
        for b, m0, m1 in SG:
            b = n["bank"][b]
            if m1 > 1:
                act(D(m0, m1), G(X, L(m0, m1)), AF.Copy)
            k = m1 - m0
            mm([(R(b, 0, 128 * k), idb, D(m0, m1))] + [(R(b, 128 * i, 128 * i + 128), nid, s) for i in range(k)])
            for i in range(k):
                act(AB(m0 + i), R(b, 128 * i, 128 * i + 128), AF.Abs)
        m = NB
        for k in AL:
            tt(D(m, m + k), G(X, L(m, m + k)), R(dw, 2176 - 128 * k, 2176), OP.subtract)
            for i in range(k):
                act(AB(m + i), D(m + i, m + i + 1), AF.Abs)
            m += k
        p1, p2 = R(n["A"], 256, 256 + 8 * Z1), R(n["B"], 0, 8 * Z2)
        keys(p1, n["a1"], 1, [R("pd", 0, 8 * Z1)] * (3 - j))
        scan(R(n["sc"], 0, 8 * Z1 * Z2, Z2), R("rst", 72, 72 + 8 * Z1), p1, OP.add, OP.min)
        keys(p2, n["a2"], 2)
        kb = 368 + 8 * Z2 * (j - 1)
        scan(R(si, kb, kb + 8 * Z2), R(n["sc"], Z2 * (N1 - 1), Z2 * (N1 - 1) + 8 * Z1 * Z2, Z1), p2, OP.max, OP.min)
        key = R(si, kb + N2 - 1, kb + 8 * Z2, Z2)
        tt(R(rs, 4 - j, 32, 4), key, R(n["sc"], 0, 8 * Z1 * Z2, Z1 * Z2), OP.is_ge)
        if j == 3:
            back = cur[2]
            cur[2] = 200
            scan(R(rs, 64, 96), R(rs, 0, 32), R(rs, 32, 64), OP.mult, OP.add)
            ts(R(n["l16"], 64, 72), R(rs, 67, 96, 4), 128.0, OP.add)
            ob = R("ob", zc(t, h), zc(t, h) + 128)
            act(ob, G(R(n["xw"], 0, 2176), R(n["l16"], 64, 72)), AF.Copy)
            snd = add("g", None, [ob], [], 300.0, sem="sent", send=(t, h), src=ob[0])
            zn = R("zz", zc(t + 1, h), zc(t + 1, h) + 128)
            add("x", None, [], [zn], 0.0, lat=COMM, sem="ar%d" % (2 * t + h), after=snd, recv=(t, h))
            if t < RO - 1:
                ts(R("rel", 8 * h, 8 * h + 8), R(rs, 67, 96, 4), 0.0, OP.is_ge)
            cur[2] = back
        bits([(key, 4095), (key, 2048 + 127)], R(n["l16"], 48, 64), R(si, 144, 160))
        act(R(n["ge"], 0, 256), G(R(dw, 0, DWW), R(n["l16"], 48, 64)), AF.Copy)
        settle(n, w, 1024 + 128 * j, [s, R(n["ge"], 0, 128), R(n["ge"], 128, 256)], j < 3)

    def rename(t, h):
        n = names(h, "n")
        si, hh, nm, sf = n["si"], n["hh"], n["nm"], n["sf"]
        H = lambda i, a=0, b=64: R(hh, 64 * i + a, 64 * i + b)
        ts(R(si, 160, 184), R(si, 368 + N2 - 1, 368 + 24 * Z2, Z2), 7, OP.arith_shift_right, 31, OP.bitwise_and)
        tcopy(R(n["l16"], 72, 96), R(si, 160, 184))
        act(R(n["kg"], 0, 384), G(R(n["kt"], 0, 32), R(n["l16"], 72, 96)), AF.Copy)
        b = n["B"]
        ps = R(b, 200, 224)
        mm([(ps, sel("z1", a), R(n["kg"], a, 384, 16)) for a in range(16)])
        tt(R(sf, 104, 128), ps, R(n["fu"], 1, 72, 3), OP.mult)
        tt(R(si, 184, 208), R(sf, 104, 128), R(n["ff"], 1, 72, 3), OP.add)
        ts(R(si, 208, 232), R(si, 184, 208), 5, OP.arith_shift_right, 2047, OP.bitwise_and)
        tt(R(sf, 128, 152), R(si, 208, 232), R(sf, 8, 32), OP.subtract)
        ts(R(sf, 152, 176), R(si, 160, 184), code(0) + 0.5, OP.is_gt)
        tt(R(sf, 80, 104), R(sf, 128, 152), R(sf, 152, 176), OP.mult)
        tt(H(8, 0, 240), G(R(sf, 72, 104), R("lr4", 0, 15)), H(12, 0, 240), OP.mult)
        mm([(R(b, 64 + 8 * j, 128), idh, H(8 + j, 0, 64 - 8 * j)) for j in range(4)]
           + [(R(b, 72, 128), idh, R(nm, 8, 64)), (R(b, 64, 120), idh, H(7, 0, 56)), (R(b, 72, 128), nih, H(7, 0, 56))])
        if t < RO - 1:
            tcopy(R(nm, 0, 64), R(b, 64, 128))

    def count(t):
        cur[:] = [0, "k", 0]
        ps = R("ps4", 500, 501)
        mm([(ps, R("one", 0, 128), C("rel", c)) for c in range(16)])
        tcopy(C("cnt", 0), ps)
        ts(C("cnt", 8), C("cnt", 0), 63, OP.bitwise_and)
        ts(C("cntf", 0), C("cnt", 8), 32.0, OP.mult)
        for h in range(2):
            ts(R("fu%d" % h, 2, 72, 3), R("k0j", 24 * h, 24 * h + 24), C("cntf", 0), OP.add)

    def outputs(h):
        n = names(h, "o")
        s = str(h)
        win = R("w%d" % ((RO - 1) % 2), 1536 * h, 1536 * h + 1536)
        for k in range(8):
            pick("sv"[k % 2], R(n["sob"], k, 1024, 8), G(win, R(n["src"], 8 * k, 8 * k + 8)))
        dma("y", "dso" + s, [(b, a) for a, b in halves(n["sob"], 0, T.so, h, 1024)], [R(n["sob"], 0, 1024)], [], 3000)
        for q in range(8):
            ts(R(n["rn"], q, 512, 8), R(n["B"], 64, 128), C("mk8", 8 + q), OP.mult)
        mm([(R(n["A"], 0, 64), sel("by", k, 7), R(n["rn"], 64 * k, 64 * k + 64)) for k in range(8)])
        act(R(n["mob"], 0, 64), R(n["A"], 0, 64), AF.Copy)
        dma("y", "dmo" + s, [(b, a) for a, b in halves(n["mob"], 0, T.mo, h, 64)], [R(n["mob"], 0, 64)], [], 2500)
        z0 = zc(RO, h)
        dma("s", "dzo" + s, [(b, a) for a, b in halves("zz", z0, T.zo, h, 128)], [R("zz", z0, z0 + 128)], [], 2500)

    for t in range(RO):
        now[0] = t
        for h in range(2):
            rows(t, h)
            store(t, h)
            gap(t, h)
            for j in (1, 2, 3):
                corr(t, h, j)
            rename(t, h)
        if t < RO - 1:
            count(t)
    for h in range(2):
        outputs(h)
    return ops


def meet(a, b):
    (_, l1, h1, s1), (_, l2, h2, s2) = a, b
    if l1 >= h2 or l2 >= h1:
        return False
    if s1 == s2:
        return (l1 - l2) % s1 == 0
    if s1 < s2:
        l1, h1, s1, l2, h2, s2 = l2, h2, s2, l1, h1, s1
    return any(l2 <= c < h2 and (c - l2) % s2 == 0 for c in range(l1, h1, s1))


def link(ops):
    hist = {}
    deps = []
    for i, o in enumerate(ops):
        o["at"] = i
        d = {}
        if o["after"] is not None:
            d[o["after"]["at"]] = False
        for kind, regs in (("r", o["rd"]), ("w", o["wr"])):
            for reg in regs:
                psum = reg[0].startswith("ps")
                for k, kk, r2 in hist.get(reg[0], ()):
                    if k == i:
                        continue
                    same = ops[k]["eng"] == o["eng"] and ops[k]["sem"] is None
                    if psum and not same:
                        d[k] = True
                    elif psum and o["eng"] == "p":
                        d.setdefault(k, False)
                    elif (kind == "w" or kk == "w") and meet(reg, r2):
                        d[k] = True
        for kind, regs in (("r", o["rd"]), ("w", o["wr"])):
            for reg in regs:
                hl = hist.setdefault(reg[0], [])
                if reg[0].startswith("ps"):
                    if o["eng"] == "p":
                        hl[:] = [x for x in hl if x[0] == i]
                elif kind == "w":
                    hl[:] = [x for x in hl if not (x[2] == reg or (reg[3] == 1 and reg[1] <= x[2][1] and x[2][2] <= reg[2]))]
                hl.append((i, kind, reg))
        deps.append(d)
    return deps


def thin(deps):
    seen = []
    out = []
    for d in deps:
        below = 0
        keep = {}
        for k in sorted(d, reverse=True):
            if not below >> k & 1:
                keep[k] = d[k]
                below |= seen[k] | 1 << k
        seen.append(below)
        out.append(keep)
    return out


def schedule(ops, deps, bias):
    n = len(ops)
    succ = [[] for _ in range(n)]
    for i in range(n):
        for k, w in deps[i].items():
            succ[k].append((i, ops[k]["lat"] + LAT if w else 0.0))
    base = [0.0] * n
    for i in range(n - 1, -1, -1):
        base[i] = ops[i]["cost"] + max([d + base[k] for k, d in succ[i]] + [ops[i]["lat"]])
    prio = [base[i] - bias * ops[i]["half"] - 1e-3 * i for i in range(n)]
    left = [len(d) for d in deps]
    ready_at = [0.0] * n
    ready = {}
    for i in range(n):
        if left[i] == 0:
            ready.setdefault(ops[i]["eng"], []).append(i)
    free = {}
    order = []
    while len(order) < n:
        first, e = min((max(free.get(e, 0.0), min(ready_at[i] for i in lst)), e) for e, lst in ready.items() if lst)
        i = max([i for i in ready[e] if ready_at[i] <= first + 30.0], key=lambda i: prio[i])
        ready[e].remove(i)
        fin = free[e] = max(free.get(e, 0.0), ready_at[i]) + ops[i]["cost"]
        order.append(i)
        for k, d in succ[i]:
            ready_at[k] = max(ready_at[k], fin + d)
            left[k] -= 1
            if left[k] == 0:
                ready.setdefault(ops[k]["eng"], []).append(k)
    return order


BIAS = (3500.0, 4500.0, 5500.0)
TRY = 200
CUT = 600.0
PASSES = 5000
LAST = 300
HEAT = 200.0
SEED = 5
PLAN = {}
SETS = [(1.56, 235.0, 0.5, 5400.0, 3.8), (2.05, 130.0, 0.5, 4200.0, 6.0), (1.3, 275.0, 0.5, 5800.0, 2.5),
        (1.8, 140.0, 0.65, 6200.0, 5.0), (2.0, 210.0, 0.5, 4200.0, 5.0)]


def table(ops, deps):
    return [(o["eng"], [(o["cost"] + o["ga"] * (ga - GA) + o["sc"] * (sc - SC)) * (cpe / CPE if o["eng"] == "p" else 1.0)
                        for ga, _, cpe, _, sc in SETS],
             [o["lat"] * cm / COMM for _, _, _, cm, _ in SETS],
             [k for k, w in d.items() if w], [k for k, w in d.items() if not w]) for o, d in zip(ops, deps)]


def replay(rows, order, s):
    lat = SETS[s][1]
    fin = [0.0] * len(rows)
    done = [0.0] * len(rows)
    free = {}
    for i in order:
        e, cs, ls, hard, soft = rows[i]
        st = free.get(e, 0.0)
        for k in hard:
            if done[k] > st:
                st = done[k]
        for k in soft:
            if fin[k] > st:
                st = fin[k]
        fin[i] = free[e] = st + cs[s]
        done[i] = st + cs[s] + ls[s] + lat
    return max(done)


def chain(rows, order, s):
    lat = SETS[s][1]
    n = len(rows)
    fin, done, why, held = [0.0] * n, [0.0] * n, [-1] * n, [False] * n
    last = {}
    for i in order:
        e, cs, ls, hard, soft = rows[i]
        st, w = 0.0, -1
        for k in hard:
            if done[k] > st:
                st, w = done[k], k
        for k in soft:
            if fin[k] > st:
                st, w = fin[k], k
        k = last.get(e, -1)
        if k >= 0 and fin[k] > st + 1.0:
            st, w = fin[k], k
            held[i] = True
        why[i] = w
        last[e] = i
        fin[i] = st + cs[s]
        done[i] = fin[i] + ls[s] + lat
    i = max(range(n), key=lambda i: done[i])
    pairs = []
    while i >= 0:
        if held[i]:
            pairs.append((i, why[i]))
        i = why[i]
    return pairs


def place(seq, eng, cost, pred):
    start = [0.0] * len(eng)
    busy = {}
    for i in seq:
        st = 0.0
        for k, d in pred[i]:
            v = start[k] + d
            if v > st:
                st = v
        a, b = busy.setdefault(eng[i], ([], []))
        c = cost[i]
        lo, hi = 0, len(b)
        while lo < hi:
            mid = (lo + hi) // 2
            if b[mid] <= st:
                lo = mid + 1
            else:
                hi = mid
        while lo < len(a) and a[lo] < st + c:
            if b[lo] > st:
                st = b[lo]
            lo += 1
        a.insert(lo, st)
        b.insert(lo, st + c)
        start[i] = st
    return start


def links(ops, deps):
    cost = [o["cost"] + 0.01 for o in ops]
    return ([o["eng"] for o in ops], cost,
            [[(k, cost[k] + (ops[k]["lat"] + LAT if w else 0.0)) for k, w in d.items()] for d in deps])


def valid(key, deps):
    key = list(key)
    for i, d in enumerate(deps):
        for k in d:
            if key[k] >= key[i]:
                key[i] = key[k] + 1e-3
    return sorted(range(len(key)), key=lambda i: key[i])


def refine(ops, deps, order, passes, first):
    n = len(ops)
    rows = table(ops, deps)
    eng, cost, fwd = links(ops, deps)
    bwd = [[(n, ops[i]["lat"])] for i in range(n)]
    for i in range(n):
        for k, d in fwd[i]:
            bwd[k].append((i, d - cost[k] + cost[i]))
    seed = [first]

    def rnd():
        seed[0] = (seed[0] * 1103515245 + 12345) % 2147483648
        return (seed[0] >> 8) / 8388608.0

    def score(o, was=None):
        got = []
        for s in range(len(SETS)):
            got.append(replay(rows, o, s))
            if was and sum(got) > sum(was[:s + 1]) + CUT:
                return None
        return got

    each = score(order)
    best = now = sum(each)
    keep = order
    cls = sorted(set(o["cls"] for o in ops))
    start = place(order, eng, cost, fwd)
    held = None
    for it in range(passes):
        shift = {}
        if it % 3:
            if not held:
                held = [chain(rows, order, s) for s in range(len(SETS))]
            pairs = held[int(rnd() * len(held))]
            for _ in range(1 + int(rnd() * 2)):
                i, k = pairs[int(rnd() * len(pairs))]
                if rnd() < 0.5:
                    shift[ops[i]["cls"]] = start[k] - start[i] - 1.0 - 400.0 * rnd() * rnd()
                else:
                    shift[ops[k]["cls"]] = start[i] - start[k] + 1.0 + 1500.0 * rnd() * rnd()
        else:
            for _ in range(1 + int(rnd() * 5)):
                shift[cls[int(rnd() * len(cls))]] = (rnd() - 0.5) * (300.0, 1000.0, 3000.0)[int(rnd() * 3)]
        st = place(valid([start[i] + shift.get(ops[i]["cls"], 0.0) for i in range(n)], deps), eng, cost, fwd)
        if it % 7 == 0:
            back = place([n] + sorted(range(n), key=lambda i: -st[i] - cost[i]), eng + ["t"], cost + [0.0], bwd + [[]])
            st = place(sorted(range(n), key=lambda i: -back[i] - cost[i]), eng, cost, fwd)
        o = sorted(range(n), key=lambda i: st[i])
        got = score(o, each)
        if got and sum(got) <= now + HEAT * (1.0 - it / passes) * rnd():
            s = sum(got)
            now, order, start, held, each = s, o, st, None, got
            if s < best:
                best, keep = s, o
    start = place(keep, eng, cost, fwd)
    for i in range(n):
        ops[i]["t0"] = start[i]
    return keep, best / len(SETS)


def plan(T):
    ops = build(T, 3)
    deps = thin(link(ops))
    tries = [refine(ops, deps, schedule(ops, deps, b), TRY, SEED + k) for k, b in enumerate(BIAS)]
    refine(ops, deps, min(tries, key=lambda x: x[1])[0], PASSES, SEED)
    at = {(o["t"], o["cls"]): o["t0"] for o in ops}
    sends = [o["t0"] for o in ops if o["eng"] == "x"]
    step = sends[2] - sends[0]
    ops = build(T)
    PLAN["deps"] = link(ops)
    deps = thin(PLAN["deps"])
    key = []
    for o in ops:
        q = min(o["t"], 1) if o["t"] < RO - 1 else 2
        key.append(at[q, o["cls"]] + step * (o["t"] - q))
    eng, cost, fwd = links(ops, deps)
    st = place(valid(key, deps), eng, cost, fwd)
    PLAN["ops"] = ops
    PLAN["order"], PLAN["end"] = refine(ops, deps, sorted(range(len(ops)), key=lambda i: st[i]), LAST, SEED)


def route(T, topo, t, r):
    src, dst = T.cores[r], T.cores[(r + 1 + t % 3) % NR]
    if topo.may_write(src, dst):
        return dst, dst
    ok = [c for c in topo.cores_of(src) if T.rank_of(c) is None and topo.may_write(c, dst)]
    near = [c for c in ok if topo.die(c) == topo.die(src)]
    return (near or ok)[0], dst


def arrivals(T, topo, t, r):
    q = (r - 1 - t % 3) % NR
    hop, dst = route(T, topo, t, q)
    return len(topo.engines(T.cores[q] if hop == dst else hop, dst))


def landing(T, t, h):
    return T.zz[:, zc(t + 1, h):zc(t + 1, h) + 128]


def relay_program(g, core, T, topo):
    sent = 0
    for t in range(RO):
        for r in range(NR):
            hop, dst = route(T, topo, t, r)
            if hop != core or hop == dst:
                continue
            rid, pid = topo.addr(dst, core)
            for h in range(2):
                sem = T.sem["ar%d" % (2 * t + h)]
                z = landing(T, t, h)
                g.wait_ge(sem, len(topo.engines(T.cores[r], core)))
                g.remote_dma(z, z, sem, T.sem.sent, pid, rid, topo.mask(core, dst))
                sent += len(topo.engines(core, dst))
    if sent:
        g.wait_ge(T.sem.sent, sent)


def rank_program(g, core, T, topo):
    rank = T.rank_of(core)
    if rank is None:
        relay_program(g, core, T, topo)
        return
    if not PLAN:
        plan(T)
    ops = build(T)
    deps = PLAN["deps"]
    queue = {"v": g.vector, "s": g.scalar, "p": g.tensor, "g": g, "y": g.sync}
    csem = {"v": "cv", "s": "cs", "p": "cp", "g": "cg"}
    count = {}
    known = {e: {} for e in queue}
    mark = {}
    for i in PLAN["order"]:
        o = ops[i]
        e = o["eng"]
        if e == "x":
            t, h = o["recv"]
            mark[i] = (o["sem"], arrivals(T, topo, t, rank), {})
            count[o["sem"]] = mark[i][1]
            continue
        kn = known[e]
        need = sorted((mark[k] for k, w in deps[i].items() if w), key=lambda m: -len(m[2]))
        top = {}
        for s, v, _ in need:
            top[s] = max(top.get(s, 0), v)
        for s, v, clock in need:
            if v == top[s] and kn.get(s, 0) < v:
                queue[e].wait_ge(T.sem[s], v)
                kn[s] = v
                for s2, v2 in clock.items():
                    kn[s2] = max(kn.get(s2, 0), v2)
        if "send" in o:
            t, h = o["send"]
            hop, _ = route(T, topo, t, rank)
            rid, pid = topo.addr(hop, core)
            g.remote_dma(landing(T, t, h), o["src"], T.sem["ar%d" % (2 * t + h)], T.sem.sent, pid, rid, topo.mask(core, hop))
            count["sent"] = count.get("sent", 0) + len(topo.engines(core, hop))
            mark[i] = ("sent", count["sent"], dict(kn))
            continue
        ins = o["fn"](queue[e])
        if o["sem"] is not None:
            s = o["sem"]
            for x in ins:
                x.then_inc(T.sem[s], 16)
            count[s] = count.get(s, 0) + 16 * len(ins)
        else:
            s = csem[e]
            ins[-1].then_inc(T.sem[s], 1)
            count[s] = count.get(s, 0) + 1
        mark[i] = (s, count[s], dict(kn))
    for s, v in count.items():
        g.wait_ge(T.sem[s], v)
